import numpy as np
import ml_dtypes


def mxq(x, axis, fmt="e4m3"):
    dtype, down = {"e4m3": (ml_dtypes.float8_e4m3fn, 7), "e5m2": (ml_dtypes.float8_e5m2, 14)}[fmt]
    v = np.moveaxis(np.asarray(x, np.float32).astype(ml_dtypes.bfloat16).astype(np.float64), axis, -1)
    blocks = v.reshape(v.shape[:-1] + (-1, 32))
    amax = np.abs(blocks).max(-1, keepdims=True)
    byte = np.maximum(np.where(amax > 0, np.frexp(amax)[1] - 1 + 127, 0) - down, 1)
    scale = np.exp2(byte - 127.0)
    codes = (blocks / scale).astype(np.float32).astype(dtype).astype(np.float64)
    return np.moveaxis((codes * scale).reshape(v.shape), -1, axis)


WIDE = False


def mx_kscale(k):
    if not WIDE:
        return np.ones(k)
    levels = np.array([10, -10, 5, -5, 0])
    if k % 512:
        return np.exp2(np.random.permutation(np.resize(levels, k // 32))).repeat(32)
    a = np.empty((k // 512, 16))
    for p in range(k // 512):
        a[p, :8] = np.random.permutation(np.resize(levels, 8))
        for g in range(8):
            far = levels[np.abs(levels - a[p, g]) >= 10]
            a[p, g + 8] = far[np.random.randint(len(far))]
    return np.exp2(a.ravel()).repeat(32)


def f64(x):
    return np.asarray(x).astype(np.float64)


def striped(idx):
    return np.tile(idx.reshape(-1, 16).T, (8, 1)).astype(np.uint16)


def unstriped(offs):
    return offs[:16].T.reshape(-1).astype(np.int64)


E2M1 = np.array([0.0, 0.5, 1.0, 1.5, 2.0, 3.0, 4.0, 6.0, -0.0, -0.5, -1.0, -1.5, -2.0, -3.0, -4.0, -6.0])


def pack_weight(w, fmt):
    k, n = w.shape
    w = f64(np.asarray(w, np.float32).astype(ml_dtypes.bfloat16)).reshape(k // 32, 32, n)
    amax = np.abs(w).max(1)
    if fmt == "e4m3":
        byte = np.frexp(amax)[1] - 1 + 127 - 7
    else:
        mant, ex = np.frexp(amax / 6.0)
        byte = np.where(mant > 0.5, ex, ex - 1) + 127
    byte = np.clip(np.where(amax > 0, byte, 1), 1, 254)
    scaled = (w * np.exp2(127.0 - byte)[:, None, :]).reshape(k, n).astype(np.float32)
    by_word = np.ascontiguousarray(scaled.reshape(k // 512, 128, 4, n).transpose(0, 1, 3, 2))
    if fmt == "e4m3":
        words = by_word.astype(ml_dtypes.float8_e4m3fn).view(np.uint8)
    else:
        c = by_word.astype(ml_dtypes.float4_e2m1fn).view(np.uint8) & 0xF
        words = (c[..., 0::2] | (c[..., 1::2] << 4)).reshape(k // 512, 128, 2 * n)
    return np.ascontiguousarray(words), np.ascontiguousarray(byte.astype(np.uint8).reshape(k // 512, 16, n))


def unpack_weight(words, scales, fmt):
    g, _, n = scales.shape
    words = np.ascontiguousarray(words).reshape(g, 128, n, -1)
    if fmt == "e4m3":
        vals = words.view(ml_dtypes.float8_e4m3fn).astype(np.float64)
    else:
        nib = np.empty((g, 128, n, 4), np.uint8)
        nib[..., 0::2] = words & 0xF
        nib[..., 1::2] = words >> 4
        vals = E2M1[nib]
    vals = vals * np.repeat(np.exp2(scales.astype(np.float64) - 127.0), 8, axis=1)[..., None]
    return vals.transpose(0, 1, 3, 2).reshape(g * 512, n)


def gelu(v):
    return 0.5 * v * (1.0 + np.tanh(np.sqrt(2.0 / np.pi) * (v + 0.044715 * v**3)))


K, T, S, T2, H, N = 512, 4096, 1024, 2048, 1024, 256

def setup_inputs():
    n = np.random.standard_normal
    s = mx_kscale(K)[:, None]
    u = mx_kscale(H)[:, None]
    perm = np.random.permutation(T2)
    tab_words, tab_scales = pack_weight(n((K, T)) * s, "e4m3")
    tab2_words, tab2_scales = pack_weight(n((K, T)) * s, "e4m3")
    w1_words, w1_scales = pack_weight(n((K, H)) / np.sqrt(K) / s, "e2m1")
    w3_words, w3_scales = pack_weight(n((K, H)) / np.sqrt(K) / s, "e4m3")
    return {
        "tab_words": tab_words, "tab_scales": tab_scales,
        "tab2_words": tab2_words, "tab2_scales": tab2_scales,
        "offs": striped(np.random.permutation(T)[:S]),
        "offs2": striped(np.random.permutation(T)[:S]),
        "offs3": striped(perm[:S]), "offs4": striped(perm[S:]),
        "w1_words": w1_words, "w1_scales": w1_scales,
        "w2": (n((K, H)) / np.sqrt(K) / s).astype(np.float32),
        "w3_words": w3_words, "w3_scales": w3_scales,
        "wg1": np.exp(0.3 * n((128, S))).astype(np.float32),
        "wg2": np.exp(0.3 * n((128, S))).astype(np.float32),
        "mix": (np.exp(0.5 * n((H, T2))) * u).astype(np.float32),
        "w4": (n((H, N)) / np.sqrt(H) / u).astype(np.float32),
    }

def reference(tab_words, tab_scales, tab2_words, tab2_scales, offs, offs2, offs3, offs4, w1_words, w1_scales, w2, w3_words, w3_scales, wg1, wg2, mix, w4):
    v = unpack_weight(tab_words, tab_scales, "e4m3")[:, unstriped(offs)]
    v2 = unpack_weight(tab2_words, tab2_scales, "e4m3")[:, unstriped(offs2)]
    h1 = np.square(np.maximum(unpack_weight(w1_words, w1_scales, "e2m1").T @ v, 0.0))
    c = mxq(f64(w2), 0, "e4m3").T @ v2
    d = unpack_weight(w3_words, w3_scales, "e4m3").T @ v2
    h2 = c * (1.0 / (1.0 + np.exp(-d)))
    page = np.zeros((H, T2))
    page[:, unstriped(offs3)] = np.tile(f64(wg1), (H // 128, 1)) * h1
    page[:, unstriped(offs4)] = np.tile(f64(wg2), (H // 128, 1)) * h2
    z = page * f64(mix)
    return mxq(f64(w4), 0, "e4m3").T @ mxq(z, 0, "e4m3")

@@ -1,0 +1,338 @@
+from contextlib import ExitStack
+
+import concourse.mybir as mybir
+
+F32 = mybir.dt.float32
+BF16 = mybir.dt.bfloat16
+I32 = mybir.dt.int32
+U32 = mybir.dt.uint32
+U16 = mybir.dt.uint16
+U8 = mybir.dt.uint8
+FP8X4 = mybir.dt.float8_e4m3fn_x4
+FP4X4 = mybir.dt.float4_e2m1fn_x4
+ACT = mybir.ActivationFunctionType
+MULT = mybir.AluOpType.mult
+
+K, T, S, T2, H, N = 512, 4096, 1024, 2048, 1024, 256
+P = 128
+BANK = 512
+FLOPS = 2 * (3 * K * H * S + H * N * T2)
+PAGES = H // P
+PAGE_SLOTS = 4
+CHUNKS = T2 // BANK
+KIB = 1024
+PAGE_AT = (0, 17 * KIB, 8 * KIB, 26 * KIB)
+W3_SCALES_AT = PAGE_AT[1] - KIB // 2
+W3_WORDS_AT = W3_SCALES_AT + KIB
+W2_ROUNDED_AT = (W3_WORDS_AT + 4 * KIB, PAGE_AT[2])
+MIX_AT = (34 * KIB, 42 * KIB, 50 * KIB)
+WOVEN_AT = (66 * KIB, 58 * KIB, 62 * KIB)
+TAB1_PLANE_AT = 70 * KIB
+TAB2_PLANE_AT = 74 * KIB
+Z_AT = (79 * KIB, 95 * KIB)
+
+
+def tile_list_deferred_tile_shading_kernel(
+    tc, tab_words, tab_scales, tab2_words, tab2_scales, offs, offs2, offs3, offs4,
+    w1_words, w1_scales, w2, w3_words, w3_scales, wg1, wg2, mix, w4, out,
+):
+    nc = tc.nc
+    with ExitStack() as ctx:
+        lists = ctx.enter_context(tc.tile_pool(name="lists", bufs=1))
+        sb = ctx.enter_context(tc.tile_pool(name="sb", bufs=1))
+        shared = ctx.enter_context(tc.tile_pool(name="shared", bufs=1))
+        ps = ctx.enter_context(tc.psum_pool(name="ps", bufs=1))
+
+        def new_tile(shape, dtype, name, tag=None, bufs=1):
+            return sb.tile(shape, dtype, name=name, tag=tag or name, bufs=bufs, align_bytes=64)
+
+        def placed_tile(shape, dtype, name, offset):
+            return shared.tile(shape, dtype, name=name, tag=name, bufs=1, align_bytes=64, offset=offset)
+
+        bank_count = [0]
+
+        def bank():
+            i = bank_count[0]
+            bank_count.append(i + 1)
+            bank_count.remove(i)
+            return ps.tile([P, BANK], F32, name="bank%d" % i, tag="bank%d" % (i % 8))
+
+        def load_list(src, name):
+            dst = lists.tile([P, S // 16], U16, name=name)
+            nc.sync.dma_start(dst[:], src)
+            return dst
+
+        def load_scale_rows(engine, queue, src, plane):
+            engine.memset(plane[:].bitcast(I32), 0)
+            for q in range(4):
+                queue.dma_start(plane[32 * q : 32 * q + 4, :].bitcast(I32), src[0, 4 * q : 4 * q + 4, :].bitcast(I32))
+            return plane
+
+        def load_scale_rows_bare(src, rows):
+            for q in range(4):
+                nc.sync.dma_start(rows[32 * q : 32 * q + 4, :].bitcast(I32), src[0, 4 * q : 4 * q + 4, :].bitcast(I32))
+            return rows
+
+        def fill_plane(rows, plane):
+            nc.vector.memset(plane[:].bitcast(I32), 0)
+            for q in range(4):
+                live = slice(32 * q, 32 * q + 4)
+                nc.vector.tensor_copy(plane[live, :].bitcast(I32), rows[live, :].bitcast(I32))
+            return plane
+
+        wg_tiles = {}
+
+        def load_wg(stream, t, quadrants=range(4)):
+            src = (wg1, wg2)[stream].rearrange("(p t) j -> t p j", t=4)[t]
+            if (stream, t) not in wg_tiles:
+                wg_tiles.setdefault((stream, t), new_tile([P, S], F32, "wg%d_%d" % (stream, t)))
+            for q in quadrants:
+                nc.sync.dma_start(wg_tiles[stream, t][32 * q : 32 * q + 32, :], src)
+
+        idx1 = load_list(offs, "idx1")
+        tab1_rows = load_scale_rows_bare(tab_scales, placed_tile([P, T], U8, "tab1_rows", WOVEN_AT[1]))
+        w1_raw = new_tile([P, 2 * H], U8, "w1_raw")
+        nc.sync.dma_start(w1_raw[:].bitcast(I32), w1_words[0].bitcast(I32))
+        tab1_w = placed_tile([P, T], I32, "tab1_w", Z_AT[0])
+        tab1_src = tab_words[0].rearrange("p n i -> p (n i)").bitcast(I32)
+        for h in range(2):
+            nc.sync.dma_start(tab1_w[:, h * T // 2 : (h + 1) * T // 2], tab1_src[:, h * T // 2 : (h + 1) * T // 2])
+        w1_rows = load_scale_rows_bare(w1_scales, new_tile([P, H], U8, "w1_rows"))
+        idx2 = load_list(offs2, "idx2")
+        idx3 = load_list(offs3, "idx3")
+        tab2_w = placed_tile([P, T], I32, "tab2_w", PAGE_AT[0])
+        load_wg(0, 0)
+        nc.sync.dma_start(tab2_w[:], tab2_words[0].rearrange("p n i -> p (n i)").bitcast(I32))
+        tab2_s = load_scale_rows(nc.gpsimd, nc.gpsimd, tab2_scales, placed_tile([P, T], U8, "tab2_s", TAB2_PLANE_AT))
+        w3_sraw = load_scale_rows(nc.gpsimd, nc.gpsimd, w3_scales, placed_tile([P, H], U8, "w3_sraw", W3_SCALES_AT))
+        tab1_s = fill_plane(tab1_rows, placed_tile([P, T], U8, "tab1_s", TAB1_PLANE_AT))
+        load_wg(0, 1)
+
+        w2_raw = []
+
+        def load_w2(b):
+            raw = placed_tile([P, 4, BANK], F32, "w2_raw%d" % b, Z_AT[1] + 8 * KIB * b)
+            nc.sync.dma_start(raw[:], w2[:, b * BANK : (b + 1) * BANK].rearrange("(p i) c -> p i c", i=4))
+            w2_raw.append(raw)
+
+        load_w2(0)
+        w3_raw = placed_tile([P, H], I32, "w3_raw", W3_WORDS_AT)
+        nc.sync.dma_start(w3_raw[:], w3_words[0].rearrange("p n i -> p (n i)").bitcast(I32))
+        idx4 = load_list(offs4, "idx4")
+        load_wg(1, 0)
+        load_wg(0, 2)
+        load_w2(1)
+        load_wg(1, 1)
+        load_wg(0, 3)
+        w4_raw = placed_tile([P, 2, 4, N], F32, "w4_raw", WOVEN_AT[2])
+        nc.sync.dma_start(w4_raw[:].rearrange("p b t n -> p b (t n)"), w4.rearrange("(b p t) n -> p b (t n)", b=2, t=4))
+
+        w1_codes = new_tile([P, 2 * H], U8, "w1_codes")
+        w1_plane = new_tile([P, H], U8, "w1_plane")
+        nc.vector.tensor_copy(
+            w1_codes[:].bitcast(U16).rearrange("p (b t m) -> p b t m", b=2, t=4),
+            w1_raw[:].bitcast(U16).rearrange("p (b m t) -> p b t m", b=2, t=4))
+        w1_sraw = fill_plane(w1_rows, new_tile([P, H], U8, "w1_sraw"))
+        nc.vector.tensor_copy(
+            w1_plane[:].rearrange("p (b t m) -> p b t m", b=2, t=4),
+            w1_sraw[:].rearrange("p (b m t) -> p b t m", b=2, t=4))
+
+        v1_codes, v1_plane = [], []
+        for h in range(2):
+            cols = slice(h * BANK // 16, (h + 1) * BANK // 16)
+            codes = new_tile([P, BANK], U32, "v1_codes%d" % h)
+            plane = new_tile([P, BANK], U8, "v1_plane%d" % h)
+            nc.vector.tensor_copy(codes[:], tab1_w[:].bitcast(U32).indirect(idx1[:, cols]))
+            nc.vector.tensor_copy(plane[:], tab1_s[:].indirect(idx1[:, cols]))
+            v1_codes.append(codes)
+            v1_plane.append(plane)
+        v2_codes = new_tile([P, S], U32, "v2_codes")
+        v2_plane = placed_tile([P, S], U8, "v2_plane", TAB1_PLANE_AT)
+        nc.vector.tensor_copy(v2_plane[:], tab2_s[:].indirect(idx2[:]))
+        nc.vector.tensor_copy(v2_codes[:], tab2_w[:].bitcast(U32).indirect(idx2[:]))
+
+        w3_codes = placed_tile([P, H], I32, "w3_codes", TAB2_PLANE_AT + KIB)
+        w3_plane = placed_tile([P, H], U8, "w3_plane", TAB2_PLANE_AT)
+
+        w2_codes, w2_plane = [], []
+
+        def quantise_w2(b):
+            grouped = placed_tile([P, 4 * BANK], BF16, "w2_bf%d" % b, W2_ROUNDED_AT[b])
+            nc.scalar.copy(
+                grouped[:].rearrange("p (t m i) -> p m i t", t=4, i=4),
+                w2_raw[b][:].rearrange("p i (m t) -> p m i t", t=4))
+            codes = new_tile([P, BANK], U32, "w2_codes%d" % b)
+            plane = new_tile([P, BANK], U8, "w2_plane%d" % b)
+            nc.vector.quantize_mx(out=codes[:].bitcast(FP8X4), scales=plane[:], in_=grouped[:])
+            w2_codes.append(codes)
+            w2_plane.append(plane)
+
+        pages = {}
+        mix_tiles = {}
+        opaque_values = {}
+        translucent_values = {}
+
+        def load_mix(s):
+            b, t = divmod(s, 4)
+            rows = placed_tile([P, T2], F32, "mix%d" % s, MIX_AT[s % 3])
+            nc.sync.dma_start(rows[:], mix[b * K : (b + 1) * K, :].rearrange("(p t) m -> t p m", t=4)[t])
+            mix_tiles.setdefault(s, rows)
+
+        z_rows = {}
+
+        def z_slot(s):
+            b, t = divmod(s, 4)
+            if b not in z_rows:
+                z_rows.setdefault(b, placed_tile([P, 4 * T2], BF16, "z_rows%d" % b, Z_AT[b]))
+            return z_rows[b][:, t * T2 : (t + 1) * T2]
+
+        def opaque(s):
+            squared = new_tile([P, S], F32, "squared%d" % s, "squared", 3)
+            vals = placed_tile([P, S], F32, "opaque%d" % s, MIX_AT[s % 3])
+            for h in range(2):
+                cols = slice(h * BANK, (h + 1) * BANK)
+                acc = bank()
+                nc.tensor.matmul_mx(
+                    out=acc[:], lhsT=w1_codes[:, 2 * P * s : 2 * P * (s + 1)].bitcast(FP4X4),
+                    lhsT_scale=w1_plane[:, P * s : P * (s + 1)],
+                    rhs=v1_codes[h][:].bitcast(FP8X4), rhs_scale=v1_plane[h][:], start=True, stop=True)
+                nc.scalar.activation(squared[:, cols], acc[:], ACT.Relu)
+                if s == 0:
+                    nc.scalar.activation(squared[:, cols], squared[:, cols], ACT.Square)
+                    nc.gpsimd.tensor_tensor(vals[:, cols], squared[:, cols], wg_tiles[0, 0][:, cols], MULT)
+            if s > 0:
+                nc.scalar.activation(squared[:], squared[:], ACT.Square)
+                nc.gpsimd.tensor_tensor(vals[:], squared[:], wg_tiles[0, s % 4][:], MULT)
+            opaque_values.setdefault(s, vals)
+
+        def translucent(s):
+            b, t = divmod(s, 4)
+            if s == 0:
+                gate = new_tile([P, S], F32, "gate0")[:]
+            else:
+                gate = z_slot(s - 1).bitcast(F32)
+            colour = new_tile([P, S], F32, "colour%d" % s, "colour", 3)
+            at = WOVEN_AT[2] + 2 * KIB if s == PAGES - 1 else MIX_AT[(s + 1) % 3] + 4 * KIB
+            vals = placed_tile([P, S], F32, "translucent%d" % s, at)
+            for h in range(2):
+                cols = slice(h * BANK, (h + 1) * BANK)
+                acc = bank()
+                nc.tensor.matmul_mx(
+                    out=acc[:], lhsT=w3_codes[:, P * s : P * (s + 1)].bitcast(FP8X4),
+                    lhsT_scale=w3_plane[:, P * s : P * (s + 1)],
+                    rhs=v2_codes[:, cols].bitcast(FP8X4), rhs_scale=v2_plane[:, cols], start=True, stop=True)
+                nc.scalar.activation(gate[:, cols], acc[:], ACT.Sigmoid)
+            nc.gpsimd.tensor_tensor(gate, gate, wg_tiles[1, t][:], MULT)
+            for h in range(2):
+                cols = slice(h * BANK, (h + 1) * BANK)
+                acc = bank()
+                nc.tensor.matmul_mx(
+                    out=acc[:], lhsT=w2_codes[b][:, P * t : P * (t + 1)].bitcast(FP8X4),
+                    lhsT_scale=w2_plane[b][:, P * t : P * (t + 1)],
+                    rhs=v2_codes[:, cols].bitcast(FP8X4), rhs_scale=v2_plane[:, cols], start=True, stop=True)
+                nc.scalar.copy(colour[:, cols], acc[:])
+            nc.gpsimd.tensor_tensor(vals[:], colour[:], gate, MULT)
+            translucent_values.setdefault(s, vals)
+
+        def scatter_opaque(s):
+            page = placed_tile([P, T2], F32, "page_%d" % s, PAGE_AT[s % PAGE_SLOTS])
+            pages.setdefault(s, page)
+            nc.vector.tensor_copy(page[:].indirect(idx3[:]), opaque_values[s][:])
+
+        def scatter_translucent(s):
+            nc.vector.tensor_copy(pages[s][:].indirect(idx4[:]), translucent_values[s][:])
+
+        z_codes = {}
+
+        def apply_mix(s):
+            last = s == PAGES - 1
+            width = BANK if last else 2 * BANK
+            for start in range(0, T2, width):
+                cols = slice(start, start + width)
+                (nc.vector if last else nc.gpsimd).tensor_tensor(
+                    z_slot(s)[:, cols], pages[s][:, cols], mix_tiles[s][:, cols], MULT)
+
+        def weave(b, c, on_vector):
+            woven = placed_tile([P, 4 * BANK], BF16, "woven%d_%d" % (b, c), WOVEN_AT[c % 3])
+            dst = woven[:].rearrange("p (m i t) -> p m t i", i=4, t=4)
+            src = z_rows[b][:].rearrange("p (t c m i) -> p c m t i", t=4, c=CHUNKS, i=4)[:, c]
+            if on_vector:
+                nc.vector.tensor_copy(dst, src)
+            else:
+                nc.scalar.copy(dst, src)
+            return woven
+
+        def quantise_z(b, c, woven):
+            codes = new_tile([P, BANK], U32, "z_codes%d_%d" % (b, c))
+            plane = new_tile([P, BANK], U8, "z_plane%d_%d" % (b, c))
+            nc.vector.quantize_mx(out=codes[:].bitcast(FP8X4), scales=plane[:], in_=woven[:])
+            z_codes.setdefault((b, c), (codes, plane))
+
+        w4_codes = new_tile([P, 2 * N], U32, "w4_codes")
+        w4_plane = new_tile([P, 2 * N], U8, "w4_plane")
+
+        def quantise_w4():
+            grouped = placed_tile([P, 2, N * 4], BF16, "w4_bf", PAGE_AT[3])
+            for b in range(2):
+                nc.scalar.copy(
+                    grouped[:, b].rearrange("p (n i t) -> p n t i", i=4, t=4),
+                    w4_raw[:, b].rearrange("p t (n i) -> p n t i", i=4))
+            nc.vector.quantize_mx(
+                out=w4_codes[:].bitcast(FP8X4), scales=w4_plane[:], in_=grouped[:].rearrange("p b x -> p (b x)"))
+
+        def shade(acc, b, c, half):
+            codes, plane = z_codes[b, c]
+            cols = slice(b * N + half * P, b * N + (half + 1) * P)
+            nc.tensor.matmul_mx(
+                out=acc[:], lhsT=w4_codes[:, cols].bitcast(FP8X4), lhsT_scale=w4_plane[:, cols],
+                rhs=codes[:].bitcast(FP8X4), rhs_scale=plane[:], start=(b == 0), stop=(b == 1))
+
+        opaque(0)
+        scatter_opaque(0)
+        nc.vector.tensor_copy(
+            w3_plane[:].rearrange("p (b t m) -> p b t m", b=2, t=4),
+            w3_sraw[:].rearrange("p (b m t) -> p b t m", b=2, t=4))
+        nc.vector.tensor_copy(
+            w3_codes[:].rearrange("p (b t m) -> p b t m", b=2, t=4),
+            w3_raw[:].rearrange("p (b m t) -> p b t m", b=2, t=4))
+        quantise_w2(0)
+        opaque(1)
+        scatter_opaque(1)
+        load_mix(0)
+        load_wg(1, 2)
+        load_wg(1, 3)
+        translucent(0)
+        scatter_translucent(0)
+        quantise_w2(1)
+        quantise_w4()
+        for s in range(PAGES - 1):
+            if s + 2 < PAGES:
+                opaque(s + 2)
+                scatter_opaque(s + 2)
+            translucent(s + 1)
+            scatter_translucent(s + 1)
+            apply_mix(s)
+            load_mix(s + 1)
+            if s == 3:
+                for c in range(CHUNKS):
+                    quantise_z(0, c, weave(0, c, False))
+
+        accs = {}
+        for c in range(CHUNKS):
+            for half in range(2):
+                accs.setdefault((c, half), bank())
+                shade(accs[c, half], 0, c, half)
+        apply_mix(PAGES - 1)
+        woven = [weave(1, c, c % 2 == 1) for c in range(CHUNKS - 1)]
+        for c in range(CHUNKS):
+            quantise_z(1, c, woven[c])
+            if c == 0:
+                woven.append(weave(1, CHUNKS - 1, True))
+            for half in range(2):
+                shade(accs[c, half], 1, c, half)
+                result = new_tile([P, BANK], F32, "result%d_%d" % (c, half), "result", 4)
+                if c >= CHUNKS - 2 and half == 1:
+                    nc.vector.tensor_copy(result[:], accs[c, half][:])
+                else:
+                    nc.scalar.copy(result[:], accs[c, half][:])
+                nc.sync.dma_start(out[half * P : (half + 1) * P, c * BANK : (c + 1) * BANK], result[:])

@@ -18,18 +18,22 @@ P = 128
 BANK = 512
 FLOPS = 2 * (3 * K * H * S + H * N * T2)
 PAGES = H // P
-PAGE_SLOTS = 4
+PAGE_SLOTS = 3
 CHUNKS = T2 // BANK
 KIB = 1024
-PAGE_AT = (0, 17 * KIB, 8 * KIB, 26 * KIB)
+W3_CODES_AT = 0
+W3_PLANE_AT = 4 * KIB
+PAGE_AT = (5 * KIB, 22 * KIB, 13 * KIB)
+TAB2_PLANE_AT = PAGE_AT[0] - 7 * KIB // 2
+TAB2_WORDS_AT = TAB2_PLANE_AT + 4 * KIB
 W3_SCALES_AT = PAGE_AT[1] - KIB // 2
 W3_WORDS_AT = W3_SCALES_AT + KIB
-W2_ROUNDED_AT = (W3_WORDS_AT + 4 * KIB, PAGE_AT[2])
-MIX_AT = (34 * KIB, 42 * KIB, 50 * KIB)
-WOVEN_AT = (66 * KIB, 58 * KIB, 62 * KIB)
-TAB1_PLANE_AT = 70 * KIB
-TAB2_PLANE_AT = 74 * KIB
-Z_AT = (79 * KIB, 95 * KIB)
+W2_ROUNDED_AT = W3_WORDS_AT + 4 * KIB
+MIX_AT = (31 * KIB, 39 * KIB, 47 * KIB)
+WOVEN_AT = 55 * KIB
+FIRST_TRANSLUCENT_AT = 71 * KIB
+TAB1_PLANE_AT = 75 * KIB
+Z_AT = (80 * KIB, 96 * KIB)
 
 
 def tile_list_deferred_tile_shading_kernel(
@@ -90,7 +94,7 @@ def tile_list_deferred_tile_shading_kernel(
                 nc.sync.dma_start(wg_tiles[stream, t][32 * q : 32 * q + 32, :], src)
 
         idx1 = load_list(offs, "idx1")
-        tab1_rows = load_scale_rows_bare(tab_scales, placed_tile([P, T], U8, "tab1_rows", WOVEN_AT[1]))
+        tab1_rows = load_scale_rows_bare(tab_scales, placed_tile([P, T], U8, "tab1_rows", WOVEN_AT))
         w1_raw = new_tile([P, 2 * H], U8, "w1_raw")
         nc.sync.dma_start(w1_raw[:].bitcast(I32), w1_words[0].bitcast(I32))
         tab1_w = placed_tile([P, T], I32, "tab1_w", Z_AT[0])
@@ -100,9 +104,9 @@ def tile_list_deferred_tile_shading_kernel(
         w1_rows = load_scale_rows_bare(w1_scales, new_tile([P, H], U8, "w1_rows"))
         idx2 = load_list(offs2, "idx2")
         idx3 = load_list(offs3, "idx3")
-        tab2_w = placed_tile([P, T], I32, "tab2_w", PAGE_AT[0])
-        load_wg(0, 0)
+        tab2_w = placed_tile([P, T], I32, "tab2_w", TAB2_WORDS_AT)
         nc.sync.dma_start(tab2_w[:], tab2_words[0].rearrange("p n i -> p (n i)").bitcast(I32))
+        load_wg(0, 0)
         tab2_s = load_scale_rows(nc.gpsimd, nc.gpsimd, tab2_scales, placed_tile([P, T], U8, "tab2_s", TAB2_PLANE_AT))
         w3_sraw = load_scale_rows(nc.gpsimd, nc.gpsimd, w3_scales, placed_tile([P, H], U8, "w3_sraw", W3_SCALES_AT))
         tab1_s = fill_plane(tab1_rows, placed_tile([P, T], U8, "tab1_s", TAB1_PLANE_AT))
@@ -124,7 +128,7 @@ def tile_list_deferred_tile_shading_kernel(
         load_w2(1)
         load_wg(1, 1)
         load_wg(0, 3)
-        w4_raw = placed_tile([P, 2, 4, N], F32, "w4_raw", WOVEN_AT[2])
+        w4_raw = placed_tile([P, 2, 4, N], F32, "w4_raw", WOVEN_AT + 8 * KIB)
         nc.sync.dma_start(w4_raw[:].rearrange("p b t n -> p b (t n)"), w4.rearrange("(b p t) n -> p b (t n)", b=2, t=4))
 
         w1_codes = new_tile([P, 2 * H], U8, "w1_codes")
@@ -132,40 +136,56 @@ def tile_list_deferred_tile_shading_kernel(
         nc.vector.tensor_copy(
             w1_codes[:].bitcast(U16).rearrange("p (b t m) -> p b t m", b=2, t=4),
             w1_raw[:].bitcast(U16).rearrange("p (b m t) -> p b t m", b=2, t=4))
-        w1_sraw = fill_plane(w1_rows, new_tile([P, H], U8, "w1_sraw"))
+
+        halves = [idx1[:, h * BANK // 16 : (h + 1) * BANK // 16] for h in range(2)]
+        v1_plane = [new_tile([P, BANK], U8, "v1_plane%d" % h) for h in range(2)]
+        v1_codes = [new_tile([P, BANK], U32, "v1_codes%d" % h) for h in range(2)]
+        for h in range(2):
+            nc.vector.tensor_copy(v1_plane[h][:], tab1_s[:].indirect(halves[h]))
+        for h in range(2):
+            nc.vector.tensor_copy(v1_codes[h][:], tab1_w[:].bitcast(U32).indirect(halves[h]))
+        w1_sraw = fill_plane(w1_rows, placed_tile([P, H], U8, "w1_sraw", TAB1_PLANE_AT + KIB // 2))
         nc.vector.tensor_copy(
             w1_plane[:].rearrange("p (b t m) -> p b t m", b=2, t=4),
             w1_sraw[:].rearrange("p (b m t) -> p b t m", b=2, t=4))
-
-        v1_codes, v1_plane = [], []
-        for h in range(2):
-            cols = slice(h * BANK // 16, (h + 1) * BANK // 16)
-            codes = new_tile([P, BANK], U32, "v1_codes%d" % h)
-            plane = new_tile([P, BANK], U8, "v1_plane%d" % h)
-            nc.vector.tensor_copy(codes[:], tab1_w[:].bitcast(U32).indirect(idx1[:, cols]))
-            nc.vector.tensor_copy(plane[:], tab1_s[:].indirect(idx1[:, cols]))
-            v1_codes.append(codes)
-            v1_plane.append(plane)
-        v2_codes = new_tile([P, S], U32, "v2_codes")
+        v2_codes = placed_tile([P, S], U32, "v2_codes", TAB1_PLANE_AT + KIB)
         v2_plane = placed_tile([P, S], U8, "v2_plane", TAB1_PLANE_AT)
         nc.vector.tensor_copy(v2_plane[:], tab2_s[:].indirect(idx2[:]))
         nc.vector.tensor_copy(v2_codes[:], tab2_w[:].bitcast(U32).indirect(idx2[:]))
 
-        w3_codes = placed_tile([P, H], I32, "w3_codes", TAB2_PLANE_AT + KIB)
-        w3_plane = placed_tile([P, H], U8, "w3_plane", TAB2_PLANE_AT)
+        w3_codes = placed_tile([P, H], I32, "w3_codes", W3_CODES_AT)
+        w3_plane = placed_tile([P, H], U8, "w3_plane", W3_PLANE_AT)
 
         w2_codes, w2_plane = [], []
 
-        def quantise_w2(b):
-            grouped = placed_tile([P, 4 * BANK], BF16, "w2_bf%d" % b, W2_ROUNDED_AT[b])
+        def round_w2(b, rounded):
             nc.scalar.copy(
-                grouped[:].rearrange("p (t m i) -> p m i t", t=4, i=4),
+                rounded.rearrange("p (t m i) -> p m i t", t=4, i=4),
                 w2_raw[b][:].rearrange("p i (m t) -> p m i t", t=4))
-            codes = new_tile([P, BANK], U32, "w2_codes%d" % b)
-            plane = new_tile([P, BANK], U8, "w2_plane%d" % b)
-            nc.vector.quantize_mx(out=codes[:].bitcast(FP8X4), scales=plane[:], in_=grouped[:])
-            w2_codes.append(codes)
-            w2_plane.append(plane)
+
+        def quantise_first_w2():
+            rounded = placed_tile([P, 4 * BANK], BF16, "w2_rounded", W2_ROUNDED_AT)
+            round_w2(0, rounded[:])
+            codes = new_tile([P, BANK], U32, "w2_codes0")
+            plane = new_tile([P, BANK], U8, "w2_plane0")
+            nc.vector.quantize_mx(out=codes[:].bitcast(FP8X4), scales=plane[:], in_=rounded[:])
+            w2_codes.append(codes[:])
+            w2_plane.append(plane[:])
+
+        def quantise_late_weights():
+            rounded = placed_tile([P, 8 * BANK], BF16, "late_rounded", WOVEN_AT)
+            round_w2(1, rounded[:, 0 : 4 * BANK])
+            for b in range(2):
+                cols = slice(4 * (BANK + b * N), 4 * (BANK + (b + 1) * N))
+                nc.scalar.copy(
+                    rounded[:, cols].rearrange("p (n i t) -> p n t i", i=4, t=4),
+                    w4_raw[:, b].rearrange("p t (n i) -> p n t i", i=4))
+            codes = placed_tile([P, 2 * BANK], U32, "late_codes", FIRST_TRANSLUCENT_AT)
+            plane = new_tile([P, 2 * BANK], U8, "late_plane")
+            nc.vector.quantize_mx(out=codes[:].bitcast(FP8X4), scales=plane[:], in_=rounded[:])
+            w2_codes.append(codes[:, 0:BANK])
+            w2_plane.append(plane[:, 0:BANK])
+            return codes[:, BANK:], plane[:, BANK:]
 
         pages = {}
         mix_tiles = {}
@@ -186,108 +206,110 @@ def tile_list_deferred_tile_shading_kernel(
                 z_rows.setdefault(b, placed_tile([P, 4 * T2], BF16, "z_rows%d" % b, Z_AT[b]))
             return z_rows[b][:, t * T2 : (t + 1) * T2]
 
-        def opaque(s):
+        squares = {}
+        gates = {}
+        colours = {}
+
+        def product(acc, codes, plane, dtype, moving, moving_plane):
+            nc.tensor.matmul_mx(
+                out=acc[:], lhsT=codes.bitcast(dtype), lhsT_scale=plane,
+                rhs=moving.bitcast(FP8X4), rhs_scale=moving_plane, start=True, stop=True)
+
+        def opaque_layer(s):
             squared = new_tile([P, S], F32, "squared%d" % s, "squared", 3)
-            vals = placed_tile([P, S], F32, "opaque%d" % s, MIX_AT[s % 3])
+            rectified = placed_tile([P, S], F32, "rectified1", W2_ROUNDED_AT) if s == 1 else squared
             for h in range(2):
                 cols = slice(h * BANK, (h + 1) * BANK)
                 acc = bank()
-                nc.tensor.matmul_mx(
-                    out=acc[:], lhsT=w1_codes[:, 2 * P * s : 2 * P * (s + 1)].bitcast(FP4X4),
-                    lhsT_scale=w1_plane[:, P * s : P * (s + 1)],
-                    rhs=v1_codes[h][:].bitcast(FP8X4), rhs_scale=v1_plane[h][:], start=True, stop=True)
-                nc.scalar.activation(squared[:, cols], acc[:], ACT.Relu)
+                product(acc, w1_codes[:, 2 * P * s : 2 * P * (s + 1)], w1_plane[:, P * s : P * (s + 1)], FP4X4,
+                        v1_codes[h][:], v1_plane[h][:])
+                nc.scalar.activation(rectified[:, cols], acc[:], ACT.Relu)
                 if s == 0:
                     nc.scalar.activation(squared[:, cols], squared[:, cols], ACT.Square)
-                    nc.gpsimd.tensor_tensor(vals[:, cols], squared[:, cols], wg_tiles[0, 0][:, cols], MULT)
             if s > 0:
-                nc.scalar.activation(squared[:], squared[:], ACT.Square)
-                nc.gpsimd.tensor_tensor(vals[:], squared[:], wg_tiles[0, s % 4][:], MULT)
-            opaque_values.setdefault(s, vals)
+                nc.scalar.activation(squared[:], rectified[:], ACT.Square)
+            squares.setdefault(s, squared)
 
-        def translucent(s):
+        def translucent_layer(s):
             b, t = divmod(s, 4)
             if s == 0:
-                gate = new_tile([P, S], F32, "gate0")[:]
+                gate = placed_tile([P, S], F32, "gate0", MIX_AT[2])
+                colour = placed_tile([P, S], F32, "colour0", WOVEN_AT)[:]
             else:
-                gate = z_slot(s - 1).bitcast(F32)
-            colour = new_tile([P, S], F32, "colour%d" % s, "colour", 3)
-            at = WOVEN_AT[2] + 2 * KIB if s == PAGES - 1 else MIX_AT[(s + 1) % 3] + 4 * KIB
-            vals = placed_tile([P, S], F32, "translucent%d" % s, at)
+                gate = new_tile([P, S], F32, "gate%d" % s, "gate", 3)
+                colour = z_slot(s - 1).bitcast(F32)
             for h in range(2):
                 cols = slice(h * BANK, (h + 1) * BANK)
                 acc = bank()
-                nc.tensor.matmul_mx(
-                    out=acc[:], lhsT=w3_codes[:, P * s : P * (s + 1)].bitcast(FP8X4),
-                    lhsT_scale=w3_plane[:, P * s : P * (s + 1)],
-                    rhs=v2_codes[:, cols].bitcast(FP8X4), rhs_scale=v2_plane[:, cols], start=True, stop=True)
+                product(acc, w3_codes[:, P * s : P * (s + 1)], w3_plane[:, P * s : P * (s + 1)], FP8X4,
+                        v2_codes[:, cols], v2_plane[:, cols])
                 nc.scalar.activation(gate[:, cols], acc[:], ACT.Sigmoid)
-            nc.gpsimd.tensor_tensor(gate, gate, wg_tiles[1, t][:], MULT)
             for h in range(2):
                 cols = slice(h * BANK, (h + 1) * BANK)
                 acc = bank()
-                nc.tensor.matmul_mx(
-                    out=acc[:], lhsT=w2_codes[b][:, P * t : P * (t + 1)].bitcast(FP8X4),
-                    lhsT_scale=w2_plane[b][:, P * t : P * (t + 1)],
-                    rhs=v2_codes[:, cols].bitcast(FP8X4), rhs_scale=v2_plane[:, cols], start=True, stop=True)
+                product(acc, w2_codes[b][:, P * t : P * (t + 1)], w2_plane[b][:, P * t : P * (t + 1)], FP8X4,
+                        v2_codes[:, cols], v2_plane[:, cols])
                 nc.scalar.copy(colour[:, cols], acc[:])
-            nc.gpsimd.tensor_tensor(vals[:], colour[:], gate, MULT)
+            gates.setdefault(s, gate)
+            colours.setdefault(s, colour)
+
+        def expose_opaque(s):
+            vals = placed_tile([P, S], F32, "opaque%d" % s, MIX_AT[s % 3])
+            width = BANK if s == 0 else S
+            for start in range(0, S, width):
+                cols = slice(start, start + width)
+                nc.gpsimd.tensor_tensor(vals[:, cols], squares[s][:, cols], wg_tiles[0, s % 4][:, cols], MULT)
+            opaque_values.setdefault(s, vals)
+
+        def expose_translucent(s):
+            at = FIRST_TRANSLUCENT_AT if s == 0 else MIX_AT[(s + 1) % 3] + 4 * KIB
+            vals = placed_tile([P, S], F32, "translucent%d" % s, at)
+            nc.gpsimd.tensor_tensor(vals[:], gates[s][:], wg_tiles[1, s % 4][:], MULT)
+            nc.gpsimd.tensor_tensor(vals[:], vals[:], colours[s], MULT)
             translucent_values.setdefault(s, vals)
 
         def scatter_opaque(s):
-            page = placed_tile([P, T2], F32, "page_%d" % s, PAGE_AT[s % PAGE_SLOTS])
+            expose_opaque(s)
+            page = placed_tile([P, T2], F32, "page_%d" % s, {3: WOVEN_AT, PAGES - 1: WOVEN_AT + 4 * KIB}.get(s, PAGE_AT[s % PAGE_SLOTS]))
             pages.setdefault(s, page)
             nc.vector.tensor_copy(page[:].indirect(idx3[:]), opaque_values[s][:])
 
         def scatter_translucent(s):
+            expose_translucent(s)
             nc.vector.tensor_copy(pages[s][:].indirect(idx4[:]), translucent_values[s][:])
 
         z_codes = {}
 
-        def apply_mix(s):
-            last = s == PAGES - 1
-            width = BANK if last else 2 * BANK
-            for start in range(0, T2, width):
-                cols = slice(start, start + width)
-                (nc.vector if last else nc.gpsimd).tensor_tensor(
-                    z_slot(s)[:, cols], pages[s][:, cols], mix_tiles[s][:, cols], MULT)
+        def apply_mix(s, engine, cols):
+            engine.tensor_tensor(z_slot(s)[:, cols], pages[s][:, cols], mix_tiles[s][:, cols], MULT)
 
-        def weave(b, c, on_vector):
-            woven = placed_tile([P, 4 * BANK], BF16, "woven%d_%d" % (b, c), WOVEN_AT[c % 3])
-            dst = woven[:].rearrange("p (m i t) -> p m t i", i=4, t=4)
-            src = z_rows[b][:].rearrange("p (t c m i) -> p c m t i", t=4, c=CHUNKS, i=4)[:, c]
-            if on_vector:
-                nc.vector.tensor_copy(dst, src)
-            else:
-                nc.scalar.copy(dst, src)
+        def weave(b, first, count, on_vector):
+            woven = placed_tile([P, count, 4 * BANK], BF16, "woven%d_%d" % (b, first), (WOVEN_AT, PAGE_AT[0])[b] + first * 4 * KIB)
+            for c in range(count):
+                dst = woven[:, c].rearrange("p (m i t) -> p m t i", i=4, t=4)
+                src = z_rows[b][:].rearrange("p (t c m i) -> p c m t i", t=4, c=CHUNKS, i=4)[:, first + c]
+                if on_vector:
+                    nc.vector.tensor_copy(dst, src)
+                else:
+                    nc.scalar.copy(dst, src)
             return woven
 
-        def quantise_z(b, c, woven):
-            codes = new_tile([P, BANK], U32, "z_codes%d_%d" % (b, c))
-            plane = new_tile([P, BANK], U8, "z_plane%d_%d" % (b, c))
-            nc.vector.quantize_mx(out=codes[:].bitcast(FP8X4), scales=plane[:], in_=woven[:])
-            z_codes.setdefault((b, c), (codes, plane))
-
-        w4_codes = new_tile([P, 2 * N], U32, "w4_codes")
-        w4_plane = new_tile([P, 2 * N], U8, "w4_plane")
-
-        def quantise_w4():
-            grouped = placed_tile([P, 2, N * 4], BF16, "w4_bf", PAGE_AT[3])
-            for b in range(2):
-                nc.scalar.copy(
-                    grouped[:, b].rearrange("p (n i t) -> p n t i", i=4, t=4),
-                    w4_raw[:, b].rearrange("p t (n i) -> p n t i", i=4))
-            nc.vector.quantize_mx(
-                out=w4_codes[:].bitcast(FP8X4), scales=w4_plane[:], in_=grouped[:].rearrange("p b x -> p (b x)"))
+        def quantise_z(b, first, count, woven):
+            codes = new_tile([P, count * BANK], U32, "z_codes%d_%d" % (b, first))
+            plane = new_tile([P, count * BANK], U8, "z_plane%d_%d" % (b, first))
+            nc.vector.quantize_mx(out=codes[:].bitcast(FP8X4), scales=plane[:], in_=woven[:].rearrange("p c x -> p (c x)"))
+            for c in range(count):
+                cols = slice(c * BANK, (c + 1) * BANK)
+                z_codes.setdefault((b, first + c), (codes[:, cols], plane[:, cols]))
 
         def shade(acc, b, c, half):
             codes, plane = z_codes[b, c]
             cols = slice(b * N + half * P, b * N + (half + 1) * P)
             nc.tensor.matmul_mx(
                 out=acc[:], lhsT=w4_codes[:, cols].bitcast(FP8X4), lhsT_scale=w4_plane[:, cols],
-                rhs=codes[:].bitcast(FP8X4), rhs_scale=plane[:], start=(b == 0), stop=(b == 1))
+                rhs=codes.bitcast(FP8X4), rhs_scale=plane, start=(b == 0), stop=(b == 1))
 
-        opaque(0)
+        opaque_layer(0)
         scatter_opaque(0)
         nc.vector.tensor_copy(
             w3_plane[:].rearrange("p (b t m) -> p b t m", b=2, t=4),
@@ -295,43 +317,60 @@ def tile_list_deferred_tile_shading_kernel(
         nc.vector.tensor_copy(
             w3_codes[:].rearrange("p (b t m) -> p b t m", b=2, t=4),
             w3_raw[:].rearrange("p (b m t) -> p b t m", b=2, t=4))
-        quantise_w2(0)
-        opaque(1)
+        opaque_layer(1)
+        quantise_first_w2()
         scatter_opaque(1)
         load_mix(0)
         load_wg(1, 2)
         load_wg(1, 3)
-        translucent(0)
+        translucent_layer(0)
         scatter_translucent(0)
-        quantise_w2(1)
-        quantise_w4()
+        opaque_layer(2)
+        translucent_layer(1)
+        w4_codes, w4_plane = quantise_late_weights()
         for s in range(PAGES - 1):
             if s + 2 < PAGES:
-                opaque(s + 2)
                 scatter_opaque(s + 2)
-            translucent(s + 1)
             scatter_translucent(s + 1)
-            apply_mix(s)
+            if s < 3:
+                opaque_layer(s + 3)
+                translucent_layer(s + 2)
+            if s == 3:
+                for ahead in range(s + 2, PAGES):
+                    if ahead + 1 < PAGES:
+                        opaque_layer(ahead + 1)
+                    translucent_layer(ahead)
+            for half in range(2):
+                apply_mix(s, nc.gpsimd, slice(half * S, (half + 1) * S))
             load_mix(s + 1)
             if s == 3:
-                for c in range(CHUNKS):
-                    quantise_z(0, c, weave(0, c, False))
+                for first in range(0, CHUNKS, 2):
+                    quantise_z(0, first, 2, weave(0, first, 2, False))
 
         accs = {}
         for c in range(CHUNKS):
             for half in range(2):
                 accs.setdefault((c, half), bank())
                 shade(accs[c, half], 0, c, half)
-        apply_mix(PAGES - 1)
-        woven = [weave(1, c, c % 2 == 1) for c in range(CHUNKS - 1)]
+        WEAVE_ON_VECTOR = (2, 3)
+        COPY_ON_VECTOR = (7,)
+        woven = {}
         for c in range(CHUNKS):
-            quantise_z(1, c, woven[c])
-            if c == 0:
-                woven.append(weave(1, CHUNKS - 1, True))
+            if c not in WEAVE_ON_VECTOR:
+                apply_mix(PAGES - 1, nc.vector, slice(c * BANK, (c + 1) * BANK))
+                woven.setdefault(c, weave(1, c, 1, False))
+        order = list(WEAVE_ON_VECTOR) + list(woven)
+        for c in order:
+            if c in WEAVE_ON_VECTOR:
+                apply_mix(PAGES - 1, nc.vector, slice(c * BANK, (c + 1) * BANK))
+                woven.setdefault(c, weave(1, c, 1, True))
+            quantise_z(1, c, 1, woven[c])
             for half in range(2):
                 shade(accs[c, half], 1, c, half)
-                result = new_tile([P, BANK], F32, "result%d_%d" % (c, half), "result", 4)
-                if c >= CHUNKS - 2 and half == 1:
+        for k, c in enumerate(order):
+            for half in range(2):
+                result = new_tile([P, BANK], F32, "result%d_%d" % (c, half), "result", 8)
+                if 2 * k + half in COPY_ON_VECTOR:
                     nc.vector.tensor_copy(result[:], accs[c, half][:])
                 else:
                     nc.scalar.copy(result[:], accs[c, half][:])

@@ -21,19 +21,27 @@ PAGES = H // P
 PAGE_SLOTS = 3
 CHUNKS = T2 // BANK
 KIB = 1024
+HALF = KIB // 2
 W3_CODES_AT = 0
 W3_PLANE_AT = 4 * KIB
-PAGE_AT = (5 * KIB, 22 * KIB, 13 * KIB)
-TAB2_PLANE_AT = PAGE_AT[0] - 7 * KIB // 2
+FIRST_SQUARED_AT = KIB
+TAB2_PLANE_AT = 5 * KIB
 TAB2_WORDS_AT = TAB2_PLANE_AT + 4 * KIB
-W3_SCALES_AT = PAGE_AT[1] - KIB // 2
+PAGE_AT = (TAB2_WORDS_AT - HALF, TAB2_WORDS_AT + 16 * KIB + HALF, TAB2_WORDS_AT + 8 * KIB - HALF)
+W3_SCALES_AT = PAGE_AT[1] - HALF
 W3_WORDS_AT = W3_SCALES_AT + KIB
 W2_ROUNDED_AT = W3_WORDS_AT + 4 * KIB
-MIX_AT = (31 * KIB, 39 * KIB, 47 * KIB)
-WOVEN_AT = 55 * KIB
-FIRST_TRANSLUCENT_AT = 71 * KIB
-TAB1_PLANE_AT = 75 * KIB
-Z_AT = (80 * KIB, 96 * KIB)
+W2_PLANE_AT = PAGE_AT[1] + 12 * KIB
+MIX_AT = (W2_PLANE_AT + 3 * HALF, W2_PLANE_AT + 19 * HALF, W2_PLANE_AT + 35 * HALF)
+FIRST_PLANES_AT = (MIX_AT[2] + 8 * KIB, MIX_AT[0] - KIB)
+LATE_PLANE_AT = MIX_AT[2] + 9 * KIB
+WOVEN_AT = LATE_PLANE_AT + KIB
+TAB1_PLANE_AT = WOVEN_AT + 16 * KIB
+Z_AT = (TAB1_PLANE_AT + 5 * KIB, TAB1_PLANE_AT + 21 * KIB)
+PAIRS_AT = Z_AT[1] + 12 * KIB
+OPAQUE_IN_SLOT = (4 * KIB, 0, 0)
+TRANSLUCENT_IN_SLOT = (0, 4 * KIB, 4 * KIB)
+TRANSLUCENT_AT = {0: PAGE_AT[1] + 8 * KIB, 1: MIX_AT[2] + 11 * HALF, 4: MIX_AT[2] + 9 * HALF, 5: MIX_AT[0] - HALF}
 
 
 def tile_list_deferred_tile_shading_kernel(
@@ -55,11 +63,11 @@ def tile_list_deferred_tile_shading_kernel(
 
         bank_count = [0]
 
-        def bank():
+        def bank(back=0):
             i = bank_count[0]
             bank_count.append(i + 1)
             bank_count.remove(i)
-            return ps.tile([P, BANK], F32, name="bank%d" % i, tag="bank%d" % (i % 8))
+            return ps.tile([P, BANK], F32, name="bank%d" % i, tag="bank%d" % ((i - back) % 8))
 
         def load_list(src, name):
             dst = lists.tile([P, S // 16], U16, name=name)
@@ -115,7 +123,7 @@ def tile_list_deferred_tile_shading_kernel(
         w2_raw = []
 
         def load_w2(b):
-            raw = placed_tile([P, 4, BANK], F32, "w2_raw%d" % b, Z_AT[1] + 8 * KIB * b)
+            raw = placed_tile([P, 4, BANK], F32, "w2_raw%d" % b, PAIRS_AT + 8 * KIB * b)
             nc.sync.dma_start(raw[:], w2[:, b * BANK : (b + 1) * BANK].rearrange("(p i) c -> p i c", i=4))
             w2_raw.append(raw)
 
@@ -153,9 +161,6 @@ def tile_list_deferred_tile_shading_kernel(
         nc.vector.tensor_copy(v2_plane[:], tab2_s[:].indirect(idx2[:]))
         nc.vector.tensor_copy(v2_codes[:], tab2_w[:].bitcast(U32).indirect(idx2[:]))
 
-        w3_codes = placed_tile([P, H], I32, "w3_codes", W3_CODES_AT)
-        w3_plane = placed_tile([P, H], U8, "w3_plane", W3_PLANE_AT)
-
         w2_codes, w2_plane = [], []
 
         def round_w2(b, rounded):
@@ -167,7 +172,7 @@ def tile_list_deferred_tile_shading_kernel(
             rounded = placed_tile([P, 4 * BANK], BF16, "w2_rounded", W2_ROUNDED_AT)
             round_w2(0, rounded[:])
             codes = new_tile([P, BANK], U32, "w2_codes0")
-            plane = new_tile([P, BANK], U8, "w2_plane0")
+            plane = placed_tile([P, BANK], U8, "w2_plane0", W2_PLANE_AT)
             nc.vector.quantize_mx(out=codes[:].bitcast(FP8X4), scales=plane[:], in_=rounded[:])
             w2_codes.append(codes[:])
             w2_plane.append(plane[:])
@@ -180,8 +185,8 @@ def tile_list_deferred_tile_shading_kernel(
                 nc.scalar.copy(
                     rounded[:, cols].rearrange("p (n i t) -> p n t i", i=4, t=4),
                     w4_raw[:, b].rearrange("p t (n i) -> p n t i", i=4))
-            codes = placed_tile([P, 2 * BANK], U32, "late_codes", FIRST_TRANSLUCENT_AT)
-            plane = new_tile([P, 2 * BANK], U8, "late_plane")
+            codes = new_tile([P, 2 * BANK], U32, "late_codes")
+            plane = placed_tile([P, 2 * BANK], U8, "late_plane", LATE_PLANE_AT)
             nc.vector.quantize_mx(out=codes[:].bitcast(FP8X4), scales=plane[:], in_=rounded[:])
             w2_codes.append(codes[:, 0:BANK])
             w2_plane.append(plane[:, 0:BANK])
@@ -194,16 +199,20 @@ def tile_list_deferred_tile_shading_kernel(
 
         def load_mix(s):
             b, t = divmod(s, 4)
-            rows = placed_tile([P, T2], F32, "mix%d" % s, MIX_AT[s % 3])
+            rows = placed_tile([P, T2], F32, "mix%d" % s, WOVEN_AT + 8 * KIB if s == PAGES - 1 else MIX_AT[s % 3])
             nc.sync.dma_start(rows[:], mix[b * K : (b + 1) * K, :].rearrange("(p t) m -> t p m", t=4)[t])
             mix_tiles.setdefault(s, rows)
 
         z_rows = {}
 
-        def z_slot(s):
+        pairs = placed_tile([P, 4 * T2], BF16, "pairs", PAIRS_AT)
+
+        def z_row(s):
             b, t = divmod(s, 4)
+            if s == PAGES - 1:
+                return pairs[:, 2 * T2 :].rearrange("p (m t) -> p t m", t=2)[:, 1]
             if b not in z_rows:
-                z_rows.setdefault(b, placed_tile([P, 4 * T2], BF16, "z_rows%d" % b, Z_AT[b]))
+                z_rows.setdefault(b, placed_tile([P, (4, 3)[b] * T2], BF16, "z_rows%d" % b, Z_AT[b]))
             return z_rows[b][:, t * T2 : (t + 1) * T2]
 
         squares = {}
@@ -216,7 +225,10 @@ def tile_list_deferred_tile_shading_kernel(
                 rhs=moving.bitcast(FP8X4), rhs_scale=moving_plane, start=True, stop=True)
 
         def opaque_layer(s):
-            squared = new_tile([P, S], F32, "squared%d" % s, "squared", 3)
+            if s == 0:
+                squared = placed_tile([P, S], F32, "squared0", FIRST_SQUARED_AT)
+            else:
+                squared = new_tile([P, S], F32, "squared%d" % s, "squared", 3)
             rectified = placed_tile([P, S], F32, "rectified1", W2_ROUNDED_AT) if s == 1 else squared
             for h in range(2):
                 cols = slice(h * BANK, (h + 1) * BANK)
@@ -233,11 +245,11 @@ def tile_list_deferred_tile_shading_kernel(
         def translucent_layer(s):
             b, t = divmod(s, 4)
             if s == 0:
-                gate = placed_tile([P, S], F32, "gate0", MIX_AT[2])
-                colour = placed_tile([P, S], F32, "colour0", WOVEN_AT)[:]
+                gate = placed_tile([P, S], F32, "gate0", WOVEN_AT)
+                colour = placed_tile([P, S], F32, "colour0", MIX_AT[2] + 3 * KIB)[:]
             else:
                 gate = new_tile([P, S], F32, "gate%d" % s, "gate", 3)
-                colour = z_slot(s - 1).bitcast(F32)
+                colour = z_row(s - 1).bitcast(F32)
             for h in range(2):
                 cols = slice(h * BANK, (h + 1) * BANK)
                 acc = bank()
@@ -246,7 +258,7 @@ def tile_list_deferred_tile_shading_kernel(
                 nc.scalar.activation(gate[:, cols], acc[:], ACT.Sigmoid)
             for h in range(2):
                 cols = slice(h * BANK, (h + 1) * BANK)
-                acc = bank()
+                acc = bank(2 if s == 0 else 0)
                 product(acc, w2_codes[b][:, P * t : P * (t + 1)], w2_plane[b][:, P * t : P * (t + 1)], FP8X4,
                         v2_codes[:, cols], v2_plane[:, cols])
                 nc.scalar.copy(colour[:, cols], acc[:])
@@ -254,7 +266,8 @@ def tile_list_deferred_tile_shading_kernel(
             colours.setdefault(s, colour)
 
         def expose_opaque(s):
-            vals = placed_tile([P, S], F32, "opaque%d" % s, MIX_AT[s % 3])
+            at = W2_PLANE_AT if s == 0 else MIX_AT[s % 3] + OPAQUE_IN_SLOT[s % 3]
+            vals = placed_tile([P, S], F32, "opaque%d" % s, at)
             width = BANK if s == 0 else S
             for start in range(0, S, width):
                 cols = slice(start, start + width)
@@ -262,7 +275,7 @@ def tile_list_deferred_tile_shading_kernel(
             opaque_values.setdefault(s, vals)
 
         def expose_translucent(s):
-            at = FIRST_TRANSLUCENT_AT if s == 0 else MIX_AT[(s + 1) % 3] + 4 * KIB
+            at = TRANSLUCENT_AT.get(s, MIX_AT[(s + 1) % 3] + TRANSLUCENT_IN_SLOT[(s + 1) % 3])
             vals = placed_tile([P, S], F32, "translucent%d" % s, at)
             nc.gpsimd.tensor_tensor(vals[:], gates[s][:], wg_tiles[1, s % 4][:], MULT)
             nc.gpsimd.tensor_tensor(vals[:], vals[:], colours[s], MULT)
@@ -270,7 +283,7 @@ def tile_list_deferred_tile_shading_kernel(
 
         def scatter_opaque(s):
             expose_opaque(s)
-            page = placed_tile([P, T2], F32, "page_%d" % s, {3: WOVEN_AT, PAGES - 1: WOVEN_AT + 4 * KIB}.get(s, PAGE_AT[s % PAGE_SLOTS]))
+            page = placed_tile([P, T2], F32, "page_%d" % s, {3: WOVEN_AT, 6: WOVEN_AT, 7: MIX_AT[1] + 4 * KIB}.get(s, PAGE_AT[s % PAGE_SLOTS]))
             pages.setdefault(s, page)
             nc.vector.tensor_copy(page[:].indirect(idx3[:]), opaque_values[s][:])
 
@@ -281,22 +294,33 @@ def tile_list_deferred_tile_shading_kernel(
         z_codes = {}
 
         def apply_mix(s, engine, cols):
-            engine.tensor_tensor(z_slot(s)[:, cols], pages[s][:, cols], mix_tiles[s][:, cols], MULT)
+            engine.tensor_tensor(z_row(s)[:, cols], pages[s][:, cols], mix_tiles[s][:, cols], MULT)
 
-        def weave(b, first, count, on_vector):
-            woven = placed_tile([P, count, 4 * BANK], BF16, "woven%d_%d" % (b, first), (WOVEN_AT, PAGE_AT[0])[b] + first * 4 * KIB)
-            for c in range(count):
-                dst = woven[:, c].rearrange("p (m i t) -> p m t i", i=4, t=4)
-                src = z_rows[b][:].rearrange("p (t c m i) -> p c m t i", t=4, c=CHUNKS, i=4)[:, first + c]
-                if on_vector:
-                    nc.vector.tensor_copy(dst, src)
-                else:
-                    nc.scalar.copy(dst, src)
+        def weave_rows(first):
+            woven = placed_tile([P, 2, 4 * BANK], BF16, "woven0_%d" % first, WOVEN_AT + first * 4 * KIB)
+            for c in range(2):
+                nc.scalar.copy(
+                    woven[:, c].rearrange("p (m i t) -> p m t i", i=4, t=4),
+                    z_rows[0][:].rearrange("p (t c m i) -> p c m t i", t=4, c=CHUNKS, i=4)[:, first + c])
+            return woven
+
+        def weave_pairs(c, on_vector):
+            woven = placed_tile([P, 1, 4 * BANK], BF16, "woven1_%d" % c, PAGE_AT[0] + c * 4 * KIB)
+            word = I32 if on_vector else U32
+            dst = woven[:, 0].bitcast(word).rearrange("p (m h) -> p m h", h=2)
+            src = pairs[:].bitcast(word).rearrange("p (h c m) -> p c m h", h=2, c=CHUNKS)[:, c]
+            if on_vector:
+                nc.vector.tensor_copy(dst, src)
+            else:
+                nc.scalar.copy(dst, src)
             return woven
 
         def quantise_z(b, first, count, woven):
             codes = new_tile([P, count * BANK], U32, "z_codes%d_%d" % (b, first))
-            plane = new_tile([P, count * BANK], U8, "z_plane%d_%d" % (b, first))
+            if b == 0:
+                plane = placed_tile([P, count * BANK], U8, "z_plane0_%d" % first, FIRST_PLANES_AT[first // 2])
+            else:
+                plane = new_tile([P, count * BANK], U8, "z_plane1_%d" % first)
             nc.vector.quantize_mx(out=codes[:].bitcast(FP8X4), scales=plane[:], in_=woven[:].rearrange("p c x -> p (c x)"))
             for c in range(count):
                 cols = slice(c * BANK, (c + 1) * BANK)
@@ -311,10 +335,12 @@ def tile_list_deferred_tile_shading_kernel(
 
         opaque_layer(0)
         scatter_opaque(0)
-        nc.vector.tensor_copy(
+        w3_codes = placed_tile([P, H], I32, "w3_codes", W3_CODES_AT)
+        w3_plane = placed_tile([P, H], U8, "w3_plane", W3_PLANE_AT)
+        nc.gpsimd.tensor_copy(
             w3_plane[:].rearrange("p (b t m) -> p b t m", b=2, t=4),
             w3_sraw[:].rearrange("p (b m t) -> p b t m", b=2, t=4))
-        nc.vector.tensor_copy(
+        nc.gpsimd.tensor_copy(
             w3_codes[:].rearrange("p (b t m) -> p b t m", b=2, t=4),
             w3_raw[:].rearrange("p (b m t) -> p b t m", b=2, t=4))
         opaque_layer(1)
@@ -327,11 +353,14 @@ def tile_list_deferred_tile_shading_kernel(
         scatter_translucent(0)
         opaque_layer(2)
         translucent_layer(1)
-        w4_codes, w4_plane = quantise_late_weights()
         for s in range(PAGES - 1):
-            if s + 2 < PAGES:
+            if s + 3 < PAGES:
                 scatter_opaque(s + 2)
             scatter_translucent(s + 1)
+            if s == 0:
+                w4_codes, w4_plane = quantise_late_weights()
+            if s == 4:
+                quantise_z(0, 2, 2, first_woven[1])
             if s < 3:
                 opaque_layer(s + 3)
                 translucent_layer(s + 2)
@@ -343,33 +372,37 @@ def tile_list_deferred_tile_shading_kernel(
             for half in range(2):
                 apply_mix(s, nc.gpsimd, slice(half * S, (half + 1) * S))
             load_mix(s + 1)
+            if s + 3 == PAGES:
+                scatter_opaque(s + 2)
             if s == 3:
-                for first in range(0, CHUNKS, 2):
-                    quantise_z(0, first, 2, weave(0, first, 2, False))
+                first_woven = [weave_rows(first) for first in range(0, CHUNKS, 2)]
+                quantise_z(0, 0, 2, first_woven[0])
+            if s == 5:
+                nc.scalar.copy(
+                    pairs[:, 0 : 2 * T2].rearrange("p (m i t) -> p m t i", i=4, t=2),
+                    z_rows[1][:, 0 : 2 * T2].rearrange("p (t m i) -> p m t i", t=2, i=4))
+            if s == 6:
+                for half in range(2):
+                    nc.scalar.copy(
+                        pairs[:, 2 * (T2 + half * S) : 2 * (T2 + (half + 1) * S)].rearrange("p (m t) -> p m t", t=2),
+                        z_row(s)[:, half * S : (half + 1) * S].unsqueeze(2).to_broadcast([P, S, 2]))
 
         accs = {}
         for c in range(CHUNKS):
             for half in range(2):
                 accs.setdefault((c, half), bank())
                 shade(accs[c, half], 0, c, half)
-        WEAVE_ON_VECTOR = (2, 3)
-        COPY_ON_VECTOR = (7,)
-        woven = {}
-        for c in range(CHUNKS):
-            if c not in WEAVE_ON_VECTOR:
-                apply_mix(PAGES - 1, nc.vector, slice(c * BANK, (c + 1) * BANK))
-                woven.setdefault(c, weave(1, c, 1, False))
-        order = list(WEAVE_ON_VECTOR) + list(woven)
+        WEAVE_ON_VECTOR = (3,)
+        COPY_ON_VECTOR = (3, 5, 7)
+        order = list(range(CHUNKS))
         for c in order:
-            if c in WEAVE_ON_VECTOR:
-                apply_mix(PAGES - 1, nc.vector, slice(c * BANK, (c + 1) * BANK))
-                woven.setdefault(c, weave(1, c, 1, True))
-            quantise_z(1, c, 1, woven[c])
+            apply_mix(PAGES - 1, nc.vector, slice(c * BANK, (c + 1) * BANK))
+            quantise_z(1, c, 1, weave_pairs(c, c in WEAVE_ON_VECTOR))
             for half in range(2):
                 shade(accs[c, half], 1, c, half)
         for k, c in enumerate(order):
             for half in range(2):
-                result = new_tile([P, BANK], F32, "result%d_%d" % (c, half), "result", 8)
+                result = new_tile([P, BANK], F32, "result%d_%d" % (c, half), "result", 6)
                 if 2 * k + half in COPY_ON_VECTOR:
                     nc.vector.tensor_copy(result[:], accs[c, half][:])
                 else:

@@ -38,10 +38,7 @@ LATE_PLANE_AT = MIX_AT[2] + 9 * KIB
 WOVEN_AT = LATE_PLANE_AT + KIB
 TAB1_PLANE_AT = WOVEN_AT + 16 * KIB
 Z_AT = (TAB1_PLANE_AT + 5 * KIB, TAB1_PLANE_AT + 21 * KIB)
-PAIRS_AT = Z_AT[1] + 12 * KIB
-OPAQUE_IN_SLOT = (4 * KIB, 0, 0)
-TRANSLUCENT_IN_SLOT = (0, 4 * KIB, 4 * KIB)
-TRANSLUCENT_AT = {0: PAGE_AT[1] + 8 * KIB, 1: MIX_AT[2] + 11 * HALF, 4: MIX_AT[2] + 9 * HALF, 5: MIX_AT[0] - HALF}
+SOURCES_SHIFT = {1: 3 * HALF, 4: HALF, 5: -HALF}
 
 
 def tile_list_deferred_tile_shading_kernel(
@@ -92,14 +89,15 @@ def tile_list_deferred_tile_shading_kernel(
                 nc.vector.tensor_copy(plane[live, :].bitcast(I32), rows[live, :].bitcast(I32))
             return plane
 
-        wg_tiles = {}
+        wg_pairs = [new_tile([P, 2, S], F32, "wg_pair%d" % k) for k in range(4)]
 
-        def load_wg(stream, t, quadrants=range(4)):
+        def exposure(stream, t):
+            return wg_pairs[(t + stream - 1) % 4][:, stream]
+
+        def load_wg(stream, t):
             src = (wg1, wg2)[stream].rearrange("(p t) j -> t p j", t=4)[t]
-            if (stream, t) not in wg_tiles:
-                wg_tiles.setdefault((stream, t), new_tile([P, S], F32, "wg%d_%d" % (stream, t)))
-            for q in quadrants:
-                nc.sync.dma_start(wg_tiles[stream, t][32 * q : 32 * q + 32, :], src)
+            for q in range(4):
+                nc.sync.dma_start(exposure(stream, t)[32 * q : 32 * q + 32, :], src)
 
         idx1 = load_list(offs, "idx1")
         tab1_rows = load_scale_rows_bare(tab_scales, placed_tile([P, T], U8, "tab1_rows", WOVEN_AT))
@@ -123,7 +121,7 @@ def tile_list_deferred_tile_shading_kernel(
         w2_raw = []
 
         def load_w2(b):
-            raw = placed_tile([P, 4, BANK], F32, "w2_raw%d" % b, PAIRS_AT + 8 * KIB * b)
+            raw = placed_tile([P, 4, BANK], F32, "w2_raw%d" % b, Z_AT[1] + 8 * KIB * b)
             nc.sync.dma_start(raw[:], w2[:, b * BANK : (b + 1) * BANK].rearrange("(p i) c -> p i c", i=4))
             w2_raw.append(raw)
 
@@ -205,15 +203,18 @@ def tile_list_deferred_tile_shading_kernel(
 
         z_rows = {}
 
-        pairs = placed_tile([P, 4 * T2], BF16, "pairs", PAIRS_AT)
-
         def z_row(s):
             b, t = divmod(s, 4)
-            if s == PAGES - 1:
-                return pairs[:, 2 * T2 :].rearrange("p (m t) -> p t m", t=2)[:, 1]
             if b not in z_rows:
-                z_rows.setdefault(b, placed_tile([P, (4, 3)[b] * T2], BF16, "z_rows%d" % b, Z_AT[b]))
+                z_rows.setdefault(b, placed_tile([P, 4 * T2], BF16, "z_rows%d" % b, Z_AT[b]))
             return z_rows[b][:, t * T2 : (t + 1) * T2]
+
+        activations = {}
+
+        def activation_pair(j):
+            if j not in activations:
+                activations.setdefault(j, new_tile([P, 2, S], F32, "activations%d" % j, "activations", 3))
+            return activations[j]
 
         squares = {}
         gates = {}
@@ -226,10 +227,10 @@ def tile_list_deferred_tile_shading_kernel(
 
         def opaque_layer(s):
             if s == 0:
-                squared = placed_tile([P, S], F32, "squared0", FIRST_SQUARED_AT)
+                squared = placed_tile([P, S], F32, "squared0", FIRST_SQUARED_AT)[:]
             else:
-                squared = new_tile([P, S], F32, "squared%d" % s, "squared", 3)
-            rectified = placed_tile([P, S], F32, "rectified1", W2_ROUNDED_AT) if s == 1 else squared
+                squared = activation_pair(s - 1)[:, 0]
+            rectified = placed_tile([P, S], F32, "rectified1", W2_ROUNDED_AT)[:] if s == 1 else squared
             for h in range(2):
                 cols = slice(h * BANK, (h + 1) * BANK)
                 acc = bank()
@@ -239,16 +240,16 @@ def tile_list_deferred_tile_shading_kernel(
                 if s == 0:
                     nc.scalar.activation(squared[:, cols], squared[:, cols], ACT.Square)
             if s > 0:
-                nc.scalar.activation(squared[:], rectified[:], ACT.Square)
+                nc.scalar.activation(squared, rectified, ACT.Square)
             squares.setdefault(s, squared)
 
         def translucent_layer(s):
             b, t = divmod(s, 4)
             if s == 0:
-                gate = placed_tile([P, S], F32, "gate0", WOVEN_AT)
+                gate = placed_tile([P, S], F32, "gate0", WOVEN_AT)[:]
                 colour = placed_tile([P, S], F32, "colour0", MIX_AT[2] + 3 * KIB)[:]
             else:
-                gate = new_tile([P, S], F32, "gate%d" % s, "gate", 3)
+                gate = activation_pair(s)[:, 1]
                 colour = z_row(s - 1).bitcast(F32)
             for h in range(2):
                 cols = slice(h * BANK, (h + 1) * BANK)
@@ -266,53 +267,53 @@ def tile_list_deferred_tile_shading_kernel(
             colours.setdefault(s, colour)
 
         def expose_opaque(s):
-            at = W2_PLANE_AT if s == 0 else MIX_AT[s % 3] + OPAQUE_IN_SLOT[s % 3]
-            vals = placed_tile([P, S], F32, "opaque%d" % s, at)
+            vals = placed_tile([P, S], F32, "opaque%d" % s, W2_PLANE_AT if s == 0 else MIX_AT[s % 3])
             width = BANK if s == 0 else S
             for start in range(0, S, width):
                 cols = slice(start, start + width)
-                nc.gpsimd.tensor_tensor(vals[:, cols], squares[s][:, cols], wg_tiles[0, s % 4][:, cols], MULT)
-            opaque_values.setdefault(s, vals)
+                nc.gpsimd.tensor_tensor(vals[:, cols], squares[s][:, cols], exposure(0, s % 4)[:, cols], MULT)
+            opaque_values.setdefault(s, vals[:])
 
-        def expose_translucent(s):
-            at = TRANSLUCENT_AT.get(s, MIX_AT[(s + 1) % 3] + TRANSLUCENT_IN_SLOT[(s + 1) % 3])
+        def expose_gate(s):
+            at = PAGE_AT[1] + 8 * KIB if s == 0 else MIX_AT[(s + 1) % 3] + 4 * KIB
             vals = placed_tile([P, S], F32, "translucent%d" % s, at)
-            nc.gpsimd.tensor_tensor(vals[:], gates[s][:], wg_tiles[1, s % 4][:], MULT)
-            nc.gpsimd.tensor_tensor(vals[:], vals[:], colours[s], MULT)
-            translucent_values.setdefault(s, vals)
+            nc.gpsimd.tensor_tensor(vals[:], gates[s], exposure(1, s % 4), MULT)
+            translucent_values.setdefault(s, vals[:])
+
+        def expose_pair(j):
+            vals = placed_tile([P, 2, S], F32, "sources%d" % j, MIX_AT[(j + 1) % 3] + SOURCES_SHIFT.get(j, 0))
+            nc.gpsimd.tensor_tensor(vals[:], activations[j][:], wg_pairs[j % 4][:], MULT)
+            opaque_values.setdefault(j + 1, vals[:, 0])
+            translucent_values.setdefault(j, vals[:, 1])
 
         def scatter_opaque(s):
-            expose_opaque(s)
+            if s not in opaque_values:
+                expose_opaque(s)
             page = placed_tile([P, T2], F32, "page_%d" % s, {3: WOVEN_AT, 6: WOVEN_AT, 7: MIX_AT[1] + 4 * KIB}.get(s, PAGE_AT[s % PAGE_SLOTS]))
             pages.setdefault(s, page)
-            nc.vector.tensor_copy(page[:].indirect(idx3[:]), opaque_values[s][:])
+            nc.vector.tensor_copy(page[:].indirect(idx3[:]), opaque_values[s])
 
         def scatter_translucent(s):
-            expose_translucent(s)
-            nc.vector.tensor_copy(pages[s][:].indirect(idx4[:]), translucent_values[s][:])
+            if s not in translucent_values:
+                expose_gate(s)
+            vals = translucent_values[s]
+            nc.gpsimd.tensor_tensor(vals, vals, colours[s], MULT)
+            nc.vector.tensor_copy(pages[s][:].indirect(idx4[:]), vals)
 
         z_codes = {}
 
         def apply_mix(s, engine, cols):
             engine.tensor_tensor(z_row(s)[:, cols], pages[s][:, cols], mix_tiles[s][:, cols], MULT)
 
-        def weave_rows(first):
-            woven = placed_tile([P, 2, 4 * BANK], BF16, "woven0_%d" % first, WOVEN_AT + first * 4 * KIB)
-            for c in range(2):
-                nc.scalar.copy(
-                    woven[:, c].rearrange("p (m i t) -> p m t i", i=4, t=4),
-                    z_rows[0][:].rearrange("p (t c m i) -> p c m t i", t=4, c=CHUNKS, i=4)[:, first + c])
-            return woven
-
-        def weave_pairs(c, on_vector):
-            woven = placed_tile([P, 1, 4 * BANK], BF16, "woven1_%d" % c, PAGE_AT[0] + c * 4 * KIB)
-            word = I32 if on_vector else U32
-            dst = woven[:, 0].bitcast(word).rearrange("p (m h) -> p m h", h=2)
-            src = pairs[:].bitcast(word).rearrange("p (h c m) -> p c m h", h=2, c=CHUNKS)[:, c]
-            if on_vector:
-                nc.vector.tensor_copy(dst, src)
-            else:
-                nc.scalar.copy(dst, src)
+        def weave(b, first, count, on_vector):
+            woven = placed_tile([P, count, 4 * BANK], BF16, "woven%d_%d" % (b, first), (WOVEN_AT, PAGE_AT[0])[b] + first * 4 * KIB)
+            for c in range(count):
+                dst = woven[:, c].rearrange("p (m i t) -> p m t i", i=4, t=4)
+                src = z_rows[b][:].rearrange("p (t c m i) -> p c m t i", t=4, c=CHUNKS, i=4)[:, first + c]
+                if on_vector:
+                    nc.vector.tensor_copy(dst, src)
+                else:
+                    nc.scalar.copy(dst, src)
             return woven
 
         def quantise_z(b, first, count, woven):
@@ -337,10 +338,10 @@ def tile_list_deferred_tile_shading_kernel(
         scatter_opaque(0)
         w3_codes = placed_tile([P, H], I32, "w3_codes", W3_CODES_AT)
         w3_plane = placed_tile([P, H], U8, "w3_plane", W3_PLANE_AT)
-        nc.gpsimd.tensor_copy(
+        nc.vector.tensor_copy(
             w3_plane[:].rearrange("p (b t m) -> p b t m", b=2, t=4),
             w3_sraw[:].rearrange("p (b m t) -> p b t m", b=2, t=4))
-        nc.gpsimd.tensor_copy(
+        nc.vector.tensor_copy(
             w3_codes[:].rearrange("p (b t m) -> p b t m", b=2, t=4),
             w3_raw[:].rearrange("p (b m t) -> p b t m", b=2, t=4))
         opaque_layer(1)
@@ -355,6 +356,7 @@ def tile_list_deferred_tile_shading_kernel(
         translucent_layer(1)
         for s in range(PAGES - 1):
             if s + 3 < PAGES:
+                expose_pair(s + 1)
                 scatter_opaque(s + 2)
             scatter_translucent(s + 1)
             if s == 0:
@@ -369,40 +371,37 @@ def tile_list_deferred_tile_shading_kernel(
                     if ahead + 1 < PAGES:
                         opaque_layer(ahead + 1)
                     translucent_layer(ahead)
-            for half in range(2):
-                apply_mix(s, nc.gpsimd, slice(half * S, (half + 1) * S))
+            apply_mix(s, nc.gpsimd, slice(0, T2))
             load_mix(s + 1)
             if s + 3 == PAGES:
                 scatter_opaque(s + 2)
             if s == 3:
-                first_woven = [weave_rows(first) for first in range(0, CHUNKS, 2)]
+                first_woven = [weave(0, first, 2, False) for first in range(0, CHUNKS, 2)]
                 quantise_z(0, 0, 2, first_woven[0])
-            if s == 5:
-                nc.scalar.copy(
-                    pairs[:, 0 : 2 * T2].rearrange("p (m i t) -> p m t i", i=4, t=2),
-                    z_rows[1][:, 0 : 2 * T2].rearrange("p (t m i) -> p m t i", t=2, i=4))
-            if s == 6:
-                for half in range(2):
-                    nc.scalar.copy(
-                        pairs[:, 2 * (T2 + half * S) : 2 * (T2 + (half + 1) * S)].rearrange("p (m t) -> p m t", t=2),
-                        z_row(s)[:, half * S : (half + 1) * S].unsqueeze(2).to_broadcast([P, S, 2]))
 
         accs = {}
         for c in range(CHUNKS):
             for half in range(2):
                 accs.setdefault((c, half), bank())
                 shade(accs[c, half], 0, c, half)
-        WEAVE_ON_VECTOR = (3,)
-        COPY_ON_VECTOR = (3, 5, 7)
-        order = list(range(CHUNKS))
+        WEAVE_ON_VECTOR = (2, 3)
+        COPY_ON_VECTOR = (7,)
+        woven = {}
+        for c in range(CHUNKS):
+            if c not in WEAVE_ON_VECTOR:
+                apply_mix(PAGES - 1, nc.vector, slice(c * BANK, (c + 1) * BANK))
+                woven.setdefault(c, weave(1, c, 1, False))
+        order = list(WEAVE_ON_VECTOR) + list(woven)
         for c in order:
-            apply_mix(PAGES - 1, nc.vector, slice(c * BANK, (c + 1) * BANK))
-            quantise_z(1, c, 1, weave_pairs(c, c in WEAVE_ON_VECTOR))
+            if c in WEAVE_ON_VECTOR:
+                apply_mix(PAGES - 1, nc.vector, slice(c * BANK, (c + 1) * BANK))
+                woven.setdefault(c, weave(1, c, 1, True))
+            quantise_z(1, c, 1, woven[c])
             for half in range(2):
                 shade(accs[c, half], 1, c, half)
         for k, c in enumerate(order):
             for half in range(2):
-                result = new_tile([P, BANK], F32, "result%d_%d" % (c, half), "result", 6)
+                result = new_tile([P, BANK], F32, "result%d_%d" % (c, half), "result", 8)
                 if 2 * k + half in COPY_ON_VECTOR:
                     nc.vector.tensor_copy(result[:], accs[c, half][:])
                 else:

@@ -18,27 +18,25 @@ P = 128
 BANK = 512
 FLOPS = 2 * (3 * K * H * S + H * N * T2)
 PAGES = H // P
-PAGE_SLOTS = 3
 CHUNKS = T2 // BANK
 KIB = 1024
 HALF = KIB // 2
-W3_CODES_AT = 0
-W3_PLANE_AT = 4 * KIB
-FIRST_SQUARED_AT = KIB
-TAB2_PLANE_AT = 5 * KIB
-TAB2_WORDS_AT = TAB2_PLANE_AT + 4 * KIB
-PAGE_AT = (TAB2_WORDS_AT - HALF, TAB2_WORDS_AT + 16 * KIB + HALF, TAB2_WORDS_AT + 8 * KIB - HALF)
-W3_SCALES_AT = PAGE_AT[1] - HALF
-W3_WORDS_AT = W3_SCALES_AT + KIB
-W2_ROUNDED_AT = W3_WORDS_AT + 4 * KIB
-W2_PLANE_AT = PAGE_AT[1] + 12 * KIB
-MIX_AT = (W2_PLANE_AT + 3 * HALF, W2_PLANE_AT + 19 * HALF, W2_PLANE_AT + 35 * HALF)
-FIRST_PLANES_AT = (MIX_AT[2] + 8 * KIB, MIX_AT[0] - KIB)
-LATE_PLANE_AT = MIX_AT[2] + 9 * KIB
-WOVEN_AT = LATE_PLANE_AT + KIB
-TAB1_PLANE_AT = WOVEN_AT + 16 * KIB
-Z_AT = (TAB1_PLANE_AT + 5 * KIB, TAB1_PLANE_AT + 21 * KIB)
-SOURCES_SHIFT = {1: 3 * HALF, 4: HALF, 5: -HALF}
+
+PAGE_AT = (0, 24 * KIB, 32 * KIB)
+Z_CODES_AT = 8 * KIB
+TAB2_WORDS_AT = Z_CODES_AT + HALF
+W2_ROUNDED_AT = PAGE_AT[1] + HALF
+Z_AT = (40 * KIB, 56 * KIB)
+WOVEN_AT = (72 * KIB, 88 * KIB)
+MIX_AT = (104 * KIB, 112 * KIB, 120 * KIB)
+TAB2_PLANE_AT = 128 * KIB
+W2_CODES_AT = TAB2_PLANE_AT + 2 * KIB
+W3_WORDS_AT = TAB2_PLANE_AT + 4 * KIB
+W3_SCALES_AT = W3_WORDS_AT + 4 * KIB
+FIRST_OPAQUE_AT = W3_SCALES_AT + KIB
+FIRST_SQUARED_AT = (W2_ROUNDED_AT + 3 * KIB, FIRST_OPAQUE_AT)
+FIRST_TRANSLUCENT_AT = FIRST_OPAQUE_AT + 4 * KIB
+LAST_SOURCES_AT = MIX_AT[PAGES % 3] + 4 * KIB
 
 
 def tile_list_deferred_tile_shading_kernel(
@@ -58,13 +56,12 @@ def tile_list_deferred_tile_shading_kernel(
         def placed_tile(shape, dtype, name, offset):
             return shared.tile(shape, dtype, name=name, tag=name, bufs=1, align_bytes=64, offset=offset)
 
-        bank_count = [0]
+        banks_used = []
 
-        def bank(back=0):
-            i = bank_count[0]
-            bank_count.append(i + 1)
-            bank_count.remove(i)
-            return ps.tile([P, BANK], F32, name="bank%d" % i, tag="bank%d" % ((i - back) % 8))
+        def bank():
+            i = len(banks_used)
+            banks_used.append(i)
+            return ps.tile([P, BANK], F32, name="bank%d" % i, tag="bank%d" % (i % 8))
 
         def load_list(src, name):
             dst = lists.tile([P, S // 16], U16, name=name)
@@ -77,137 +74,91 @@ def tile_list_deferred_tile_shading_kernel(
                 queue.dma_start(plane[32 * q : 32 * q + 4, :].bitcast(I32), src[0, 4 * q : 4 * q + 4, :].bitcast(I32))
             return plane
 
-        def load_scale_rows_bare(src, rows):
-            for q in range(4):
-                nc.sync.dma_start(rows[32 * q : 32 * q + 4, :].bitcast(I32), src[0, 4 * q : 4 * q + 4, :].bitcast(I32))
-            return rows
-
-        def fill_plane(rows, plane):
-            nc.vector.memset(plane[:].bitcast(I32), 0)
-            for q in range(4):
-                live = slice(32 * q, 32 * q + 4)
-                nc.vector.tensor_copy(plane[live, :].bitcast(I32), rows[live, :].bitcast(I32))
-            return plane
-
         wg_pairs = [new_tile([P, 2, S], F32, "wg_pair%d" % k) for k in range(4)]
 
         def exposure(stream, t):
             return wg_pairs[(t + stream - 1) % 4][:, stream]
 
-        def load_wg(stream, t):
+        def load_wg(stream, t, quadrants=range(4)):
             src = (wg1, wg2)[stream].rearrange("(p t) j -> t p j", t=4)[t]
-            for q in range(4):
+            for q in quadrants:
                 nc.sync.dma_start(exposure(stream, t)[32 * q : 32 * q + 32, :], src)
 
         idx1 = load_list(offs, "idx1")
-        tab1_rows = load_scale_rows_bare(tab_scales, placed_tile([P, T], U8, "tab1_rows", WOVEN_AT))
-        w1_raw = new_tile([P, 2 * H], U8, "w1_raw")
+        w1_rows = placed_tile([P, H], U8, "w1_rows", Z_AT[1] + 7 * KIB)
+        for q in range(4):
+            nc.sync.dma_start(w1_rows[32 * q : 32 * q + 4, :].bitcast(I32), w1_scales[0, 4 * q : 4 * q + 4, :].bitcast(I32))
+        w1_raw = placed_tile([P, 2 * H], U8, "w1_raw", Z_AT[1] + 4 * KIB)
         nc.sync.dma_start(w1_raw[:].bitcast(I32), w1_words[0].bitcast(I32))
-        tab1_w = placed_tile([P, T], I32, "tab1_w", Z_AT[0])
-        tab1_src = tab_words[0].rearrange("p n i -> p (n i)").bitcast(I32)
-        for h in range(2):
-            nc.sync.dma_start(tab1_w[:, h * T // 2 : (h + 1) * T // 2], tab1_src[:, h * T // 2 : (h + 1) * T // 2])
-        w1_rows = load_scale_rows_bare(w1_scales, new_tile([P, H], U8, "w1_rows"))
-        idx2 = load_list(offs2, "idx2")
+        tab1_w = placed_tile([P, T], I32, "tab1_w", WOVEN_AT[1])
+        nc.sync.dma_start(tab1_w[:], tab_words[0].rearrange("p n i -> p (n i)").bitcast(I32))
         idx3 = load_list(offs3, "idx3")
+        load_wg(0, 0, range(1))
+        tab1_s = load_scale_rows(nc.vector, nc.sync, tab_scales, placed_tile([P, T], U8, "tab1_s", Z_AT[1]))
+        w1_sraw = placed_tile([P, H], U8, "w1_sraw", Z_AT[1] + 6 * KIB)
+        nc.vector.memset(w1_sraw[:].bitcast(I32), 0)
+        for q in range(4):
+            live = slice(32 * q, 32 * q + 4)
+            nc.vector.tensor_copy(w1_sraw[live, :].bitcast(I32), w1_rows[live, :].bitcast(I32))
+        load_wg(0, 0, range(1, 4))
+        idx2 = load_list(offs2, "idx2")
+        tab2_s = load_scale_rows(nc.gpsimd, nc.sync, tab2_scales, placed_tile([P, T], U8, "tab2_s", TAB2_PLANE_AT))
         tab2_w = placed_tile([P, T], I32, "tab2_w", TAB2_WORDS_AT)
         nc.sync.dma_start(tab2_w[:], tab2_words[0].rearrange("p n i -> p (n i)").bitcast(I32))
-        load_wg(0, 0)
-        tab2_s = load_scale_rows(nc.gpsimd, nc.gpsimd, tab2_scales, placed_tile([P, T], U8, "tab2_s", TAB2_PLANE_AT))
-        w3_sraw = load_scale_rows(nc.gpsimd, nc.gpsimd, w3_scales, placed_tile([P, H], U8, "w3_sraw", W3_SCALES_AT))
-        tab1_s = fill_plane(tab1_rows, placed_tile([P, T], U8, "tab1_s", TAB1_PLANE_AT))
-        load_wg(0, 1)
-
-        w2_raw = []
-
-        def load_w2(b):
-            raw = placed_tile([P, 4, BANK], F32, "w2_raw%d" % b, Z_AT[1] + 8 * KIB * b)
-            nc.sync.dma_start(raw[:], w2[:, b * BANK : (b + 1) * BANK].rearrange("(p i) c -> p i c", i=4))
-            w2_raw.append(raw)
-
-        load_w2(0)
+        w3_sraw = load_scale_rows(nc.gpsimd, nc.sync, w3_scales, placed_tile([P, H], U8, "w3_sraw", W3_SCALES_AT))
         w3_raw = placed_tile([P, H], I32, "w3_raw", W3_WORDS_AT)
         nc.sync.dma_start(w3_raw[:], w3_words[0].rearrange("p n i -> p (n i)").bitcast(I32))
-        idx4 = load_list(offs4, "idx4")
-        load_wg(1, 0)
-        load_wg(0, 2)
-        load_w2(1)
-        load_wg(1, 1)
-        load_wg(0, 3)
-        w4_raw = placed_tile([P, 2, 4, N], F32, "w4_raw", WOVEN_AT + 8 * KIB)
-        nc.sync.dma_start(w4_raw[:].rearrange("p b t n -> p b (t n)"), w4.rearrange("(b p t) n -> p b (t n)", b=2, t=4))
 
-        w1_codes = new_tile([P, 2 * H], U8, "w1_codes")
-        w1_plane = new_tile([P, H], U8, "w1_plane")
-        nc.vector.tensor_copy(
-            w1_codes[:].bitcast(U16).rearrange("p (b t m) -> p b t m", b=2, t=4),
-            w1_raw[:].bitcast(U16).rearrange("p (b m t) -> p b t m", b=2, t=4))
+        def load_w2(b):
+            raw = placed_tile([P, 4, BANK], F32, "w2_raw%d" % b, WOVEN_AT[0] + 8 * KIB * b)
+            nc.sync.dma_start(raw[:], w2[:, b * BANK : (b + 1) * BANK].rearrange("(p i) c -> p i c", i=4))
+            return raw
 
-        halves = [idx1[:, h * BANK // 16 : (h + 1) * BANK // 16] for h in range(2)]
-        v1_plane = [new_tile([P, BANK], U8, "v1_plane%d" % h) for h in range(2)]
-        v1_codes = [new_tile([P, BANK], U32, "v1_codes%d" % h) for h in range(2)]
-        for h in range(2):
-            nc.vector.tensor_copy(v1_plane[h][:], tab1_s[:].indirect(halves[h]))
-        for h in range(2):
-            nc.vector.tensor_copy(v1_codes[h][:], tab1_w[:].bitcast(U32).indirect(halves[h]))
-        w1_sraw = fill_plane(w1_rows, placed_tile([P, H], U8, "w1_sraw", TAB1_PLANE_AT + KIB // 2))
-        nc.vector.tensor_copy(
-            w1_plane[:].rearrange("p (b t m) -> p b t m", b=2, t=4),
-            w1_sraw[:].rearrange("p (b m t) -> p b t m", b=2, t=4))
-        v2_codes = placed_tile([P, S], U32, "v2_codes", TAB1_PLANE_AT + KIB)
-        v2_plane = placed_tile([P, S], U8, "v2_plane", TAB1_PLANE_AT)
-        nc.vector.tensor_copy(v2_plane[:], tab2_s[:].indirect(idx2[:]))
-        nc.vector.tensor_copy(v2_codes[:], tab2_w[:].bitcast(U32).indirect(idx2[:]))
-
-        w2_codes, w2_plane = [], []
-
-        def round_w2(b, rounded):
-            nc.scalar.copy(
-                rounded.rearrange("p (t m i) -> p m i t", t=4, i=4),
-                w2_raw[b][:].rearrange("p i (m t) -> p m i t", t=4))
-
-        def quantise_first_w2():
-            rounded = placed_tile([P, 4 * BANK], BF16, "w2_rounded", W2_ROUNDED_AT)
-            round_w2(0, rounded[:])
-            codes = new_tile([P, BANK], U32, "w2_codes0")
-            plane = placed_tile([P, BANK], U8, "w2_plane0", W2_PLANE_AT)
-            nc.vector.quantize_mx(out=codes[:].bitcast(FP8X4), scales=plane[:], in_=rounded[:])
-            w2_codes.append(codes[:])
-            w2_plane.append(plane[:])
-
-        def quantise_late_weights():
-            rounded = placed_tile([P, 8 * BANK], BF16, "late_rounded", WOVEN_AT)
-            round_w2(1, rounded[:, 0 : 4 * BANK])
-            for b in range(2):
-                cols = slice(4 * (BANK + b * N), 4 * (BANK + (b + 1) * N))
-                nc.scalar.copy(
-                    rounded[:, cols].rearrange("p (n i t) -> p n t i", i=4, t=4),
-                    w4_raw[:, b].rearrange("p t (n i) -> p n t i", i=4))
-            codes = new_tile([P, 2 * BANK], U32, "late_codes")
-            plane = placed_tile([P, 2 * BANK], U8, "late_plane", LATE_PLANE_AT)
-            nc.vector.quantize_mx(out=codes[:].bitcast(FP8X4), scales=plane[:], in_=rounded[:])
-            w2_codes.append(codes[:, 0:BANK])
-            w2_plane.append(plane[:, 0:BANK])
-            return codes[:, BANK:], plane[:, BANK:]
-
-        pages = {}
         mix_tiles = {}
-        opaque_values = {}
-        translucent_values = {}
 
         def load_mix(s):
             b, t = divmod(s, 4)
-            rows = placed_tile([P, T2], F32, "mix%d" % s, WOVEN_AT + 8 * KIB if s == PAGES - 1 else MIX_AT[s % 3])
+            rows = placed_tile([P, T2], F32, "mix%d" % s, MIX_AT[s % 3])
             nc.sync.dma_start(rows[:], mix[b * K : (b + 1) * K, :].rearrange("(p t) m -> t p m", t=4)[t])
             mix_tiles.setdefault(s, rows)
 
-        z_rows = {}
+        w2_raw = [load_w2(0)]
+        load_wg(0, 1)
+        w2_raw.append(load_w2(1))
+        load_wg(1, 0)
+        idx4 = load_list(offs4, "idx4")
+        load_wg(0, 2)
+        load_wg(1, 1)
+        load_mix(0)
+        load_wg(0, 3)
+        load_wg(1, 2)
+        load_mix(1)
+        load_wg(1, 3)
+        w4_raw = placed_tile([P, 2, 4, N], F32, "w4_raw", WOVEN_AT[1])
+        nc.sync.dma_start(w4_raw[:].rearrange("p b t n -> p b (t n)"), w4.rearrange("(b p t) n -> p b (t n)", b=2, t=4))
 
-        def z_row(s):
-            b, t = divmod(s, 4)
-            if b not in z_rows:
-                z_rows.setdefault(b, placed_tile([P, 4 * T2], BF16, "z_rows%d" % b, Z_AT[b]))
-            return z_rows[b][:, t * T2 : (t + 1) * T2]
+        def deal_columns(name, raw, shape, dtype, view):
+            dealt = new_tile(shape, dtype, name)
+            nc.vector.tensor_copy(
+                dealt[:].bitcast(view).rearrange("p (b t m) -> p b m t", b=2, t=4),
+                raw[:].bitcast(view).rearrange("p (b m t) -> p b m t", b=2, t=4))
+            return dealt
+
+        w1_codes = deal_columns("w1_codes", w1_raw, [P, 2 * H], U8, U16)
+
+        halves1 = [idx1[:, h * BANK // 16 : (h + 1) * BANK // 16] for h in range(2)]
+        halves3 = [idx3[:, h * BANK // 16 : (h + 1) * BANK // 16] for h in range(2)]
+        v1_plane = [new_tile([P, BANK], U8, "v1_plane%d" % h) for h in range(2)]
+        v1_codes = [new_tile([P, BANK], U32, "v1_codes%d" % h) for h in range(2)]
+        w1_plane = deal_columns("w1_plane", w1_sraw, [P, H], U8, U8)
+        for h in range(2):
+            nc.vector.tensor_copy(v1_codes[h][:], tab1_w[:].bitcast(U32).indirect(halves1[h]))
+            nc.vector.tensor_copy(v1_plane[h][:], tab1_s[:].indirect(halves1[h]))
+
+        def product(acc, codes, plane, dtype, moving, moving_plane):
+            nc.tensor.matmul_mx(
+                out=acc[:], lhsT=codes.bitcast(dtype), lhsT_scale=plane,
+                rhs=moving.bitcast(FP8X4), rhs_scale=moving_plane, start=True, stop=True)
 
         activations = {}
 
@@ -216,41 +167,64 @@ def tile_list_deferred_tile_shading_kernel(
                 activations.setdefault(j, new_tile([P, 2, S], F32, "activations%d" % j, "activations", 3))
             return activations[j]
 
-        squares = {}
-        gates = {}
-        colours = {}
+        def rectify(s, h, dst):
+            acc = bank()
+            product(acc, w1_codes[:, 2 * P * s : 2 * P * (s + 1)], w1_plane[:, P * s : P * (s + 1)], FP4X4,
+                    v1_codes[h][:], v1_plane[h][:])
+            nc.scalar.activation(dst, acc[:], ACT.Relu)
 
-        def product(acc, codes, plane, dtype, moving, moving_plane):
-            nc.tensor.matmul_mx(
-                out=acc[:], lhsT=codes.bitcast(dtype), lhsT_scale=plane,
-                rhs=moving.bitcast(FP8X4), rhs_scale=moving_plane, start=True, stop=True)
-
-        def opaque_layer(s):
-            if s == 0:
-                squared = placed_tile([P, S], F32, "squared0", FIRST_SQUARED_AT)[:]
-            else:
-                squared = activation_pair(s - 1)[:, 0]
-            rectified = placed_tile([P, S], F32, "rectified1", W2_ROUNDED_AT)[:] if s == 1 else squared
+        def opaque_layer(s, squared):
             for h in range(2):
-                cols = slice(h * BANK, (h + 1) * BANK)
-                acc = bank()
-                product(acc, w1_codes[:, 2 * P * s : 2 * P * (s + 1)], w1_plane[:, P * s : P * (s + 1)], FP4X4,
-                        v1_codes[h][:], v1_plane[h][:])
-                nc.scalar.activation(rectified[:, cols], acc[:], ACT.Relu)
-                if s == 0:
-                    nc.scalar.activation(squared[:, cols], squared[:, cols], ACT.Square)
-            if s > 0:
-                nc.scalar.activation(squared, rectified, ACT.Square)
-            squares.setdefault(s, squared)
+                rectify(s, h, squared[:, h * BANK : (h + 1) * BANK])
+            nc.scalar.activation(squared, squared, ACT.Square)
+
+        pages = {}
+
+        def new_page(s):
+            pages.setdefault(s, placed_tile([P, T2], F32, "page%d" % s, PAGE_AT[s % 3]))
+            return pages[s]
+
+        new_page(0)
+        for h in range(2):
+            squared = placed_tile([P, BANK], F32, "first_squared%d" % h, FIRST_SQUARED_AT[h])
+            rectify(0, h, squared[:])
+            nc.scalar.activation(squared[:], squared[:], ACT.Square)
+            nc.vector.tensor_tensor(
+                pages[0][:].indirect(halves3[h]), squared[:], exposure(0, 0)[:, h * BANK : (h + 1) * BANK], MULT)
+
+        v2_codes = new_tile([P, S], U32, "v2_codes")
+        nc.vector.tensor_copy(v2_codes[:], tab2_w[:].bitcast(U32).indirect(idx2[:]))
+        w3_plane = deal_columns("w3_plane", w3_sraw, [P, H], U8, U8)
+        w3_codes = deal_columns("w3_codes", w3_raw, [P, H], I32, I32)
+
+        def round_w2(b, rounded):
+            nc.scalar.copy(
+                rounded.rearrange("p (t m i) -> p m i t", t=4, i=4),
+                w2_raw[b][:].rearrange("p i (m t) -> p m i t", t=4))
+
+        opaque_layer(1, activation_pair(0)[:, 0])
+        opaque1 = placed_tile([P, S], F32, "opaque1", FIRST_OPAQUE_AT)
+        nc.gpsimd.tensor_tensor(opaque1[:], activations[0][:, 0], exposure(0, 1), MULT)
+
+        w2_rounded = placed_tile([P, 8 * BANK], BF16, "w2_rounded", W2_ROUNDED_AT)
+        for b in range(2):
+            round_w2(b, w2_rounded[:, 4 * BANK * b : 4 * BANK * (b + 1)])
+        v2_plane = placed_tile([P, S], U8, "v2_plane", WOVEN_AT[0] + 15 * KIB)
+        nc.vector.tensor_copy(v2_plane[:], tab2_s[:].indirect(idx2[:]))
+        w2_codes = placed_tile([P, H], U32, "w2_codes", W2_CODES_AT)
+        w2_plane = placed_tile([P, H], U8, "w2_plane", W3_SCALES_AT)
+        nc.vector.quantize_mx(out=w2_codes[:].bitcast(FP8X4), scales=w2_plane[:], in_=w2_rounded[:])
+        nc.vector.tensor_copy(new_page(1)[:].indirect(idx3[:]), opaque1[:])
+
+        colours = {}
+        z_rows = [placed_tile([P, 4 * T2], BF16, "z_rows%d" % b, Z_AT[b]) for b in range(2)]
+
+        def z_row(s):
+            return z_rows[s // 4][:, s % 4 * T2 : (s % 4 + 1) * T2]
 
         def translucent_layer(s):
-            b, t = divmod(s, 4)
-            if s == 0:
-                gate = placed_tile([P, S], F32, "gate0", WOVEN_AT)[:]
-                colour = placed_tile([P, S], F32, "colour0", MIX_AT[2] + 3 * KIB)[:]
-            else:
-                gate = activation_pair(s)[:, 1]
-                colour = z_row(s - 1).bitcast(F32)
+            gate = activation_pair(s)[:, 1]
+            colour = z_row(s - 1).bitcast(F32) if s > 0 else placed_tile([P, S], F32, "colour0", MIX_AT[2])[:]
             for h in range(2):
                 cols = slice(h * BANK, (h + 1) * BANK)
                 acc = bank()
@@ -259,151 +233,108 @@ def tile_list_deferred_tile_shading_kernel(
                 nc.scalar.activation(gate[:, cols], acc[:], ACT.Sigmoid)
             for h in range(2):
                 cols = slice(h * BANK, (h + 1) * BANK)
-                acc = bank(2 if s == 0 else 0)
-                product(acc, w2_codes[b][:, P * t : P * (t + 1)], w2_plane[b][:, P * t : P * (t + 1)], FP8X4,
+                acc = bank()
+                product(acc, w2_codes[:, P * s : P * (s + 1)], w2_plane[:, P * s : P * (s + 1)], FP8X4,
                         v2_codes[:, cols], v2_plane[:, cols])
                 nc.scalar.copy(colour[:, cols], acc[:])
-            gates.setdefault(s, gate)
             colours.setdefault(s, colour)
 
-        def expose_opaque(s):
-            vals = placed_tile([P, S], F32, "opaque%d" % s, W2_PLANE_AT if s == 0 else MIX_AT[s % 3])
-            width = BANK if s == 0 else S
-            for start in range(0, S, width):
-                cols = slice(start, start + width)
-                nc.gpsimd.tensor_tensor(vals[:, cols], squares[s][:, cols], exposure(0, s % 4)[:, cols], MULT)
-            opaque_values.setdefault(s, vals[:])
+        def expose(j):
+            at = MIX_AT[(j + 1) % 3]
+            if j in (0, PAGES - 1):
+                vals = placed_tile([P, S], F32, "sources%d" % j, FIRST_TRANSLUCENT_AT if j == 0 else LAST_SOURCES_AT)
+                nc.gpsimd.tensor_tensor(vals[:], activations[j][:, 1], exposure(1, j % 4), MULT)
+                opaque, translucent = None, vals[:]
+            else:
+                vals = placed_tile([P, 2, S], F32, "sources%d" % j, at)
+                nc.gpsimd.tensor_tensor(vals[:], activations[j][:], wg_pairs[j % 4][:], MULT)
+                opaque, translucent = vals[:, 0], vals[:, 1]
+            nc.gpsimd.tensor_tensor(translucent, translucent, colours[j], MULT)
+            return opaque, translucent
 
-        def expose_gate(s):
-            at = PAGE_AT[1] + 8 * KIB if s == 0 else MIX_AT[(s + 1) % 3] + 4 * KIB
-            vals = placed_tile([P, S], F32, "translucent%d" % s, at)
-            nc.gpsimd.tensor_tensor(vals[:], gates[s], exposure(1, s % 4), MULT)
-            translucent_values.setdefault(s, vals[:])
+        def scatter(j, sources):
+            opaque, translucent = sources
+            if opaque is not None:
+                nc.vector.tensor_copy(new_page(j + 1)[:].indirect(idx3[:]), opaque)
+            nc.vector.tensor_copy(pages[j][:].indirect(idx4[:]), translucent)
 
-        def expose_pair(j):
-            vals = placed_tile([P, 2, S], F32, "sources%d" % j, MIX_AT[(j + 1) % 3] + SOURCES_SHIFT.get(j, 0))
-            nc.gpsimd.tensor_tensor(vals[:], activations[j][:], wg_pairs[j % 4][:], MULT)
-            opaque_values.setdefault(j + 1, vals[:, 0])
-            translucent_values.setdefault(j, vals[:, 1])
+        def layers(j):
+            if j + 1 < PAGES:
+                opaque_layer(j + 1, activation_pair(j)[:, 0])
+            translucent_layer(j)
 
-        def scatter_opaque(s):
-            if s not in opaque_values:
-                expose_opaque(s)
-            page = placed_tile([P, T2], F32, "page_%d" % s, {3: WOVEN_AT, 6: WOVEN_AT, 7: MIX_AT[1] + 4 * KIB}.get(s, PAGE_AT[s % PAGE_SLOTS]))
-            pages.setdefault(s, page)
-            nc.vector.tensor_copy(page[:].indirect(idx3[:]), opaque_values[s])
-
-        def scatter_translucent(s):
-            if s not in translucent_values:
-                expose_gate(s)
-            vals = translucent_values[s]
-            nc.gpsimd.tensor_tensor(vals, vals, colours[s], MULT)
-            nc.vector.tensor_copy(pages[s][:].indirect(idx4[:]), vals)
-
-        z_codes = {}
+        def round_w4():
+            rounded = placed_tile([P, 2, 4 * N], BF16, "w4_rounded", FIRST_TRANSLUCENT_AT)
+            for b in range(2):
+                nc.scalar.copy(
+                    rounded[:, b].rearrange("p (n i t) -> p n t i", i=4, t=4),
+                    w4_raw[:, b].rearrange("p t (n i) -> p n t i", i=4))
+            return rounded
 
         def apply_mix(s, engine, cols):
             engine.tensor_tensor(z_row(s)[:, cols], pages[s][:, cols], mix_tiles[s][:, cols], MULT)
 
-        def weave(b, first, count, on_vector):
-            woven = placed_tile([P, count, 4 * BANK], BF16, "woven%d_%d" % (b, first), (WOVEN_AT, PAGE_AT[0])[b] + first * 4 * KIB)
-            for c in range(count):
-                dst = woven[:, c].rearrange("p (m i t) -> p m t i", i=4, t=4)
-                src = z_rows[b][:].rearrange("p (t c m i) -> p c m t i", t=4, c=CHUNKS, i=4)[:, first + c]
-                if on_vector:
-                    nc.vector.tensor_copy(dst, src)
-                else:
-                    nc.scalar.copy(dst, src)
-            return woven
-
-        def quantise_z(b, first, count, woven):
-            codes = new_tile([P, count * BANK], U32, "z_codes%d_%d" % (b, first))
-            if b == 0:
-                plane = placed_tile([P, count * BANK], U8, "z_plane0_%d" % first, FIRST_PLANES_AT[first // 2])
-            else:
-                plane = new_tile([P, count * BANK], U8, "z_plane1_%d" % first)
-            nc.vector.quantize_mx(out=codes[:].bitcast(FP8X4), scales=plane[:], in_=woven[:].rearrange("p c x -> p (c x)"))
-            for c in range(count):
-                cols = slice(c * BANK, (c + 1) * BANK)
-                z_codes.setdefault((b, first + c), (codes[:, cols], plane[:, cols]))
-
-        def shade(acc, b, c, half):
-            codes, plane = z_codes[b, c]
-            cols = slice(b * N + half * P, b * N + (half + 1) * P)
-            nc.tensor.matmul_mx(
-                out=acc[:], lhsT=w4_codes[:, cols].bitcast(FP8X4), lhsT_scale=w4_plane[:, cols],
-                rhs=codes.bitcast(FP8X4), rhs_scale=plane, start=(b == 0), stop=(b == 1))
-
-        opaque_layer(0)
-        scatter_opaque(0)
-        w3_codes = placed_tile([P, H], I32, "w3_codes", W3_CODES_AT)
-        w3_plane = placed_tile([P, H], U8, "w3_plane", W3_PLANE_AT)
-        nc.vector.tensor_copy(
-            w3_plane[:].rearrange("p (b t m) -> p b t m", b=2, t=4),
-            w3_sraw[:].rearrange("p (b m t) -> p b t m", b=2, t=4))
-        nc.vector.tensor_copy(
-            w3_codes[:].rearrange("p (b t m) -> p b t m", b=2, t=4),
-            w3_raw[:].rearrange("p (b m t) -> p b t m", b=2, t=4))
-        opaque_layer(1)
-        quantise_first_w2()
-        scatter_opaque(1)
-        load_mix(0)
-        load_wg(1, 2)
-        load_wg(1, 3)
-        translucent_layer(0)
-        scatter_translucent(0)
-        opaque_layer(2)
-        translucent_layer(1)
-        for s in range(PAGES - 1):
-            if s + 3 < PAGES:
-                expose_pair(s + 1)
-                scatter_opaque(s + 2)
-            scatter_translucent(s + 1)
-            if s == 0:
-                w4_codes, w4_plane = quantise_late_weights()
-            if s == 4:
-                quantise_z(0, 2, 2, first_woven[1])
-            if s < 3:
-                opaque_layer(s + 3)
-                translucent_layer(s + 2)
-            if s == 3:
-                for ahead in range(s + 2, PAGES):
-                    if ahead + 1 < PAGES:
-                        opaque_layer(ahead + 1)
-                    translucent_layer(ahead)
-            apply_mix(s, nc.gpsimd, slice(0, T2))
-            load_mix(s + 1)
-            if s + 3 == PAGES:
-                scatter_opaque(s + 2)
-            if s == 3:
-                first_woven = [weave(0, first, 2, False) for first in range(0, CHUNKS, 2)]
-                quantise_z(0, 0, 2, first_woven[0])
-
-        accs = {}
-        for c in range(CHUNKS):
-            for half in range(2):
-                accs.setdefault((c, half), bank())
-                shade(accs[c, half], 0, c, half)
-        WEAVE_ON_VECTOR = (2, 3)
-        COPY_ON_VECTOR = (7,)
         woven = {}
+
+        def weave(b, c, on_vector):
+            tile = placed_tile([P, 4 * BANK], BF16, "woven%d_%d" % (b, c), WOVEN_AT[b] + c * 4 * KIB)
+            dst = tile[:].rearrange("p (m i t) -> p m t i", i=4, t=4)
+            src = z_rows[b][:].rearrange("p (t c m i) -> p c m t i", t=4, c=CHUNKS, i=4)[:, c]
+            if on_vector:
+                nc.vector.tensor_copy(dst, src)
+            else:
+                nc.scalar.copy(dst, src)
+            woven.setdefault((b, c), tile)
+
+        def quantise_z(b, c):
+            codes = placed_tile([P, BANK], U32, "z_codes%d_%d" % (b, c), Z_CODES_AT + (b * CHUNKS + c) * 2 * KIB)
+            if b == 0:
+                plane = placed_tile([P, BANK], U8, "z_plane0_%d" % c, LAST_SOURCES_AT + c * HALF)
+            else:
+                plane = new_tile([P, BANK], U8, "z_plane1_%d" % c)
+            nc.vector.quantize_mx(out=codes[:].bitcast(FP8X4), scales=plane[:], in_=woven[b, c][:])
+            return codes, plane
+
+        translucent_layer(0)
+        scatter(0, expose(0))
+        layers(1)
+        scatter(1, expose(1))
+        layers(2)
+        for s in range(PAGES - 1):
+            apply_mix(s, nc.gpsimd, slice(0, T2))
+            if s + 2 < PAGES:
+                scatter(s + 2, expose(s + 2))
+            if s + 3 < PAGES:
+                layers(s + 3)
+            if 1 <= s and s + 1 < PAGES:
+                load_mix(s + 1)
+            if s == 1:
+                w4_rounded = round_w4()
+            if s == 3:
+                for c in range(CHUNKS):
+                    weave(0, c, False)
+
         for c in range(CHUNKS):
-            if c not in WEAVE_ON_VECTOR:
-                apply_mix(PAGES - 1, nc.vector, slice(c * BANK, (c + 1) * BANK))
-                woven.setdefault(c, weave(1, c, 1, False))
-        order = list(WEAVE_ON_VECTOR) + list(woven)
+            apply_mix(PAGES - 1, nc.vector, slice(c * BANK, (c + 1) * BANK))
+        for c in range(CHUNKS):
+            weave(1, c, c >= 2)
+        w4_codes = new_tile([P, 2 * N], U32, "w4_codes")
+        w4_plane = placed_tile([P, 2 * N], U8, "w4_plane", LAST_SOURCES_AT + CHUNKS * HALF)
+        nc.vector.quantize_mx(out=w4_codes[:].bitcast(FP8X4), scales=w4_plane[:], in_=w4_rounded[:].rearrange("p b x -> p (b x)"))
+        order = (0, 2, 3, 1)
         for c in order:
-            if c in WEAVE_ON_VECTOR:
-                apply_mix(PAGES - 1, nc.vector, slice(c * BANK, (c + 1) * BANK))
-                woven.setdefault(c, weave(1, c, 1, True))
-            quantise_z(1, c, 1, woven[c])
+            accs = [bank() for half in range(2)]
+            for b in range(2):
+                codes, plane = quantise_z(b, c)
+                for half in range(2):
+                    cols = slice(b * N + half * P, b * N + (half + 1) * P)
+                    nc.tensor.matmul_mx(
+                        out=accs[half][:], lhsT=w4_codes[:, cols].bitcast(FP8X4), lhsT_scale=w4_plane[:, cols],
+                        rhs=codes[:].bitcast(FP8X4), rhs_scale=plane[:], start=(b == 0), stop=(b == 1))
             for half in range(2):
-                shade(accs[c, half], 1, c, half)
-        for k, c in enumerate(order):
-            for half in range(2):
-                result = new_tile([P, BANK], F32, "result%d_%d" % (c, half), "result", 8)
-                if 2 * k + half in COPY_ON_VECTOR:
-                    nc.vector.tensor_copy(result[:], accs[c, half][:])
+                result = placed_tile([P, BANK], F32, "result%d_%d" % (c, half), Z_AT[0] + (2 * c + half) * 2 * KIB)
+                if c == order[-1] and half == 1:
+                    nc.vector.tensor_copy(result[:], accs[half][:])
                 else:
-                    nc.scalar.copy(result[:], accs[c, half][:])
+                    nc.scalar.copy(result[:], accs[half][:])
                 nc.sync.dma_start(out[half * P : (half + 1) * P, c * BANK : (c + 1) * BANK], result[:])

@@ -1,6 +1,7 @@
 from contextlib import ExitStack
 
 import concourse.mybir as mybir
+from concourse.masks import make_identity
 
 F32 = mybir.dt.float32
 BF16 = mybir.dt.bfloat16
@@ -18,25 +19,32 @@ P = 128
 BANK = 512
 FLOPS = 2 * (3 * K * H * S + H * N * T2)
 PAGES = H // P
+EARLY = PAGES // 2
 CHUNKS = T2 // BANK
+BLOCKS = BANK // P
 KIB = 1024
 HALF = KIB // 2
+QUADRANTS = (0, 2, 1, 3)
 
 PAGE_AT = (0, 24 * KIB, 32 * KIB)
 Z_CODES_AT = 8 * KIB
 TAB2_WORDS_AT = Z_CODES_AT + HALF
-W2_ROUNDED_AT = PAGE_AT[1] + HALF
-Z_AT = (40 * KIB, 56 * KIB)
+W3_LATE_WORDS_AT = PAGE_AT[1] + HALF
+W2_ROUNDED_AT = PAGE_AT[1] + 4 * KIB
+ROWS_AT = 40 * KIB
+PAIRS_AT = 56 * KIB
 WOVEN_AT = (72 * KIB, 88 * KIB)
+TURNED_AT = WOVEN_AT[1]
 MIX_AT = (104 * KIB, 112 * KIB, 120 * KIB)
 TAB2_PLANE_AT = 128 * KIB
-W2_CODES_AT = TAB2_PLANE_AT + 2 * KIB
-W3_WORDS_AT = TAB2_PLANE_AT + 4 * KIB
-W3_SCALES_AT = W3_WORDS_AT + 4 * KIB
-FIRST_OPAQUE_AT = W3_SCALES_AT + KIB
+FIRST_OPAQUE_AT = TAB2_PLANE_AT + 4 * KIB
 FIRST_SQUARED_AT = (W2_ROUNDED_AT + 3 * KIB, FIRST_OPAQUE_AT)
 FIRST_TRANSLUCENT_AT = FIRST_OPAQUE_AT + 4 * KIB
-LAST_SOURCES_AT = MIX_AT[PAGES % 3] + 4 * KIB
+LATE_ROWS_AT = FIRST_TRANSLUCENT_AT + 4 * KIB
+LAST_SOURCES_AT = LATE_ROWS_AT + 8 * KIB
+LAYER_BANKS = (0, 1, 2, 3, 4, 5)
+TURN_BANKS = (6, 7)
+SUM_BANKS = (0, 1, 2, 3, 4, 5, 6, 7)
 
 
 def tile_list_deferred_tile_shading_kernel(
@@ -56,121 +64,144 @@ def tile_list_deferred_tile_shading_kernel(
         def placed_tile(shape, dtype, name, offset):
             return shared.tile(shape, dtype, name=name, tag=name, bufs=1, align_bytes=64, offset=offset)
 
-        banks_used = []
+        turns_taken = {}
 
-        def bank():
-            i = len(banks_used)
-            banks_used.append(i)
-            return ps.tile([P, BANK], F32, name="bank%d" % i, tag="bank%d" % (i % 8))
+        def bank(ring, dtype=F32):
+            taken = turns_taken.setdefault(ring, [])
+            taken.append(ring[len(taken) % len(ring)])
+            return ps.tile([P, BANK], dtype, name="bank%d_%d" % (len(ring), len(taken)), tag="bank%d" % taken[-1])
 
         def load_list(src, name):
             dst = lists.tile([P, S // 16], U16, name=name)
             nc.sync.dma_start(dst[:], src)
             return dst
 
-        def load_scale_rows(engine, queue, src, plane):
-            engine.memset(plane[:].bitcast(I32), 0)
-            for q in range(4):
-                queue.dma_start(plane[32 * q : 32 * q + 4, :].bitcast(I32), src[0, 4 * q : 4 * q + 4, :].bitcast(I32))
+        def load_scale_rows(src, rows):
+            for q in QUADRANTS:
+                nc.sync.dma_start(rows[32 * q : 32 * q + 4, :].bitcast(I32), src[0, 4 * q : 4 * q + 4, :].bitcast(I32))
+            return rows
+
+        def zeroed(engine, plane):
+            engine.memset(plane.bitcast(I32), 0)
             return plane
 
-        wg_pairs = [new_tile([P, 2, S], F32, "wg_pair%d" % k) for k in range(4)]
+        def words_of(src):
+            return src[0].rearrange("p n i -> p (n i)").bitcast(I32)
 
-        def exposure(stream, t):
-            return wg_pairs[(t + stream - 1) % 4][:, stream]
+        def load(dst, src):
+            nc.sync.dma_start(dst[:], src)
+            return dst
 
-        def load_wg(stream, t, quadrants=range(4)):
-            src = (wg1, wg2)[stream].rearrange("(p t) j -> t p j", t=4)[t]
-            for q in quadrants:
-                nc.sync.dma_start(exposure(stream, t)[32 * q : 32 * q + 32, :], src)
+        def load_dealt(dst, src, t):
+            for q in QUADRANTS:
+                nc.sync.dma_start(dst[32 * q : 32 * q + 32, :], src.rearrange("(p t) j -> t p j", t=4)[t])
 
+        tab1_rows = load_scale_rows(tab_scales, placed_tile([P, T], U8, "tab1_rows", PAIRS_AT)[:])
         idx1 = load_list(offs, "idx1")
-        w1_rows = placed_tile([P, H], U8, "w1_rows", Z_AT[1] + 7 * KIB)
-        for q in range(4):
-            nc.sync.dma_start(w1_rows[32 * q : 32 * q + 4, :].bitcast(I32), w1_scales[0, 4 * q : 4 * q + 4, :].bitcast(I32))
-        w1_raw = placed_tile([P, 2 * H], U8, "w1_raw", Z_AT[1] + 4 * KIB)
-        nc.sync.dma_start(w1_raw[:].bitcast(I32), w1_words[0].bitcast(I32))
-        tab1_w = placed_tile([P, T], I32, "tab1_w", WOVEN_AT[1])
-        nc.sync.dma_start(tab1_w[:], tab_words[0].rearrange("p n i -> p (n i)").bitcast(I32))
-        idx3 = load_list(offs3, "idx3")
-        load_wg(0, 0, range(1))
-        tab1_s = load_scale_rows(nc.vector, nc.sync, tab_scales, placed_tile([P, T], U8, "tab1_s", Z_AT[1]))
-        w1_sraw = placed_tile([P, H], U8, "w1_sraw", Z_AT[1] + 6 * KIB)
-        nc.vector.memset(w1_sraw[:].bitcast(I32), 0)
-        for q in range(4):
+        w1_words_sb = new_tile([P, 2 * H], U8, "w1_words_sb")
+        nc.sync.dma_start(w1_words_sb[:].bitcast(I32), w1_words[0].bitcast(I32))
+        tab1_w = load(placed_tile([P, T], I32, "tab1_w", WOVEN_AT[1]), words_of(tab_words))
+        w1_plane = load_scale_rows(w1_scales, zeroed(nc.vector, new_tile([P, H], U8, "w1_plane")[:]))
+        tab1_s = placed_tile([P, T], U8, "tab1_s", PAIRS_AT + 4 * KIB)
+        zeroed(nc.vector, tab1_s[:])
+        for q in QUADRANTS:
             live = slice(32 * q, 32 * q + 4)
-            nc.vector.tensor_copy(w1_sraw[live, :].bitcast(I32), w1_rows[live, :].bitcast(I32))
-        load_wg(0, 0, range(1, 4))
+            nc.vector.tensor_copy(tab1_s[live, :].bitcast(I32), tab1_rows[live, :].bitcast(I32))
+        idx3 = load_list(offs3, "idx3")
+        first_exposures = new_tile([P, 3, S], F32, "first_exposures")
+        nc.sync.dma_start(first_exposures[:, 1], wg1)
+        w2_raw = [placed_tile([P, 4, BANK], F32, "w2_raw%d" % b, WOVEN_AT[0] + 8 * KIB * b) for b in range(2)]
+        w2_rows = w2.rearrange("(p i) (b c) -> b p i c", i=4, b=2)
+        load(w2_raw[0], w2_rows[0])
         idx2 = load_list(offs2, "idx2")
-        tab2_s = load_scale_rows(nc.gpsimd, nc.sync, tab2_scales, placed_tile([P, T], U8, "tab2_s", TAB2_PLANE_AT))
-        tab2_w = placed_tile([P, T], I32, "tab2_w", TAB2_WORDS_AT)
-        nc.sync.dma_start(tab2_w[:], tab2_words[0].rearrange("p n i -> p (n i)").bitcast(I32))
-        w3_sraw = load_scale_rows(nc.gpsimd, nc.sync, w3_scales, placed_tile([P, H], U8, "w3_sraw", W3_SCALES_AT))
-        w3_raw = placed_tile([P, H], I32, "w3_raw", W3_WORDS_AT)
-        nc.sync.dma_start(w3_raw[:], w3_words[0].rearrange("p n i -> p (n i)").bitcast(I32))
-
-        def load_w2(b):
-            raw = placed_tile([P, 4, BANK], F32, "w2_raw%d" % b, WOVEN_AT[0] + 8 * KIB * b)
-            nc.sync.dma_start(raw[:], w2[:, b * BANK : (b + 1) * BANK].rearrange("(p i) c -> p i c", i=4))
-            return raw
+        tab2_s = placed_tile([P, T], U8, "tab2_s", TAB2_PLANE_AT)
+        load_scale_rows(tab2_scales, zeroed(nc.gpsimd, tab2_s[:]))
+        load(w2_raw[1], w2_rows[1])
+        tab2_w = load(placed_tile([P, T], I32, "tab2_w", TAB2_WORDS_AT), words_of(tab2_words))
+        translucent_planes = new_tile([P, 3 * BANK], U8, "translucent_planes")
+        w3_plane = load_scale_rows(w3_scales, zeroed(nc.gpsimd, translucent_planes[:, 0:H]))
+        w3_late_words = load(placed_tile([P, BANK], I32, "w3_late_words", W3_LATE_WORDS_AT), words_of(w3_words)[:, BANK:])
+        w3_early_codes = load(new_tile([P, BANK], I32, "w3_early_codes"), words_of(w3_words)[:, 0:BANK])
+        nc.sync.dma_start(first_exposures[:, 2], wg2)
+        idx4 = load_list(offs4, "idx4")
 
         mix_tiles = {}
 
         def load_mix(s):
-            b, t = divmod(s, 4)
-            rows = placed_tile([P, T2], F32, "mix%d" % s, MIX_AT[s % 3])
-            nc.sync.dma_start(rows[:], mix[b * K : (b + 1) * K, :].rearrange("(p t) m -> t p m", t=4)[t])
+            src = mix[s * P : (s + 1) * P, :] if s < EARLY else mix[K:, :].rearrange("(p t) m -> t p m", t=4)[s - EARLY]
+            if s + 1 < PAGES:
+                rows = last_pairs if s + 2 == PAGES else placed_tile([P, T2], F32, "mix%d" % s, MIX_AT[s % 3])[:]
+                nc.sync.dma_start(rows, src)
+            else:
+                rows = [
+                    load(placed_tile([P, BANK], F32, "last_mix%d" % c, MIX_AT[0] + c * 2 * KIB), src[:, c * BANK : (c + 1) * BANK])
+                    for c in range(CHUNKS)]
             mix_tiles.setdefault(s, rows)
 
-        w2_raw = [load_w2(0)]
-        load_wg(0, 1)
-        w2_raw.append(load_w2(1))
-        load_wg(1, 0)
-        idx4 = load_list(offs4, "idx4")
-        load_wg(0, 2)
-        load_wg(1, 1)
         load_mix(0)
-        load_wg(0, 3)
-        load_wg(1, 2)
         load_mix(1)
-        load_wg(1, 3)
-        w4_raw = placed_tile([P, 2, 4, N], F32, "w4_raw", WOVEN_AT[1])
+        w4_raw = placed_tile([P, 2, 4, N], F32, "w4_raw", PAIRS_AT + 8 * KIB)
         nc.sync.dma_start(w4_raw[:].rearrange("p b t n -> p b (t n)"), w4.rearrange("(b p t) n -> p b (t n)", b=2, t=4))
+        load_dealt(first_exposures[:, 0], wg1, 0)
+        late_exposures = [new_tile([P, 2, S], F32, "late_exposures%d" % t) for t in range(3)]
+        for t in range(3):
+            load_dealt(late_exposures[t][:, 0], wg1, t + 1)
+            load_dealt(late_exposures[t][:, 1], wg2, t)
+        last_exposure = new_tile([P, S], F32, "last_exposure")
+        load_dealt(last_exposure[:], wg2, 3)
 
-        def deal_columns(name, raw, shape, dtype, view):
-            dealt = new_tile(shape, dtype, name)
-            nc.vector.tensor_copy(
-                dealt[:].bitcast(view).rearrange("p (b t m) -> p b m t", b=2, t=4),
-                raw[:].bitcast(view).rearrange("p (b m t) -> p b m t", b=2, t=4))
-            return dealt
+        def exposure_pair(j):
+            if j >= EARLY:
+                return late_exposures[j - EARLY][:]
+            return first_exposures[:, 1:3] if j + 1 < EARLY else first_exposures[:, 0:3:2]
 
-        w1_codes = deal_columns("w1_codes", w1_raw, [P, 2 * H], U8, U16)
+        identity = {}
+        for dtype, name in ((BF16, "identity_values"), (F32, "identity_words")):
+            identity.setdefault(dtype, new_tile([P, P], dtype, name))
+            make_identity(nc, identity[dtype][:])
+
+        def deal_columns(dealt, raw):
+            nc.vector.tensor_copy(dealt.rearrange("p (t m) -> p m t", t=4), raw.rearrange("p (m t) -> p m t", t=4))
+
+        table_warm_up = new_tile([P, 2], F32, "table_warm_up")
+        nc.vector.memset(table_warm_up[:, 0:1], 0.0)
+        nc.scalar.activation(table_warm_up[:, 1:2], table_warm_up[:, 0:1], ACT.Sigmoid)
 
         halves1 = [idx1[:, h * BANK // 16 : (h + 1) * BANK // 16] for h in range(2)]
         halves3 = [idx3[:, h * BANK // 16 : (h + 1) * BANK // 16] for h in range(2)]
-        v1_plane = [new_tile([P, BANK], U8, "v1_plane%d" % h) for h in range(2)]
+        v1_plane = new_tile([P, S], U8, "v1_plane")
         v1_codes = [new_tile([P, BANK], U32, "v1_codes%d" % h) for h in range(2)]
-        w1_plane = deal_columns("w1_plane", w1_sraw, [P, H], U8, U8)
+        nc.vector.tensor_copy(v1_plane[:], tab1_s[:].indirect(idx1[:]))
         for h in range(2):
             nc.vector.tensor_copy(v1_codes[h][:], tab1_w[:].bitcast(U32).indirect(halves1[h]))
-            nc.vector.tensor_copy(v1_plane[h][:], tab1_s[:].indirect(halves1[h]))
+        w1_late_codes = new_tile([P, H], U8, "w1_late_codes")
+        deal_columns(w1_late_codes[:].bitcast(U16), w1_words_sb[:, H:].bitcast(U16))
+        w1_late_plane = new_tile([P, BANK], U8, "w1_late_plane")
+        deal_columns(w1_late_plane[:], w1_plane[:, BANK:])
 
-        def product(acc, codes, plane, dtype, moving, moving_plane):
+        def page_columns(early, late, s, width):
+            u = s % EARLY
+            return (early if s < EARLY else late)[:, width * u : width * (u + 1)]
+
+        def product(codes, plane, dtype, moving, moving_plane):
+            acc = bank(LAYER_BANKS)
             nc.tensor.matmul_mx(
                 out=acc[:], lhsT=codes.bitcast(dtype), lhsT_scale=plane,
                 rhs=moving.bitcast(FP8X4), rhs_scale=moving_plane, start=True, stop=True)
+            return acc
 
         activations = {}
 
         def activation_pair(j):
+            if j == 1 and j not in activations:
+                activations.setdefault(j, placed_tile([P, 2, S], F32, "activations1", WOVEN_AT[0] + 4 * KIB))
             if j not in activations:
-                activations.setdefault(j, new_tile([P, 2, S], F32, "activations%d" % j, "activations", 3))
+                activations.setdefault(j, new_tile([P, 2, S], F32, "activations%d" % j, "activations", 2))
             return activations[j]
 
         def rectify(s, h, dst):
-            acc = bank()
-            product(acc, w1_codes[:, 2 * P * s : 2 * P * (s + 1)], w1_plane[:, P * s : P * (s + 1)], FP4X4,
-                    v1_codes[h][:], v1_plane[h][:])
+            acc = product(page_columns(w1_words_sb, w1_late_codes, s, 2 * P), page_columns(w1_plane, w1_late_plane, s, P),
+                          FP4X4, v1_codes[h][:], v1_plane[:, h * BANK : (h + 1) * BANK])
             nc.scalar.activation(dst, acc[:], ACT.Relu)
 
         def opaque_layer(s, squared):
@@ -190,66 +221,88 @@ def tile_list_deferred_tile_shading_kernel(
             rectify(0, h, squared[:])
             nc.scalar.activation(squared[:], squared[:], ACT.Square)
             nc.vector.tensor_tensor(
-                pages[0][:].indirect(halves3[h]), squared[:], exposure(0, 0)[:, h * BANK : (h + 1) * BANK], MULT)
+                pages[0][:].indirect(halves3[h]), squared[:], first_exposures[:, 1, h * BANK : (h + 1) * BANK], MULT)
 
-        v2_codes = new_tile([P, S], U32, "v2_codes")
-        nc.vector.tensor_copy(v2_codes[:], tab2_w[:].bitcast(U32).indirect(idx2[:]))
-        w3_plane = deal_columns("w3_plane", w3_sraw, [P, H], U8, U8)
-        w3_codes = deal_columns("w3_codes", w3_raw, [P, H], I32, I32)
-
-        def round_w2(b, rounded):
-            nc.scalar.copy(
-                rounded.rearrange("p (t m i) -> p m i t", t=4, i=4),
-                w2_raw[b][:].rearrange("p i (m t) -> p m i t", t=4))
-
+        v2_plane = new_tile([P, S], U8, "v2_plane")
+        nc.vector.tensor_copy(v2_plane[:], tab2_s[:].indirect(idx2[:]))
         opaque_layer(1, activation_pair(0)[:, 0])
         opaque1 = placed_tile([P, S], F32, "opaque1", FIRST_OPAQUE_AT)
-        nc.gpsimd.tensor_tensor(opaque1[:], activations[0][:, 0], exposure(0, 1), MULT)
+        nc.gpsimd.tensor_tensor(opaque1[:], activations[0][:, 0], first_exposures[:, 1], MULT)
+
+        def round_rows(rounded, raw):
+            nc.scalar.copy(
+                rounded.rearrange("p (n i t) -> p n t i", i=4, t=4), raw.rearrange("p t (n i) -> p n t i", i=4))
 
         w2_rounded = placed_tile([P, 8 * BANK], BF16, "w2_rounded", W2_ROUNDED_AT)
-        for b in range(2):
-            round_w2(b, w2_rounded[:, 4 * BANK * b : 4 * BANK * (b + 1)])
-        v2_plane = placed_tile([P, S], U8, "v2_plane", WOVEN_AT[0] + 15 * KIB)
-        nc.vector.tensor_copy(v2_plane[:], tab2_s[:].indirect(idx2[:]))
-        w2_codes = placed_tile([P, H], U32, "w2_codes", W2_CODES_AT)
-        w2_plane = placed_tile([P, H], U8, "w2_plane", W3_SCALES_AT)
-        nc.vector.quantize_mx(out=w2_codes[:].bitcast(FP8X4), scales=w2_plane[:], in_=w2_rounded[:])
+        round_rows(w2_rounded[:, 0 : 4 * BANK], w2_raw[0][:])
+        nc.scalar.copy(
+            w2_rounded[:, 4 * BANK :].rearrange("p (t m i) -> p m i t", t=4, i=4),
+            w2_raw[1][:].rearrange("p i (m t) -> p m i t", t=4))
+        v2_codes = placed_tile([P, S], U32, "v2_codes", WOVEN_AT[0] + 12 * KIB)
+        nc.vector.tensor_copy(v2_codes[:], tab2_w[:].bitcast(U32).indirect(idx2[:]))
+        w3_late_plane = new_tile([P, BANK], U8, "w3_late_plane")
+        deal_columns(w3_late_plane[:], w3_plane[:, BANK:])
+        w3_late_codes = new_tile([P, BANK], I32, "w3_late_codes")
+        deal_columns(w3_late_codes[:], w3_late_words[:])
+        w2_codes = placed_tile([P, H], U32, "w2_codes", TAB2_PLANE_AT)
+        w2_plane = translucent_planes[:, BANK:]
+        nc.vector.quantize_mx(out=w2_codes[:].bitcast(FP8X4), scales=w2_plane, in_=w2_rounded[:])
         nc.vector.tensor_copy(new_page(1)[:].indirect(idx3[:]), opaque1[:])
 
+        late_rows = placed_tile([P, 2 * T2], BF16, "late_rows", LATE_ROWS_AT)
+        pairs = placed_tile([P, 2, T2, 2], BF16, "pairs", PAIRS_AT)
+        last_pairs = pairs[:, 1].rearrange("p m e -> p (m e)").bitcast(F32)
         colours = {}
-        z_rows = [placed_tile([P, 4 * T2], BF16, "z_rows%d" % b, Z_AT[b]) for b in range(2)]
 
         def z_row(s):
-            return z_rows[s // 4][:, s % 4 * T2 : (s % 4 + 1) * T2]
+            if s < EARLY:
+                return placed_tile([P, T2], BF16, "z%d" % s, ROWS_AT + 4 * KIB * s)[:]
+            if s < EARLY + 2:
+                return late_rows[:, (s - EARLY) * T2 : (s - EARLY + 1) * T2]
+            return pairs[:, 1, :, s - EARLY - 2]
+
+        def colour_halves(s):
+            if s == PAGES - 1:
+                return [z_row(s - 2).bitcast(F32)[:, 0:BANK], last_pairs[:, 0:BANK]]
+            if s == EARLY + 1:
+                whole = z_row(s - 1).bitcast(F32)
+            else:
+                at = {0: MIX_AT[2], PAGES - 2: LAST_SOURCES_AT}.get(s, ROWS_AT + 4 * KIB * (s - 1))
+                whole = placed_tile([P, S], F32, "colour%d" % s, at)[:]
+            colours.setdefault(s, whole)
+            return [whole[:, h * BANK : (h + 1) * BANK] for h in range(2)]
 
         def translucent_layer(s):
             gate = activation_pair(s)[:, 1]
-            colour = z_row(s - 1).bitcast(F32) if s > 0 else placed_tile([P, S], F32, "colour0", MIX_AT[2])[:]
+            colour = colour_halves(s)
             for h in range(2):
                 cols = slice(h * BANK, (h + 1) * BANK)
-                acc = bank()
-                product(acc, w3_codes[:, P * s : P * (s + 1)], w3_plane[:, P * s : P * (s + 1)], FP8X4,
-                        v2_codes[:, cols], v2_plane[:, cols])
+                acc = product(page_columns(w3_early_codes, w3_late_codes, s, P), page_columns(w3_plane, w3_late_plane, s, P),
+                              FP8X4, v2_codes[:, cols], v2_plane[:, cols])
                 nc.scalar.activation(gate[:, cols], acc[:], ACT.Sigmoid)
             for h in range(2):
                 cols = slice(h * BANK, (h + 1) * BANK)
-                acc = bank()
-                product(acc, w2_codes[:, P * s : P * (s + 1)], w2_plane[:, P * s : P * (s + 1)], FP8X4,
-                        v2_codes[:, cols], v2_plane[:, cols])
-                nc.scalar.copy(colour[:, cols], acc[:])
+                acc = product(w2_codes[:, P * s : P * (s + 1)], w2_plane[:, P * s : P * (s + 1)], FP8X4,
+                              v2_codes[:, cols], v2_plane[:, cols])
+                nc.scalar.copy(colour[h], acc[:])
             colours.setdefault(s, colour)
 
         def expose(j):
-            at = MIX_AT[(j + 1) % 3]
             if j in (0, PAGES - 1):
                 vals = placed_tile([P, S], F32, "sources%d" % j, FIRST_TRANSLUCENT_AT if j == 0 else LAST_SOURCES_AT)
-                nc.gpsimd.tensor_tensor(vals[:], activations[j][:, 1], exposure(1, j % 4), MULT)
+                nc.gpsimd.tensor_tensor(
+                    vals[:], activations[j][:, 1], first_exposures[:, 2] if j == 0 else last_exposure[:], MULT)
                 opaque, translucent = None, vals[:]
             else:
-                vals = placed_tile([P, 2, S], F32, "sources%d" % j, at)
-                nc.gpsimd.tensor_tensor(vals[:], activations[j][:], wg_pairs[j % 4][:], MULT)
+                vals = placed_tile([P, 2, S], F32, "sources%d" % j, MIX_AT[(j + 1) % 3])
+                nc.gpsimd.tensor_tensor(vals[:], activations[j][:], exposure_pair(j), MULT)
                 opaque, translucent = vals[:, 0], vals[:, 1]
-            nc.gpsimd.tensor_tensor(translucent, translucent, colours[j], MULT)
+            if j + 1 < PAGES:
+                nc.gpsimd.tensor_tensor(translucent, translucent, colours[j], MULT)
+            else:
+                for h in range(2):
+                    cols = slice(h * BANK, (h + 1) * BANK)
+                    nc.gpsimd.tensor_tensor(translucent[:, cols], translucent[:, cols], colours[j][h], MULT)
             return opaque, translucent
 
         def scatter(j, sources):
@@ -263,37 +316,35 @@ def tile_list_deferred_tile_shading_kernel(
                 opaque_layer(j + 1, activation_pair(j)[:, 0])
             translucent_layer(j)
 
-        def round_w4():
-            rounded = placed_tile([P, 2, 4 * N], BF16, "w4_rounded", FIRST_TRANSLUCENT_AT)
-            for b in range(2):
-                nc.scalar.copy(
-                    rounded[:, b].rearrange("p (n i t) -> p n t i", i=4, t=4),
-                    w4_raw[:, b].rearrange("p t (n i) -> p n t i", i=4))
-            return rounded
+        turned = [placed_tile([P, BLOCKS, 2, P], F32, "turned%d" % c, TURNED_AT + c * 4 * KIB) for c in range(CHUNKS)]
 
-        def apply_mix(s, engine, cols):
-            engine.tensor_tensor(z_row(s)[:, cols], pages[s][:, cols], mix_tiles[s][:, cols], MULT)
+        def turn(s, z):
+            for c in range(CHUNKS):
+                acc = bank(TURN_BANKS, BF16)
+                for k in range(BLOCKS):
+                    at = c * BANK + k * P
+                    nc.tensor.transpose(acc[:, k * P : (k + 1) * P], z[:, at : at + P], identity[BF16][:])
+                nc.scalar.copy(
+                    turned[c][:, :, :, 32 * s : 32 * (s + 1)],
+                    acc[:].bitcast(F32).rearrange("p (k q v) -> p k v q", k=BLOCKS, v=2))
 
         woven = {}
 
-        def weave(b, c, on_vector):
-            tile = placed_tile([P, 4 * BANK], BF16, "woven%d_%d" % (b, c), WOVEN_AT[b] + c * 4 * KIB)
-            dst = tile[:].rearrange("p (m i t) -> p m t i", i=4, t=4)
-            src = z_rows[b][:].rearrange("p (t c m i) -> p c m t i", t=4, c=CHUNKS, i=4)[:, c]
-            if on_vector:
-                nc.vector.tensor_copy(dst, src)
-            else:
-                nc.scalar.copy(dst, src)
-            woven.setdefault((b, c), tile)
+        def woven_tile(b, c):
+            woven.setdefault((b, c), placed_tile([P, 4 * BANK], BF16, "woven%d_%d" % (b, c), WOVEN_AT[b] + c * 4 * KIB))
+            return woven[b, c]
 
-        def quantise_z(b, c):
-            codes = placed_tile([P, BANK], U32, "z_codes%d_%d" % (b, c), Z_CODES_AT + (b * CHUNKS + c) * 2 * KIB)
-            if b == 0:
-                plane = placed_tile([P, BANK], U8, "z_plane0_%d" % c, LAST_SOURCES_AT + c * HALF)
-            else:
-                plane = new_tile([P, BANK], U8, "z_plane1_%d" % c)
-            nc.vector.quantize_mx(out=codes[:].bitcast(FP8X4), scales=plane[:], in_=woven[b, c][:])
-            return codes, plane
+        def turn_back(c):
+            words = woven_tile(0, c)[:].bitcast(F32)
+            for pair in range(BLOCKS // 2):
+                acc = bank(TURN_BANKS)
+                for k in range(2):
+                    for v in range(2):
+                        at = (2 * k + v) * P
+                        nc.tensor.transpose(acc[:, at : at + P], turned[c][:, 2 * pair + k, v], identity[F32][:])
+                nc.scalar.copy(
+                    words[:, pair * BANK : (pair + 1) * BANK].rearrange("p (k m v) -> p k m v", k=2, v=2),
+                    acc[:].rearrange("p (k v m) -> p k m v", k=2, v=2))
 
         translucent_layer(0)
         scatter(0, expose(0))
@@ -301,40 +352,72 @@ def tile_list_deferred_tile_shading_kernel(
         scatter(1, expose(1))
         layers(2)
         for s in range(PAGES - 1):
-            apply_mix(s, nc.gpsimd, slice(0, T2))
-            if s + 2 < PAGES:
-                scatter(s + 2, expose(s + 2))
+            z = z_row(s)
+            nc.gpsimd.tensor_tensor(z, pages[s][:], mix_tiles[s], MULT)
             if s + 3 < PAGES:
+                scatter(s + 2, expose(s + 2))
                 layers(s + 3)
-            if 1 <= s and s + 1 < PAGES:
+            if s + 4 == PAGES:
+                scatter(s + 3, expose(s + 3))
+            if s >= 1:
                 load_mix(s + 1)
+            if s < EARLY:
+                turn(s, z)
             if s == 1:
-                w4_rounded = round_w4()
-            if s == 3:
+                w4_rounded = placed_tile([P, 2, 4 * N], BF16, "w4_rounded", FIRST_TRANSLUCENT_AT)
+                for b in range(2):
+                    round_rows(w4_rounded[:, b], w4_raw[:, b])
+            if s + 1 == EARLY:
                 for c in range(CHUNKS):
-                    weave(0, c, False)
+                    turn_back(c)
+            if s == EARLY + 1:
+                nc.scalar.copy(pairs[:, 0], late_rows[:].rearrange("p (e m) -> p m e", e=2))
 
-        for c in range(CHUNKS):
-            apply_mix(PAGES - 1, nc.vector, slice(c * BANK, (c + 1) * BANK))
-        for c in range(CHUNKS):
-            weave(1, c, c >= 2)
-        w4_codes = new_tile([P, 2 * N], U32, "w4_codes")
-        w4_plane = placed_tile([P, 2 * N], U8, "w4_plane", LAST_SOURCES_AT + CHUNKS * HALF)
-        nc.vector.quantize_mx(out=w4_codes[:].bitcast(FP8X4), scales=w4_plane[:], in_=w4_rounded[:].rearrange("p b x -> p (b x)"))
-        order = (0, 2, 3, 1)
-        for c in order:
-            accs = [bank() for half in range(2)]
-            for b in range(2):
-                codes, plane = quantise_z(b, c)
-                for half in range(2):
-                    cols = slice(b * N + half * P, b * N + (half + 1) * P)
-                    nc.tensor.matmul_mx(
-                        out=accs[half][:], lhsT=w4_codes[:, cols].bitcast(FP8X4), lhsT_scale=w4_plane[:, cols],
-                        rhs=codes[:].bitcast(FP8X4), rhs_scale=plane[:], start=(b == 0), stop=(b == 1))
+        last = PAGES - 1
+        accs = {}
+
+        def last_row(c):
+            cols = slice(c * BANK, (c + 1) * BANK)
+            nc.vector.tensor_tensor(z_row(last)[:, cols], pages[last][:, cols], mix_tiles[last][c][:], MULT)
+            words = pairs[:].rearrange("p u m e -> p u (m e)").bitcast(U32)
+            nc.scalar.copy(
+                woven_tile(1, c)[:].bitcast(U32).rearrange("p (m u) -> p m u", u=2), words[:, :, cols].rearrange("p u m -> p m u"))
+
+        def shade(b, c):
+            codes = placed_tile([P, BANK], U32, "z_codes%d_%d" % (b, c), Z_CODES_AT + (b * CHUNKS + c) * 2 * KIB)
+            if b == 0:
+                plane = placed_tile([P, BANK], U8, "z_plane0_%d" % c, MIX_AT[0] + c * 2 * KIB)
+            else:
+                plane = new_tile([P, BANK], U8, "z_plane1_%d" % c)
+            nc.vector.quantize_mx(out=codes[:].bitcast(FP8X4), scales=plane[:], in_=woven[b, c][:])
             for half in range(2):
-                result = placed_tile([P, BANK], F32, "result%d_%d" % (c, half), Z_AT[0] + (2 * c + half) * 2 * KIB)
-                if c == order[-1] and half == 1:
-                    nc.vector.tensor_copy(result[:], accs[half][:])
-                else:
-                    nc.scalar.copy(result[:], accs[half][:])
-                nc.sync.dma_start(out[half * P : (half + 1) * P, c * BANK : (c + 1) * BANK], result[:])
+                if b == 0:
+                    accs.setdefault((c, half), bank(SUM_BANKS))
+                cols = slice(b * N + half * P, b * N + (half + 1) * P)
+                nc.tensor.matmul_mx(
+                    out=accs[c, half][:], lhsT=w4_codes[:, cols].bitcast(FP8X4), lhsT_scale=w4_plane[:, cols],
+                    rhs=codes[:].bitcast(FP8X4), rhs_scale=plane[:], start=(b == 0), stop=(b == 1))
+
+        def store(c, half, on_vector):
+            result = placed_tile([P, BANK], F32, "result%d_%d" % (c, half), ROWS_AT + (2 * c + half) * 2 * KIB)
+            if on_vector:
+                nc.vector.tensor_copy(result[:], accs[c, half][:])
+            else:
+                nc.scalar.copy(result[:], accs[c, half][:])
+            nc.sync.dma_start(out[half * P : (half + 1) * P, c * BANK : (c + 1) * BANK], result[:])
+
+        last_row(0)
+        w4_codes = new_tile([P, 2 * N], U32, "w4_codes")
+        w4_plane = placed_tile([P, 2 * N], U8, "w4_plane", LAST_SOURCES_AT + 2 * KIB)
+        nc.vector.quantize_mx(out=w4_codes[:].bitcast(FP8X4), scales=w4_plane[:], in_=w4_rounded[:].rearrange("p b x -> p (b x)"))
+        for c in range(1, CHUNKS):
+            if c <= CHUNKS // 2:
+                shade(0, c - 1)
+            last_row(c)
+        for c in range(CHUNKS):
+            if c >= CHUNKS // 2:
+                shade(0, c)
+            shade(1, c)
+        for c in range(CHUNKS):
+            for half in range(2):
+                store(c, half, c >= CHUNKS // 2 and half == 1)

@@ -25,24 +25,39 @@ BLOCKS = BANK // P
 KIB = 1024
 HALF = KIB // 2
 QUADRANTS = (0, 2, 1, 3)
+SCALE_ROWS = 16
+OPAQUE_ROWS_FROM = 112
+TRANSLUCENT_ROWS_FROM = 48
+FIRST_PIECES = ((0, 256), (256, 512), (512, 1024))
 
-PAGE_AT = (0, 24 * KIB, 32 * KIB)
-Z_CODES_AT = 8 * KIB
-TAB2_WORDS_AT = Z_CODES_AT + HALF
-W3_LATE_WORDS_AT = PAGE_AT[1] + HALF
-W2_ROUNDED_AT = PAGE_AT[1] + 4 * KIB
-ROWS_AT = 40 * KIB
-PAIRS_AT = 56 * KIB
-WOVEN_AT = (72 * KIB, 88 * KIB)
+PAGE_AT = (0, 8 * KIB, 52 * KIB)
+MIX_AT = (16 * KIB, 24 * KIB, 40 * KIB)
+ACTIVATIONS_AT = (193 * KIB, 32 * KIB)
+TAB2_WORDS_AT = MIX_AT[0] - HALF
+W2_EARLY_RAW_AT = ACTIVATIONS_AT[1] - HALF
+TAB2_ROWS_AT = W2_EARLY_RAW_AT - 2 * KIB
+SECOND_OPAQUE_AT = MIX_AT[2] + 4 * KIB
+SECOND_TRANSLUCENT_AT = MIX_AT[2] + 8 * KIB
+Z_AT = (60 * KIB, 66 * KIB, 72 * KIB, 76 * KIB)
+COLOUR_AT = (SECOND_TRANSLUCENT_AT - 2 * KIB, 62 * KIB, 68 * KIB, 72 * KIB, 76 * KIB)
+W2_LATE_ROUNDED_AT = 64 * KIB
+RESULTS_AT = Z_AT[0]
+PAIRS_AT = 80 * KIB
+GATHERED_ROWS_AT = PAIRS_AT + 8 * KIB
+WOVEN_AT = (96 * KIB, 112 * KIB)
 TURNED_AT = WOVEN_AT[1]
-MIX_AT = (104 * KIB, 112 * KIB, 120 * KIB)
-TAB2_PLANE_AT = 128 * KIB
-FIRST_OPAQUE_AT = TAB2_PLANE_AT + 4 * KIB
-FIRST_SQUARED_AT = (W2_ROUNDED_AT + 3 * KIB, FIRST_OPAQUE_AT)
-FIRST_TRANSLUCENT_AT = FIRST_OPAQUE_AT + 4 * KIB
-LATE_ROWS_AT = FIRST_TRANSLUCENT_AT + 4 * KIB
-LAST_SOURCES_AT = LATE_ROWS_AT + 8 * KIB
-LAYER_BANKS = (0, 1, 2, 3, 4, 5)
+TAB1_WORDS_AT = 120 * KIB + HALF
+AFTER_TAB1_AT = 128 * KIB
+FIRST_OPAQUE_AT = 137 * KIB
+FIRST_SQUARED_AT = (FIRST_OPAQUE_AT, AFTER_TAB1_AT + 4 * KIB - HALF, WOVEN_AT[0] + 7 * KIB)
+EXPOSURES_AT = FIRST_OPAQUE_AT + 4 * KIB - HALF
+FIRST_TRANSLUCENT_AT = 173 * KIB
+LATE_ROWS_AT = 181 * KIB
+LAST_SOURCES_AT = 189 * KIB
+STAGE_AT = 201 * KIB
+Z_CODES_AT = (PAGE_AT[2], MIX_AT[2])
+OPAQUE_BANKS = (0, 1)
+TRANSLUCENT_BANKS = (2, 3, 4, 5, 5, 4, 3, 2)
 TURN_BANKS = (6, 7)
 SUM_BANKS = (0, 1, 2, 3, 4, 5, 6, 7)
 
@@ -58,8 +73,8 @@ def tile_list_deferred_tile_shading_kernel(
         shared = ctx.enter_context(tc.tile_pool(name="shared", bufs=1))
         ps = ctx.enter_context(tc.psum_pool(name="ps", bufs=1))
 
-        def new_tile(shape, dtype, name, tag=None, bufs=1):
-            return sb.tile(shape, dtype, name=name, tag=tag or name, bufs=bufs, align_bytes=64)
+        def new_tile(shape, dtype, name):
+            return sb.tile(shape, dtype, name=name, tag=name, bufs=1, align_bytes=64)
 
         def placed_tile(shape, dtype, name, offset):
             return shared.tile(shape, dtype, name=name, tag=name, bufs=1, align_bytes=64, offset=offset)
@@ -69,21 +84,12 @@ def tile_list_deferred_tile_shading_kernel(
         def bank(ring, dtype=F32):
             taken = turns_taken.setdefault(ring, [])
             taken.append(ring[len(taken) % len(ring)])
-            return ps.tile([P, BANK], dtype, name="bank%d_%d" % (len(ring), len(taken)), tag="bank%d" % taken[-1])
+            return ps.tile([P, BANK], dtype, name="bank%d_%d_%d" % (ring[0], len(ring), len(taken)), tag="bank%d" % taken[-1])
 
         def load_list(src, name):
             dst = lists.tile([P, S // 16], U16, name=name)
             nc.sync.dma_start(dst[:], src)
             return dst
-
-        def load_scale_rows(src, rows):
-            for q in QUADRANTS:
-                nc.sync.dma_start(rows[32 * q : 32 * q + 4, :].bitcast(I32), src[0, 4 * q : 4 * q + 4, :].bitcast(I32))
-            return rows
-
-        def zeroed(engine, plane):
-            engine.memset(plane.bitcast(I32), 0)
-            return plane
 
         def words_of(src):
             return src[0].rearrange("p n i -> p (n i)").bitcast(I32)
@@ -92,122 +98,108 @@ def tile_list_deferred_tile_shading_kernel(
             nc.sync.dma_start(dst[:], src)
             return dst
 
-        def load_dealt(dst, src, t):
-            for q in QUADRANTS:
-                nc.sync.dma_start(dst[32 * q : 32 * q + 32, :], src.rearrange("(p t) j -> t p j", t=4)[t])
+        def dealt_rows(src, t):
+            return src.rearrange("(a t b) j -> t a b j", t=4, b=4)[t]
 
-        tab1_rows = load_scale_rows(tab_scales, placed_tile([P, T], U8, "tab1_rows", PAIRS_AT)[:])
+        def to_quadrants(queue, plane, rows):
+            for q in QUADRANTS:
+                queue.dma_start(plane[32 * q : 32 * q + 4, :].bitcast(I32), rows[4 * q : 4 * q + 4, :].bitcast(I32))
+
+        opaque_rows = slice(OPAQUE_ROWS_FROM, OPAQUE_ROWS_FROM + SCALE_ROWS)
+        translucent_rows = slice(TRANSLUCENT_ROWS_FROM, TRANSLUCENT_ROWS_FROM + SCALE_ROWS)
+        tab1_s = placed_tile([P, T], U8, "tab1_s", PAIRS_AT)
+        tab2_s = placed_tile([P, T], U8, "tab2_s", TAB2_ROWS_AT)
+        stage = placed_tile([P, S + BANK], U8, "stage", STAGE_AT)
+        nc.scalar.dma_start(tab1_s[opaque_rows, :].bitcast(I32), tab_scales[0].bitcast(I32))
+        nc.scalar.dma_start(tab2_s[translucent_rows, :].bitcast(I32), tab2_scales[0].bitcast(I32))
+        nc.scalar.dma_start(stage[opaque_rows, S:].bitcast(I32), w1_scales[0, :, 0:BANK].bitcast(I32))
         idx1 = load_list(offs, "idx1")
+        idx2 = load_list(offs2, "idx2")
+        idx3 = load_list(offs3, "idx3")
+        tab1_w = load(placed_tile([P, T], I32, "tab1_w", TAB1_WORDS_AT), words_of(tab_words))
         w1_words_sb = new_tile([P, 2 * H], U8, "w1_words_sb")
         nc.sync.dma_start(w1_words_sb[:].bitcast(I32), w1_words[0].bitcast(I32))
-        tab1_w = load(placed_tile([P, T], I32, "tab1_w", WOVEN_AT[1]), words_of(tab_words))
-        w1_plane = load_scale_rows(w1_scales, zeroed(nc.vector, new_tile([P, H], U8, "w1_plane")[:]))
-        tab1_s = placed_tile([P, T], U8, "tab1_s", PAIRS_AT + 4 * KIB)
-        zeroed(nc.vector, tab1_s[:])
-        for q in QUADRANTS:
-            live = slice(32 * q, 32 * q + 4)
-            nc.vector.tensor_copy(tab1_s[live, :].bitcast(I32), tab1_rows[live, :].bitcast(I32))
-        idx3 = load_list(offs3, "idx3")
-        first_exposures = new_tile([P, 3, S], F32, "first_exposures")
-        nc.sync.dma_start(first_exposures[:, 1], wg1)
-        w2_raw = [placed_tile([P, 4, BANK], F32, "w2_raw%d" % b, WOVEN_AT[0] + 8 * KIB * b) for b in range(2)]
-        w2_rows = w2.rearrange("(p i) (b c) -> b p i c", i=4, b=2)
-        load(w2_raw[0], w2_rows[0])
-        idx2 = load_list(offs2, "idx2")
-        tab2_s = placed_tile([P, T], U8, "tab2_s", TAB2_PLANE_AT)
-        load_scale_rows(tab2_scales, zeroed(nc.gpsimd, tab2_s[:]))
-        load(w2_raw[1], w2_rows[1])
-        tab2_w = load(placed_tile([P, T], I32, "tab2_w", TAB2_WORDS_AT), words_of(tab2_words))
-        translucent_planes = new_tile([P, 3 * BANK], U8, "translucent_planes")
-        w3_plane = load_scale_rows(w3_scales, zeroed(nc.gpsimd, translucent_planes[:, 0:H]))
-        w3_late_words = load(placed_tile([P, BANK], I32, "w3_late_words", W3_LATE_WORDS_AT), words_of(w3_words)[:, BANK:])
-        w3_early_codes = load(new_tile([P, BANK], I32, "w3_early_codes"), words_of(w3_words)[:, 0:BANK])
-        nc.sync.dma_start(first_exposures[:, 2], wg2)
         idx4 = load_list(offs4, "idx4")
+        opaque_exposure = load(new_tile([P, S], F32, "opaque_exposure"), wg1)
 
-        mix_tiles = {}
-
-        def load_mix(s):
-            src = mix[s * P : (s + 1) * P, :] if s < EARLY else mix[K:, :].rearrange("(p t) m -> t p m", t=4)[s - EARLY]
-            if s + 1 < PAGES:
-                rows = last_pairs if s + 2 == PAGES else placed_tile([P, T2], F32, "mix%d" % s, MIX_AT[s % 3])[:]
-                nc.sync.dma_start(rows, src)
-            else:
-                rows = [
-                    load(placed_tile([P, BANK], F32, "last_mix%d" % c, MIX_AT[0] + c * 2 * KIB), src[:, c * BANK : (c + 1) * BANK])
-                    for c in range(CHUNKS)]
-            mix_tiles.setdefault(s, rows)
-
-        load_mix(0)
-        load_mix(1)
-        w4_raw = placed_tile([P, 2, 4, N], F32, "w4_raw", PAIRS_AT + 8 * KIB)
-        nc.sync.dma_start(w4_raw[:].rearrange("p b t n -> p b (t n)"), w4.rearrange("(b p t) n -> p b (t n)", b=2, t=4))
-        load_dealt(first_exposures[:, 0], wg1, 0)
-        late_exposures = [new_tile([P, 2, S], F32, "late_exposures%d" % t) for t in range(3)]
-        for t in range(3):
-            load_dealt(late_exposures[t][:, 0], wg1, t + 1)
-            load_dealt(late_exposures[t][:, 1], wg2, t)
-        last_exposure = new_tile([P, S], F32, "last_exposure")
-        load_dealt(last_exposure[:], wg2, 3)
-
-        def exposure_pair(j):
-            if j >= EARLY:
-                return late_exposures[j - EARLY][:]
-            return first_exposures[:, 1:3] if j + 1 < EARLY else first_exposures[:, 0:3:2]
-
-        identity = {}
-        for dtype, name in ((BF16, "identity_values"), (F32, "identity_words")):
-            identity.setdefault(dtype, new_tile([P, P], dtype, name))
-            make_identity(nc, identity[dtype][:])
-
-        def deal_columns(dealt, raw):
-            nc.vector.tensor_copy(dealt.rearrange("p (t m) -> p m t", t=4), raw.rearrange("p (m t) -> p m t", t=4))
-
+        nc.vector.memset(tab1_s[0 : opaque_rows.start, :].bitcast(I32), 0)
+        nc.gpsimd.memset(tab2_s[0 : translucent_rows.start, :].bitcast(I32), 0)
+        nc.gpsimd.memset(tab2_s[translucent_rows.stop :, :].bitcast(I32), 0)
+        carried_planes = new_tile([P, S + BANK + S], U8, "carried_planes")
+        nc.gpsimd.memset(carried_planes[:].bitcast(I32), 0)
+        late_planes = new_tile([P, 2 * BANK], U8, "late_planes")
+        nc.gpsimd.memset(late_planes[:].bitcast(I32), 0)
         table_warm_up = new_tile([P, 2], F32, "table_warm_up")
         nc.vector.memset(table_warm_up[:, 0:1], 0.0)
         nc.scalar.activation(table_warm_up[:, 1:2], table_warm_up[:, 0:1], ACT.Sigmoid)
 
-        halves1 = [idx1[:, h * BANK // 16 : (h + 1) * BANK // 16] for h in range(2)]
-        halves3 = [idx3[:, h * BANK // 16 : (h + 1) * BANK // 16] for h in range(2)]
-        v1_plane = new_tile([P, S], U8, "v1_plane")
-        v1_codes = [new_tile([P, BANK], U32, "v1_codes%d" % h) for h in range(2)]
-        nc.vector.tensor_copy(v1_plane[:], tab1_s[:].indirect(idx1[:]))
-        for h in range(2):
-            nc.vector.tensor_copy(v1_codes[h][:], tab1_w[:].bitcast(U32).indirect(halves1[h]))
-        w1_late_codes = new_tile([P, H], U8, "w1_late_codes")
-        deal_columns(w1_late_codes[:].bitcast(U16), w1_words_sb[:, H:].bitcast(U16))
-        w1_late_plane = new_tile([P, BANK], U8, "w1_late_plane")
-        deal_columns(w1_late_plane[:], w1_plane[:, BANK:])
+        v1_rows = placed_tile([P, S], U8, "v1_rows", GATHERED_ROWS_AT)
+        nc.vector.tensor_copy(v1_rows[:], tab1_s[:].indirect(idx1[:]))
+        nc.vector.tensor_copy(stage[96:, 0:S].bitcast(I32), v1_rows[96:, :].bitcast(I32))
+        to_quadrants(nc.scalar, carried_planes[:, 0 : S + BANK], stage[opaque_rows, :])
+        v1_plane, w1_plane, v2_plane = carried_planes[:, 0:S], carried_planes[:, S : S + BANK], carried_planes[:, S + BANK :]
+        v2_rows = placed_tile([P, S], U8, "v2_rows", GATHERED_ROWS_AT)
+        nc.vector.tensor_copy(v2_rows[:], tab2_s[:].indirect(idx2[:]))
+
+        w2_rows = w2.rearrange("(p i) (b c) -> b p i c", i=4, b=2)
+        w2_early_raw = load(placed_tile([P, 4, BANK], F32, "w2_early_raw", W2_EARLY_RAW_AT), w2_rows[0])
+        to_quadrants(nc.sync, v2_plane, v2_rows[translucent_rows, :])
+        tab2_w = load(placed_tile([P, T], I32, "tab2_w", TAB2_WORDS_AT), words_of(tab2_words))
+
+        def gather_words(table, idx, name):
+            halves = []
+            for h in range(2):
+                halves.append(new_tile([P, BANK], U32, "%s%d" % (name, h)))
+                nc.vector.tensor_copy(halves[h][:], table[:].bitcast(U32).indirect(idx[:, h * BANK // 16 : (h + 1) * BANK // 16]))
+            return halves
+
+        v1_codes = gather_words(tab1_w, idx1, "v1_codes")
+
+        w3_plane = placed_tile([P, BANK], U8, "w3_plane", AFTER_TAB1_AT + 6 * KIB)
+        nc.gpsimd.memset(w3_plane[:].bitcast(I32), 0)
+        to_quadrants(nc.sync, w3_plane, w3_scales[0, :, 0:BANK])
+
+        identity = {}
+        for dtype, name, at in ((F32, "identity_words", 0), (BF16, "identity_values", HALF)):
+            identity.setdefault(dtype, placed_tile([P, P], dtype, name, AFTER_TAB1_AT + 7 * KIB + HALF + at))
+            make_identity(nc, identity[dtype][:])
+
+        def deal_columns(dealt, raw):
+            nc.scalar.copy(
+                dealt.bitcast(U32).rearrange("p (t a w) -> p t a w", t=4, a=32),
+                raw.bitcast(U32).rearrange("p (a t w) -> p t a w", t=4, a=32))
+            return dealt
 
         def page_columns(early, late, s, width):
             u = s % EARLY
             return (early if s < EARLY else late)[:, width * u : width * (u + 1)]
 
-        def product(codes, plane, dtype, moving, moving_plane):
-            acc = bank(LAYER_BANKS)
+        def product(codes, plane, dtype, moving, moving_plane, width=BANK):
+            acc = bank(OPAQUE_BANKS if dtype == FP4X4 else TRANSLUCENT_BANKS)[:, 0:width]
             nc.tensor.matmul_mx(
-                out=acc[:], lhsT=codes.bitcast(dtype), lhsT_scale=plane,
+                out=acc, lhsT=codes.bitcast(dtype), lhsT_scale=plane,
                 rhs=moving.bitcast(FP8X4), rhs_scale=moving_plane, start=True, stop=True)
             return acc
+
+        late = {}
+
+        def rectify(s, lo, hi, dst):
+            h = lo // BANK
+            acc = product(page_columns(w1_words_sb, late.get("w1_codes"), s, 2 * P), page_columns(w1_plane, late.get("w1_plane"), s, P),
+                          FP4X4, v1_codes[h][:, lo - h * BANK : hi - h * BANK], v1_plane[:, lo:hi], hi - lo)
+            nc.scalar.activation(dst, acc, ACT.Relu)
+
+        def opaque_layer(s, squared):
+            for h in range(2):
+                rectify(s, h * BANK, (h + 1) * BANK, squared[:, h * BANK : (h + 1) * BANK])
+            nc.scalar.activation(squared, squared, ACT.Square)
 
         activations = {}
 
         def activation_pair(j):
-            if j == 1 and j not in activations:
-                activations.setdefault(j, placed_tile([P, 2, S], F32, "activations1", WOVEN_AT[0] + 4 * KIB))
             if j not in activations:
-                activations.setdefault(j, new_tile([P, 2, S], F32, "activations%d" % j, "activations", 2))
+                activations.setdefault(j, placed_tile([P, 2, S], F32, "activations%d" % j, ACTIVATIONS_AT[j % 2]))
             return activations[j]
-
-        def rectify(s, h, dst):
-            acc = product(page_columns(w1_words_sb, w1_late_codes, s, 2 * P), page_columns(w1_plane, w1_late_plane, s, P),
-                          FP4X4, v1_codes[h][:], v1_plane[:, h * BANK : (h + 1) * BANK])
-            nc.scalar.activation(dst, acc[:], ACT.Relu)
-
-        def opaque_layer(s, squared):
-            for h in range(2):
-                rectify(s, h, squared[:, h * BANK : (h + 1) * BANK])
-            nc.scalar.activation(squared, squared, ACT.Square)
 
         pages = {}
 
@@ -216,47 +208,74 @@ def tile_list_deferred_tile_shading_kernel(
             return pages[s]
 
         new_page(0)
-        for h in range(2):
-            squared = placed_tile([P, BANK], F32, "first_squared%d" % h, FIRST_SQUARED_AT[h])
-            rectify(0, h, squared[:])
+        for i, (lo, hi) in enumerate(FIRST_PIECES):
+            squared = placed_tile([P, hi - lo], F32, "first_squared%d" % i, FIRST_SQUARED_AT[i])
+            rectify(0, lo, hi, squared[:])
             nc.scalar.activation(squared[:], squared[:], ACT.Square)
-            nc.vector.tensor_tensor(
-                pages[0][:].indirect(halves3[h]), squared[:], first_exposures[:, 1, h * BANK : (h + 1) * BANK], MULT)
+            nc.vector.tensor_tensor(pages[0][:].indirect(idx3[:, lo // 16 : hi // 16]), squared[:], opaque_exposure[:, lo:hi], MULT)
 
-        v2_plane = new_tile([P, S], U8, "v2_plane")
-        nc.vector.tensor_copy(v2_plane[:], tab2_s[:].indirect(idx2[:]))
-        opaque_layer(1, activation_pair(0)[:, 0])
-        opaque1 = placed_tile([P, S], F32, "opaque1", FIRST_OPAQUE_AT)
-        nc.gpsimd.tensor_tensor(opaque1[:], activations[0][:, 0], first_exposures[:, 1], MULT)
+        w3_early_codes = load(placed_tile([P, BANK], I32, "w3_early_codes", AFTER_TAB1_AT + 4 * KIB), words_of(w3_words)[:, 0:BANK])
+        translucent_exposure = load(placed_tile([P, S], F32, "translucent_exposure", AFTER_TAB1_AT), wg2)
 
         def round_rows(rounded, raw):
             nc.scalar.copy(
                 rounded.rearrange("p (n i t) -> p n t i", i=4, t=4), raw.rearrange("p t (n i) -> p n t i", i=4))
 
-        w2_rounded = placed_tile([P, 8 * BANK], BF16, "w2_rounded", W2_ROUNDED_AT)
-        round_rows(w2_rounded[:, 0 : 4 * BANK], w2_raw[0][:])
-        nc.scalar.copy(
-            w2_rounded[:, 4 * BANK :].rearrange("p (t m i) -> p m i t", t=4, i=4),
-            w2_raw[1][:].rearrange("p i (m t) -> p m i t", t=4))
-        v2_codes = placed_tile([P, S], U32, "v2_codes", WOVEN_AT[0] + 12 * KIB)
-        nc.vector.tensor_copy(v2_codes[:], tab2_w[:].bitcast(U32).indirect(idx2[:]))
-        w3_late_plane = new_tile([P, BANK], U8, "w3_late_plane")
-        deal_columns(w3_late_plane[:], w3_plane[:, BANK:])
-        w3_late_codes = new_tile([P, BANK], I32, "w3_late_codes")
-        deal_columns(w3_late_codes[:], w3_late_words[:])
-        w2_codes = placed_tile([P, H], U32, "w2_codes", TAB2_PLANE_AT)
-        w2_plane = translucent_planes[:, BANK:]
-        nc.vector.quantize_mx(out=w2_codes[:].bitcast(FP8X4), scales=w2_plane, in_=w2_rounded[:])
+        def quantised(codes, name, rounded):
+            plane = new_tile([P, BANK], U8, name)
+            nc.vector.quantize_mx(out=codes[:].bitcast(FP8X4), scales=plane[:], in_=rounded)
+            return codes, plane
+
+        w2_early_rounded = placed_tile([P, 4 * BANK], BF16, "w2_early_rounded", FIRST_OPAQUE_AT)
+        round_rows(w2_early_rounded[:], w2_early_raw[:])
+        opaque_layer(1, activation_pair(0)[:, 0])
+        late.setdefault("w1_codes", deal_columns(new_tile([P, H], U8, "w1_late_codes")[:], w1_words_sb[:, H:]))
+        w2_early_codes, w2_early_plane = quantised(new_tile([P, BANK], U32, "w2_early_codes"), "w2_early_plane", w2_early_rounded[:])
+        v2_codes = gather_words(tab2_w, idx2, "v2_codes")
+        opaque1 = placed_tile([P, S], F32, "opaque1", FIRST_OPAQUE_AT)
+        nc.gpsimd.tensor_tensor(opaque1[:], activations[0][:, 0], opaque_exposure[:], MULT)
         nc.vector.tensor_copy(new_page(1)[:].indirect(idx3[:]), opaque1[:])
 
         late_rows = placed_tile([P, 2 * T2], BF16, "late_rows", LATE_ROWS_AT)
         pairs = placed_tile([P, 2, T2, 2], BF16, "pairs", PAIRS_AT)
         last_pairs = pairs[:, 1].rearrange("p m e -> p (m e)").bitcast(F32)
+        mix_tiles = {}
+
+        def load_mix(s):
+            src = mix[s * P : (s + 1) * P, :].unsqueeze(0) if s < EARLY else dealt_rows(mix[K:, :], s - EARLY)
+            if s + 1 < PAGES:
+                rows = last_pairs if s + 2 == PAGES else placed_tile([P, T2], F32, "mix%d" % s, MIX_AT[s % 3])[:]
+                nc.sync.dma_start(rows, src)
+            else:
+                rows = [
+                    load(placed_tile([P, BANK], F32, "last_mix%d" % c, MIX_AT[0] + c * 2 * KIB), src[:, :, c * BANK : (c + 1) * BANK])
+                    for c in range(CHUNKS)]
+            mix_tiles.setdefault(s, rows)
+
+        w2_late_raw = load(placed_tile([P, 4, BANK], F32, "w2_late_raw", WOVEN_AT[0]), w2_rows[1])
+        load_mix(0)
+        load_mix(1)
+        w4_raw = placed_tile([P, 2, 4, N], F32, "w4_raw", WOVEN_AT[0] + 8 * KIB)
+        nc.sync.dma_start(w4_raw[:, 0].rearrange("p t n -> p (t n)"), w4[0:K, :].rearrange("(p t) n -> p (t n)", t=4))
+        for t in range(4):
+            nc.sync.dma_start(w4_raw[:, 1, t], dealt_rows(w4[K:, :], t))
+        late_exposures = placed_tile([P, 8, S], F32, "late_exposures", EXPOSURES_AT)
+
+        def load_exposure(src, at, t):
+            for q in QUADRANTS:
+                nc.sync.dma_start(late_exposures[32 * q : 32 * q + 32, at + t], dealt_rows(src, t))
+
+        load_exposure(wg1, 0, 0)
+        for t in range(3):
+            load_exposure(wg1, 0, t + 1)
+            load_exposure(wg2, 4, t)
+        load_exposure(wg2, 4, 3)
+
         colours = {}
 
         def z_row(s):
             if s < EARLY:
-                return placed_tile([P, T2], BF16, "z%d" % s, ROWS_AT + 4 * KIB * s)[:]
+                return placed_tile([P, T2], BF16, "z%d" % s, Z_AT[s])[:]
             if s < EARLY + 2:
                 return late_rows[:, (s - EARLY) * T2 : (s - EARLY + 1) * T2]
             return pairs[:, 1, :, s - EARLY - 2]
@@ -267,8 +286,7 @@ def tile_list_deferred_tile_shading_kernel(
             if s == EARLY + 1:
                 whole = z_row(s - 1).bitcast(F32)
             else:
-                at = {0: MIX_AT[2], PAGES - 2: LAST_SOURCES_AT}.get(s, ROWS_AT + 4 * KIB * (s - 1))
-                whole = placed_tile([P, S], F32, "colour%d" % s, at)[:]
+                whole = placed_tile([P, S], F32, "colour%d" % s, LAST_SOURCES_AT if s == PAGES - 2 else COLOUR_AT[s])[:]
             colours.setdefault(s, whole)
             return [whole[:, h * BANK : (h + 1) * BANK] for h in range(2)]
 
@@ -277,25 +295,42 @@ def tile_list_deferred_tile_shading_kernel(
             colour = colour_halves(s)
             for h in range(2):
                 cols = slice(h * BANK, (h + 1) * BANK)
-                acc = product(page_columns(w3_early_codes, w3_late_codes, s, P), page_columns(w3_plane, w3_late_plane, s, P),
-                              FP8X4, v2_codes[:, cols], v2_plane[:, cols])
-                nc.scalar.activation(gate[:, cols], acc[:], ACT.Sigmoid)
-            for h in range(2):
-                cols = slice(h * BANK, (h + 1) * BANK)
-                acc = product(w2_codes[:, P * s : P * (s + 1)], w2_plane[:, P * s : P * (s + 1)], FP8X4,
-                              v2_codes[:, cols], v2_plane[:, cols])
-                nc.scalar.copy(colour[h], acc[:])
+                acc = product(page_columns(w2_early_codes, late.get("w2_codes"), s, P), page_columns(w2_early_plane, late.get("w2_plane"), s, P),
+                              FP8X4, v2_codes[h][:], v2_plane[:, cols])
+                nc.scalar.copy(colour[h], acc)
+                acc = product(page_columns(w3_early_codes, late.get("w3_codes"), s, P), page_columns(w3_plane, late.get("w3_plane"), s, P),
+                              FP8X4, v2_codes[h][:], v2_plane[:, cols])
+                nc.scalar.activation(gate[:, cols], acc, ACT.Sigmoid)
             colours.setdefault(s, colour)
 
         def expose(j):
-            if j in (0, PAGES - 1):
-                vals = placed_tile([P, S], F32, "sources%d" % j, FIRST_TRANSLUCENT_AT if j == 0 else LAST_SOURCES_AT)
+            opaque = None
+            if j == 0:
+                translucent = placed_tile([P, S], F32, "sources0", FIRST_TRANSLUCENT_AT)[:]
+                for h in range(2):
+                    cols = slice(h * BANK, (h + 1) * BANK)
+                    nc.gpsimd.tensor_tensor(translucent[:, cols], colours[0][:, cols], translucent_exposure[:, cols], MULT)
+                for h in range(2):
+                    cols = slice(h * BANK, (h + 1) * BANK)
+                    nc.gpsimd.tensor_tensor(translucent[:, cols], translucent[:, cols], activations[0][:, 1, cols], MULT)
+                return opaque, translucent
+            if j == PAGES - 1:
+                translucent = placed_tile([P, S], F32, "sources%d" % j, LAST_SOURCES_AT)[:]
+                nc.gpsimd.tensor_tensor(translucent, activations[j][:, 1], late_exposures[:, 7], MULT)
+            elif j < EARLY:
+                if j == 1:
+                    opaque = placed_tile([P, S], F32, "opaque2", SECOND_OPAQUE_AT)[:]
+                    translucent = placed_tile([P, S], F32, "translucent1", SECOND_TRANSLUCENT_AT)[:]
+                else:
+                    vals = placed_tile([P, 2, S], F32, "sources%d" % j, MIX_AT[(j + 1) % 3])
+                    opaque, translucent = vals[:, 0], vals[:, 1]
+                nc.gpsimd.tensor_tensor(translucent, activations[j][:, 1], translucent_exposure[:], MULT)
                 nc.gpsimd.tensor_tensor(
-                    vals[:], activations[j][:, 1], first_exposures[:, 2] if j == 0 else last_exposure[:], MULT)
-                opaque, translucent = None, vals[:]
+                    opaque, activations[j][:, 0], opaque_exposure[:] if j + 1 < EARLY else late_exposures[:, 0], MULT)
             else:
+                t = j - EARLY
                 vals = placed_tile([P, 2, S], F32, "sources%d" % j, MIX_AT[(j + 1) % 3])
-                nc.gpsimd.tensor_tensor(vals[:], activations[j][:], exposure_pair(j), MULT)
+                nc.gpsimd.tensor_tensor(vals[:], activations[j][:], late_exposures[:, t + 1 : t + 5 : 3], MULT)
                 opaque, translucent = vals[:, 0], vals[:, 1]
             if j + 1 < PAGES:
                 nc.gpsimd.tensor_tensor(translucent, translucent, colours[j], MULT)
@@ -348,9 +383,28 @@ def tile_list_deferred_tile_shading_kernel(
 
         translucent_layer(0)
         scatter(0, expose(0))
+        w3_late_words = load(placed_tile([P, BANK], I32, "w3_late_words", FIRST_TRANSLUCENT_AT + HALF), words_of(w3_words)[:, BANK:])
+        late_scale_rows = placed_tile([P, 2, BANK], U8, "late_scale_rows", FIRST_TRANSLUCENT_AT - HALF)
+        to_quadrants(nc.sync, late_scale_rows[:, 0], w1_scales[0, :, BANK:])
+        to_quadrants(nc.sync, late_scale_rows[:, 1], w3_scales[0, :, BANK:])
         layers(1)
         scatter(1, expose(1))
+        w2_late_rounded = placed_tile([P, 4 * BANK], BF16, "w2_late_rounded", W2_LATE_ROUNDED_AT)
+        nc.scalar.copy(
+            w2_late_rounded[:].rearrange("p (t a b i) -> p t a b i", t=4, b=4, i=4),
+            w2_late_raw[:].rearrange("p i (a t b) -> p t a b i", t=4, b=4))
+        w2_late = quantised(placed_tile([P, BANK], U32, "w2_late_codes", SECOND_TRANSLUCENT_AT), "w2_late_plane", w2_late_rounded[:])
+        late.setdefault("w2_codes", w2_late[0])
+        late.setdefault("w2_plane", w2_late[1])
         layers(2)
+        late.setdefault("w3_codes", deal_columns(new_tile([P, BANK], I32, "w3_late_codes")[:], w3_late_words[:]))
+        for q in QUADRANTS:
+            live = slice(32 * q, 32 * q + 4)
+            nc.scalar.copy(
+                late_planes[live, :].bitcast(U32).rearrange("p (o t a) -> p o t a", o=2, t=4),
+                late_scale_rows[live].rearrange("p o n -> p (o n)").bitcast(U32).rearrange("p (o a t) -> p o t a", o=2, t=4))
+        late.setdefault("w1_plane", late_planes[:, 0:BANK])
+        late.setdefault("w3_plane", late_planes[:, BANK:])
         for s in range(PAGES - 1):
             z = z_row(s)
             nc.gpsimd.tensor_tensor(z, pages[s][:], mix_tiles[s], MULT)
@@ -364,7 +418,7 @@ def tile_list_deferred_tile_shading_kernel(
             if s < EARLY:
                 turn(s, z)
             if s == 1:
-                w4_rounded = placed_tile([P, 2, 4 * N], BF16, "w4_rounded", FIRST_TRANSLUCENT_AT)
+                w4_rounded = placed_tile([P, 2, 4 * N], BF16, "w4_rounded", FIRST_TRANSLUCENT_AT + 3 * KIB + HALF)
                 for b in range(2):
                     round_rows(w4_rounded[:, b], w4_raw[:, b])
             if s + 1 == EARLY:
@@ -384,7 +438,7 @@ def tile_list_deferred_tile_shading_kernel(
                 woven_tile(1, c)[:].bitcast(U32).rearrange("p (m u) -> p m u", u=2), words[:, :, cols].rearrange("p u m -> p m u"))
 
         def shade(b, c):
-            codes = placed_tile([P, BANK], U32, "z_codes%d_%d" % (b, c), Z_CODES_AT + (b * CHUNKS + c) * 2 * KIB)
+            codes = placed_tile([P, BANK], U32, "z_codes%d_%d" % (b, c), Z_CODES_AT[b] + c * 2 * KIB)
             if b == 0:
                 plane = placed_tile([P, BANK], U8, "z_plane0_%d" % c, MIX_AT[0] + c * 2 * KIB)
             else:
@@ -399,7 +453,7 @@ def tile_list_deferred_tile_shading_kernel(
                     rhs=codes[:].bitcast(FP8X4), rhs_scale=plane[:], start=(b == 0), stop=(b == 1))
 
         def store(c, half, on_vector):
-            result = placed_tile([P, BANK], F32, "result%d_%d" % (c, half), ROWS_AT + (2 * c + half) * 2 * KIB)
+            result = placed_tile([P, BANK], F32, "result%d_%d" % (c, half), RESULTS_AT + (2 * c + half) * 2 * KIB)
             if on_vector:
                 nc.vector.tensor_copy(result[:], accs[c, half][:])
             else:

@@ -122,15 +122,14 @@ def tile_list_deferred_tile_shading_kernel(
         idx4 = load_list(offs4, "idx4")
         opaque_exposure = load(new_tile([P, S], F32, "opaque_exposure"), wg1)
 
-        nc.vector.memset(tab1_s[0 : opaque_rows.start, :].bitcast(I32), 0)
-        nc.gpsimd.memset(tab2_s[0 : translucent_rows.start, :].bitcast(I32), 0)
-        nc.gpsimd.memset(tab2_s[translucent_rows.stop :, :].bitcast(I32), 0)
+        table_warm_up = new_tile([P, 2], F32, "table_warm_up")
+        nc.gpsimd.memset(table_warm_up[:, 0:1], 0.0)
+        nc.gpsimd.memset(tab1_s[0 : opaque_rows.start, :].bitcast(I32), 0)
         carried_planes = new_tile([P, S + BANK + S], U8, "carried_planes")
         nc.gpsimd.memset(carried_planes[:].bitcast(I32), 0)
-        late_planes = new_tile([P, 2 * BANK], U8, "late_planes")
-        nc.gpsimd.memset(late_planes[:].bitcast(I32), 0)
-        table_warm_up = new_tile([P, 2], F32, "table_warm_up")
-        nc.vector.memset(table_warm_up[:, 0:1], 0.0)
+        nc.gpsimd.memset(tab2_s[0 : translucent_rows.start, :].bitcast(I32), 0)
+        nc.gpsimd.memset(tab2_s[translucent_rows.stop :, :].bitcast(I32), 0)
+        late_planes = placed_tile([P, 2 * BANK], U8, "late_planes", AFTER_TAB1_AT + 6 * KIB + HALF)
         nc.scalar.activation(table_warm_up[:, 1:2], table_warm_up[:, 0:1], ACT.Sigmoid)
 
         v1_rows = placed_tile([P, S], U8, "v1_rows", GATHERED_ROWS_AT)
@@ -157,6 +156,7 @@ def tile_list_deferred_tile_shading_kernel(
 
         w3_plane = placed_tile([P, BANK], U8, "w3_plane", AFTER_TAB1_AT + 6 * KIB)
         nc.gpsimd.memset(w3_plane[:].bitcast(I32), 0)
+        nc.gpsimd.memset(late_planes[:].bitcast(I32), 0)
         to_quadrants(nc.sync, w3_plane, w3_scales[0, :, 0:BANK])
 
         identity = {}
@@ -464,13 +464,10 @@ def tile_list_deferred_tile_shading_kernel(
         w4_codes = new_tile([P, 2 * N], U32, "w4_codes")
         w4_plane = placed_tile([P, 2 * N], U8, "w4_plane", LAST_SOURCES_AT + 2 * KIB)
         nc.vector.quantize_mx(out=w4_codes[:].bitcast(FP8X4), scales=w4_plane[:], in_=w4_rounded[:].rearrange("p b x -> p (b x)"))
-        for c in range(1, CHUNKS):
-            if c <= CHUNKS // 2:
-                shade(0, c - 1)
-            last_row(c)
         for c in range(CHUNKS):
-            if c >= CHUNKS // 2:
-                shade(0, c)
+            if c + 1 < CHUNKS:
+                last_row(c + 1)
+            shade(0, c)
             shade(1, c)
         for c in range(CHUNKS):
             for half in range(2):

@@ -30,12 +30,13 @@ OPAQUE_ROWS_FROM = 112
 TRANSLUCENT_ROWS_FROM = 48
 FIRST_PIECES = ((0, 256), (256, 512), (512, 1024))
 
-PAGE_AT = (0, 8 * KIB, 52 * KIB)
+PAGE_AT = (191 * KIB, 5 * KIB + HALF, 52 * KIB)
 MIX_AT = (16 * KIB, 24 * KIB, 40 * KIB)
-ACTIVATIONS_AT = (193 * KIB, 32 * KIB)
-TAB2_WORDS_AT = MIX_AT[0] - HALF
+ACTIVATIONS_AT = (183 * KIB, 32 * KIB)
+W2_EARLY_CODES_AT = PAGE_AT[1] + 8 * KIB
+TAB2_WORDS_AT = W2_EARLY_CODES_AT - HALF
 W2_EARLY_RAW_AT = ACTIVATIONS_AT[1] - HALF
-TAB2_ROWS_AT = W2_EARLY_RAW_AT - 2 * KIB
+TAB2_ROWS_AT = W2_EARLY_RAW_AT - 3 * KIB
 SECOND_OPAQUE_AT = MIX_AT[2] + 4 * KIB
 SECOND_TRANSLUCENT_AT = MIX_AT[2] + 8 * KIB
 Z_AT = (60 * KIB, 66 * KIB, 72 * KIB, 76 * KIB)
@@ -46,15 +47,18 @@ PAIRS_AT = 80 * KIB
 GATHERED_ROWS_AT = PAIRS_AT + 8 * KIB
 WOVEN_AT = (96 * KIB, 112 * KIB)
 TURNED_AT = WOVEN_AT[1]
-TAB1_WORDS_AT = 120 * KIB + HALF
+TAB1_WORDS_AT = 114 * KIB + HALF
 AFTER_TAB1_AT = 128 * KIB
-FIRST_OPAQUE_AT = 137 * KIB
-FIRST_SQUARED_AT = (FIRST_OPAQUE_AT, AFTER_TAB1_AT + 4 * KIB - HALF, WOVEN_AT[0] + 7 * KIB)
-EXPOSURES_AT = FIRST_OPAQUE_AT + 4 * KIB - HALF
-FIRST_TRANSLUCENT_AT = 173 * KIB
-LATE_ROWS_AT = 181 * KIB
-LAST_SOURCES_AT = 189 * KIB
-STAGE_AT = 201 * KIB
+W2_EARLY_ROUNDED_AT = KIB + HALF
+FIRST_OPAQUE_AT = WOVEN_AT[0] + 7 * KIB
+EARLY_EXPOSURES_AT = 199 * KIB
+W3_EARLY_CODES_AT = EARLY_EXPOSURES_AT + 8 * KIB
+FIRST_SQUARED_AT = (W2_EARLY_ROUNDED_AT, W3_EARLY_CODES_AT - HALF, FIRST_OPAQUE_AT)
+FIRST_TRANSLUCENT_AT = 163 * KIB
+EXPOSURES_AT = FIRST_TRANSLUCENT_AT + HALF - 32 * KIB
+LATE_ROWS_AT = 171 * KIB
+LAST_SOURCES_AT = 179 * KIB
+STAGE_AT = 0
 Z_CODES_AT = (PAGE_AT[2], MIX_AT[2])
 OPAQUE_BANKS = (0, 1)
 TRANSLUCENT_BANKS = (2, 3, 4, 5, 5, 4, 3, 2)
@@ -129,7 +133,7 @@ def tile_list_deferred_tile_shading_kernel(
         nc.gpsimd.memset(carried_planes[:].bitcast(I32), 0)
         nc.gpsimd.memset(tab2_s[0 : translucent_rows.start, :].bitcast(I32), 0)
         nc.gpsimd.memset(tab2_s[translucent_rows.stop :, :].bitcast(I32), 0)
-        late_planes = placed_tile([P, 2 * BANK], U8, "late_planes", AFTER_TAB1_AT + 6 * KIB + HALF)
+        late_planes = placed_tile([P, 2 * BANK], U8, "late_planes", AFTER_TAB1_AT + HALF)
         nc.scalar.activation(table_warm_up[:, 1:2], table_warm_up[:, 0:1], ACT.Sigmoid)
 
         v1_rows = placed_tile([P, S], U8, "v1_rows", GATHERED_ROWS_AT)
@@ -154,14 +158,14 @@ def tile_list_deferred_tile_shading_kernel(
 
         v1_codes = gather_words(tab1_w, idx1, "v1_codes")
 
-        w3_plane = placed_tile([P, BANK], U8, "w3_plane", AFTER_TAB1_AT + 6 * KIB)
+        w3_plane = placed_tile([P, BANK], U8, "w3_plane", AFTER_TAB1_AT)
         nc.gpsimd.memset(w3_plane[:].bitcast(I32), 0)
         nc.gpsimd.memset(late_planes[:].bitcast(I32), 0)
         to_quadrants(nc.sync, w3_plane, w3_scales[0, :, 0:BANK])
 
         identity = {}
         for dtype, name, at in ((F32, "identity_words", 0), (BF16, "identity_values", HALF)):
-            identity.setdefault(dtype, placed_tile([P, P], dtype, name, AFTER_TAB1_AT + 7 * KIB + HALF + at))
+            identity.setdefault(dtype, placed_tile([P, P], dtype, name, AFTER_TAB1_AT + KIB + HALF + at))
             make_identity(nc, identity[dtype][:])
 
         def deal_columns(dealt, raw):
@@ -214,8 +218,9 @@ def tile_list_deferred_tile_shading_kernel(
             nc.scalar.activation(squared[:], squared[:], ACT.Square)
             nc.vector.tensor_tensor(pages[0][:].indirect(idx3[:, lo // 16 : hi // 16]), squared[:], opaque_exposure[:, lo:hi], MULT)
 
-        w3_early_codes = load(placed_tile([P, BANK], I32, "w3_early_codes", AFTER_TAB1_AT + 4 * KIB), words_of(w3_words)[:, 0:BANK])
-        translucent_exposure = load(placed_tile([P, S], F32, "translucent_exposure", AFTER_TAB1_AT), wg2)
+        w3_early_codes = load(placed_tile([P, BANK], I32, "w3_early_codes", W3_EARLY_CODES_AT), words_of(w3_words)[:, 0:BANK])
+        early_exposures = placed_tile([P, 2, S], F32, "early_exposures", EARLY_EXPOSURES_AT)
+        nc.sync.dma_start(early_exposures[:, 1], wg2)
 
         def round_rows(rounded, raw):
             nc.scalar.copy(
@@ -226,12 +231,14 @@ def tile_list_deferred_tile_shading_kernel(
             nc.vector.quantize_mx(out=codes[:].bitcast(FP8X4), scales=plane[:], in_=rounded)
             return codes, plane
 
-        w2_early_rounded = placed_tile([P, 4 * BANK], BF16, "w2_early_rounded", FIRST_OPAQUE_AT)
-        round_rows(w2_early_rounded[:], w2_early_raw[:])
+        w2_early_rounded = placed_tile([P, 4 * BANK], BF16, "w2_early_rounded", W2_EARLY_ROUNDED_AT)
         opaque_layer(1, activation_pair(0)[:, 0])
+        round_rows(w2_early_rounded[:], w2_early_raw[:])
         late.setdefault("w1_codes", deal_columns(new_tile([P, H], U8, "w1_late_codes")[:], w1_words_sb[:, H:]))
-        w2_early_codes, w2_early_plane = quantised(new_tile([P, BANK], U32, "w2_early_codes"), "w2_early_plane", w2_early_rounded[:])
+        nc.scalar.copy(early_exposures[:, 0], opaque_exposure[:])
         v2_codes = gather_words(tab2_w, idx2, "v2_codes")
+        w2_early_codes, w2_early_plane = quantised(
+            placed_tile([P, BANK], U32, "w2_early_codes", W2_EARLY_CODES_AT), "w2_early_plane", w2_early_rounded[:])
         opaque1 = placed_tile([P, S], F32, "opaque1", FIRST_OPAQUE_AT)
         nc.gpsimd.tensor_tensor(opaque1[:], activations[0][:, 0], opaque_exposure[:], MULT)
         nc.vector.tensor_copy(new_page(1)[:].indirect(idx3[:]), opaque1[:])
@@ -261,15 +268,10 @@ def tile_list_deferred_tile_shading_kernel(
             nc.sync.dma_start(w4_raw[:, 1, t], dealt_rows(w4[K:, :], t))
         late_exposures = placed_tile([P, 8, S], F32, "late_exposures", EXPOSURES_AT)
 
-        def load_exposure(src, at, t):
+        def load_exposure(dst, src, t):
             for q in QUADRANTS:
-                nc.sync.dma_start(late_exposures[32 * q : 32 * q + 32, at + t], dealt_rows(src, t))
+                nc.sync.dma_start(dst[32 * q : 32 * q + 32], dealt_rows(src, t))
 
-        load_exposure(wg1, 0, 0)
-        for t in range(3):
-            load_exposure(wg1, 0, t + 1)
-            load_exposure(wg2, 4, t)
-        load_exposure(wg2, 4, 3)
 
         colours = {}
 
@@ -298,6 +300,8 @@ def tile_list_deferred_tile_shading_kernel(
                 acc = product(page_columns(w2_early_codes, late.get("w2_codes"), s, P), page_columns(w2_early_plane, late.get("w2_plane"), s, P),
                               FP8X4, v2_codes[h][:], v2_plane[:, cols])
                 nc.scalar.copy(colour[h], acc)
+            for h in range(2):
+                cols = slice(h * BANK, (h + 1) * BANK)
                 acc = product(page_columns(w3_early_codes, late.get("w3_codes"), s, P), page_columns(w3_plane, late.get("w3_plane"), s, P),
                               FP8X4, v2_codes[h][:], v2_plane[:, cols])
                 nc.scalar.activation(gate[:, cols], acc, ACT.Sigmoid)
@@ -309,28 +313,24 @@ def tile_list_deferred_tile_shading_kernel(
                 translucent = placed_tile([P, S], F32, "sources0", FIRST_TRANSLUCENT_AT)[:]
                 for h in range(2):
                     cols = slice(h * BANK, (h + 1) * BANK)
-                    nc.gpsimd.tensor_tensor(translucent[:, cols], colours[0][:, cols], translucent_exposure[:, cols], MULT)
+                    nc.gpsimd.tensor_tensor(translucent[:, cols], colours[0][:, cols], early_exposures[:, 1, cols], MULT)
                 for h in range(2):
                     cols = slice(h * BANK, (h + 1) * BANK)
                     nc.gpsimd.tensor_tensor(translucent[:, cols], translucent[:, cols], activations[0][:, 1, cols], MULT)
+                    nc.vector.tensor_copy(
+                        pages[0][:].indirect(idx4[:, h * BANK // 16 : (h + 1) * BANK // 16]), translucent[:, cols])
                 return opaque, translucent
             if j == PAGES - 1:
                 translucent = placed_tile([P, S], F32, "sources%d" % j, LAST_SOURCES_AT)[:]
                 nc.gpsimd.tensor_tensor(translucent, activations[j][:, 1], late_exposures[:, 7], MULT)
-            elif j < EARLY:
-                if j == 1:
-                    opaque = placed_tile([P, S], F32, "opaque2", SECOND_OPAQUE_AT)[:]
-                    translucent = placed_tile([P, S], F32, "translucent1", SECOND_TRANSLUCENT_AT)[:]
-                else:
-                    vals = placed_tile([P, 2, S], F32, "sources%d" % j, MIX_AT[(j + 1) % 3])
-                    opaque, translucent = vals[:, 0], vals[:, 1]
-                nc.gpsimd.tensor_tensor(translucent, activations[j][:, 1], translucent_exposure[:], MULT)
-                nc.gpsimd.tensor_tensor(
-                    opaque, activations[j][:, 0], opaque_exposure[:] if j + 1 < EARLY else late_exposures[:, 0], MULT)
             else:
-                t = j - EARLY
-                vals = placed_tile([P, 2, S], F32, "sources%d" % j, MIX_AT[(j + 1) % 3])
-                nc.gpsimd.tensor_tensor(vals[:], activations[j][:], late_exposures[:, t + 1 : t + 5 : 3], MULT)
+                vals = placed_tile([P, 2, S], F32, "sources%d" % j, SECOND_OPAQUE_AT if j == 1 else MIX_AT[(j + 1) % 3])
+                if j + 1 == EARLY:
+                    nc.gpsimd.tensor_tensor(vals[:, 1], activations[j][:, 1], early_exposures[:, 1], MULT)
+                    nc.gpsimd.tensor_tensor(vals[:, 0], activations[j][:, 0], late_exposures[:, 0], MULT)
+                else:
+                    exposures = early_exposures[:] if j < EARLY else late_exposures[:, j - EARLY + 1 : j - EARLY + 5 : 3]
+                    nc.gpsimd.tensor_tensor(vals[:], activations[j][:], exposures, MULT)
                 opaque, translucent = vals[:, 0], vals[:, 1]
             if j + 1 < PAGES:
                 nc.gpsimd.tensor_tensor(translucent, translucent, colours[j], MULT)
@@ -382,11 +382,16 @@ def tile_list_deferred_tile_shading_kernel(
                     acc[:].rearrange("p (k v m) -> p k m v", k=2, v=2))
 
         translucent_layer(0)
-        scatter(0, expose(0))
-        w3_late_words = load(placed_tile([P, BANK], I32, "w3_late_words", FIRST_TRANSLUCENT_AT + HALF), words_of(w3_words)[:, BANK:])
-        late_scale_rows = placed_tile([P, 2, BANK], U8, "late_scale_rows", FIRST_TRANSLUCENT_AT - HALF)
+        expose(0)
+        w3_late_words = load(placed_tile([P, BANK], I32, "w3_late_words", FIRST_TRANSLUCENT_AT + KIB + HALF), words_of(w3_words)[:, BANK:])
+        late_scale_rows = placed_tile([P, 2, BANK], U8, "late_scale_rows", FIRST_TRANSLUCENT_AT + HALF)
         to_quadrants(nc.sync, late_scale_rows[:, 0], w1_scales[0, :, BANK:])
         to_quadrants(nc.sync, late_scale_rows[:, 1], w3_scales[0, :, BANK:])
+        load_exposure(late_exposures[:, 0], wg1, 0)
+        for t in range(3):
+            load_exposure(late_exposures[:, t + 1], wg1, t + 1)
+            load_exposure(late_exposures[:, 4 + t], wg2, t)
+        load_exposure(late_exposures[:, 7], wg2, 3)
         layers(1)
         scatter(1, expose(1))
         w2_late_rounded = placed_tile([P, 4 * BANK], BF16, "w2_late_rounded", W2_LATE_ROUNDED_AT)
@@ -442,7 +447,7 @@ def tile_list_deferred_tile_shading_kernel(
             if b == 0:
                 plane = placed_tile([P, BANK], U8, "z_plane0_%d" % c, MIX_AT[0] + c * 2 * KIB)
             else:
-                plane = new_tile([P, BANK], U8, "z_plane1_%d" % c)
+                plane = placed_tile([P, BANK], U8, "z_plane1_%d" % c, STAGE_AT + 3 * KIB + HALF + c * HALF)
             nc.vector.quantize_mx(out=codes[:].bitcast(FP8X4), scales=plane[:], in_=woven[b, c][:])
             for half in range(2):
                 if b == 0:
@@ -461,7 +466,7 @@ def tile_list_deferred_tile_shading_kernel(
             nc.sync.dma_start(out[half * P : (half + 1) * P, c * BANK : (c + 1) * BANK], result[:])
 
         last_row(0)
-        w4_codes = new_tile([P, 2 * N], U32, "w4_codes")
+        w4_codes = placed_tile([P, 2 * N], U32, "w4_codes", STAGE_AT + KIB + HALF)
         w4_plane = placed_tile([P, 2 * N], U8, "w4_plane", LAST_SOURCES_AT + 2 * KIB)
         nc.vector.quantize_mx(out=w4_codes[:].bitcast(FP8X4), scales=w4_plane[:], in_=w4_rounded[:].rearrange("p b x -> p (b x)"))
         for c in range(CHUNKS):

@@ -30,35 +30,37 @@ OPAQUE_ROWS_FROM = 112
 TRANSLUCENT_ROWS_FROM = 48
 FIRST_PIECES = ((0, 256), (256, 512), (512, 1024))
 
-PAGE_AT = (191 * KIB, 5 * KIB + HALF, 52 * KIB)
-MIX_AT = (16 * KIB, 24 * KIB, 40 * KIB)
-ACTIVATIONS_AT = (183 * KIB, 32 * KIB)
+AFTER_TAB1_AT = 0
+TAB1_WORDS_AT = AFTER_TAB1_AT
+PAGE_AT = (191 * KIB, 8 * KIB, 54 * KIB + HALF)
 W2_EARLY_CODES_AT = PAGE_AT[1] + 8 * KIB
 TAB2_WORDS_AT = W2_EARLY_CODES_AT - HALF
-W2_EARLY_RAW_AT = ACTIVATIONS_AT[1] - HALF
-TAB2_ROWS_AT = W2_EARLY_RAW_AT - 3 * KIB
+MIX_AT = (18 * KIB, 26 * KIB, 42 * KIB + HALF)
+ACTIVATIONS_AT = (183 * KIB, 34 * KIB)
+W2_EARLY_RAW_AT = ACTIVATIONS_AT[1]
+TAB1_ROWS_AT = W2_EARLY_RAW_AT + 8 * KIB - HALF
 SECOND_OPAQUE_AT = MIX_AT[2] + 4 * KIB
 SECOND_TRANSLUCENT_AT = MIX_AT[2] + 8 * KIB
-Z_AT = (60 * KIB, 66 * KIB, 72 * KIB, 76 * KIB)
-COLOUR_AT = (SECOND_TRANSLUCENT_AT - 2 * KIB, 62 * KIB, 68 * KIB, 72 * KIB, 76 * KIB)
-W2_LATE_ROUNDED_AT = 64 * KIB
-RESULTS_AT = Z_AT[0]
-PAIRS_AT = 80 * KIB
+ROWS_AT = PAGE_AT[2] + 8 * KIB
+Z_AT = (ROWS_AT, ROWS_AT + 6 * KIB, ROWS_AT + 12 * KIB, ROWS_AT + 16 * KIB)
+COLOUR_AT = (SECOND_TRANSLUCENT_AT - 2 * KIB, ROWS_AT + 2 * KIB, ROWS_AT + 8 * KIB, Z_AT[2], Z_AT[3])
+W2_LATE_ROUNDED_AT = ROWS_AT + 4 * KIB
+RESULTS_AT = ROWS_AT
+PAIRS_AT = ROWS_AT + 20 * KIB
 GATHERED_ROWS_AT = PAIRS_AT + 8 * KIB
-WOVEN_AT = (96 * KIB, 112 * KIB)
+WOVEN_AT = (PAIRS_AT + 16 * KIB, PAIRS_AT + 32 * KIB)
 TURNED_AT = WOVEN_AT[1]
-TAB1_WORDS_AT = 114 * KIB + HALF
-AFTER_TAB1_AT = 128 * KIB
-W2_EARLY_ROUNDED_AT = KIB + HALF
+STAGE_AT = TURNED_AT
 FIRST_OPAQUE_AT = WOVEN_AT[0] + 7 * KIB
 EARLY_EXPOSURES_AT = 199 * KIB
-W3_EARLY_CODES_AT = EARLY_EXPOSURES_AT + 8 * KIB
-FIRST_SQUARED_AT = (W2_EARLY_ROUNDED_AT, W3_EARLY_CODES_AT - HALF, FIRST_OPAQUE_AT)
+LAST_RECTIFIED_AT = EARLY_EXPOSURES_AT + 7 * KIB
+W2_EARLY_ROUNDED_AT = LAST_RECTIFIED_AT + KIB
+W3_EARLY_CODES_AT = W2_EARLY_ROUNDED_AT + 4 * KIB
+FIRST_SQUARED_AT = (STAGE_AT + 2 * KIB, W3_EARLY_CODES_AT, FIRST_OPAQUE_AT)
 FIRST_TRANSLUCENT_AT = 163 * KIB
 EXPOSURES_AT = FIRST_TRANSLUCENT_AT + HALF - 32 * KIB
 LATE_ROWS_AT = 171 * KIB
 LAST_SOURCES_AT = 179 * KIB
-STAGE_AT = 0
 Z_CODES_AT = (PAGE_AT[2], MIX_AT[2])
 OPAQUE_BANKS = (0, 1)
 TRANSLUCENT_BANKS = (2, 3, 4, 5, 5, 4, 3, 2)
@@ -111,12 +113,12 @@ def tile_list_deferred_tile_shading_kernel(
 
         opaque_rows = slice(OPAQUE_ROWS_FROM, OPAQUE_ROWS_FROM + SCALE_ROWS)
         translucent_rows = slice(TRANSLUCENT_ROWS_FROM, TRANSLUCENT_ROWS_FROM + SCALE_ROWS)
-        tab1_s = placed_tile([P, T], U8, "tab1_s", PAIRS_AT)
-        tab2_s = placed_tile([P, T], U8, "tab2_s", TAB2_ROWS_AT)
-        stage = placed_tile([P, S + BANK], U8, "stage", STAGE_AT)
+        tab1_s = placed_tile([P, T], U8, "tab1_s", TAB1_ROWS_AT)
+        tab2_s = placed_tile([P, T], U8, "tab2_s", PAIRS_AT)
+        stage = placed_tile([P, 2 * BANK], U8, "stage", STAGE_AT)
         nc.scalar.dma_start(tab1_s[opaque_rows, :].bitcast(I32), tab_scales[0].bitcast(I32))
         nc.scalar.dma_start(tab2_s[translucent_rows, :].bitcast(I32), tab2_scales[0].bitcast(I32))
-        nc.scalar.dma_start(stage[opaque_rows, S:].bitcast(I32), w1_scales[0, :, 0:BANK].bitcast(I32))
+        nc.scalar.dma_start(stage[opaque_rows, BANK:].bitcast(I32), w1_scales[0, :, 0:BANK].bitcast(I32))
         idx1 = load_list(offs, "idx1")
         idx2 = load_list(offs2, "idx2")
         idx3 = load_list(offs3, "idx3")
@@ -129,25 +131,26 @@ def tile_list_deferred_tile_shading_kernel(
         table_warm_up = new_tile([P, 2], F32, "table_warm_up")
         nc.gpsimd.memset(table_warm_up[:, 0:1], 0.0)
         nc.gpsimd.memset(tab1_s[0 : opaque_rows.start, :].bitcast(I32), 0)
-        carried_planes = new_tile([P, S + BANK + S], U8, "carried_planes")
+        carried_planes = new_tile([P, 3 * BANK], U8, "carried_planes")
         nc.gpsimd.memset(carried_planes[:].bitcast(I32), 0)
         nc.gpsimd.memset(tab2_s[0 : translucent_rows.start, :].bitcast(I32), 0)
         nc.gpsimd.memset(tab2_s[translucent_rows.stop :, :].bitcast(I32), 0)
-        late_planes = placed_tile([P, 2 * BANK], U8, "late_planes", AFTER_TAB1_AT + HALF)
+        late_planes = placed_tile([P, 2 * BANK], U8, "late_planes", AFTER_TAB1_AT + KIB + HALF)
         nc.scalar.activation(table_warm_up[:, 1:2], table_warm_up[:, 0:1], ACT.Sigmoid)
 
-        v1_rows = placed_tile([P, S], U8, "v1_rows", GATHERED_ROWS_AT)
-        nc.vector.tensor_copy(v1_rows[:], tab1_s[:].indirect(idx1[:]))
-        nc.vector.tensor_copy(stage[96:, 0:S].bitcast(I32), v1_rows[96:, :].bitcast(I32))
-        to_quadrants(nc.scalar, carried_planes[:, 0 : S + BANK], stage[opaque_rows, :])
-        v1_plane, w1_plane, v2_plane = carried_planes[:, 0:S], carried_planes[:, S : S + BANK], carried_planes[:, S + BANK :]
-        v2_rows = placed_tile([P, S], U8, "v2_rows", GATHERED_ROWS_AT)
+        halves1 = [idx1[:, h * BANK // 16 : (h + 1) * BANK // 16] for h in range(2)]
+        v1_rows = [placed_tile([P, BANK], U8, "v1_rows%d" % h, GATHERED_ROWS_AT - h * HALF // 2) for h in range(2)]
+        nc.vector.tensor_copy(v1_rows[0][:], tab1_s[:].indirect(halves1[0]))
+        nc.vector.tensor_copy(stage[96:, 0:BANK].bitcast(I32), v1_rows[0][96:, :].bitcast(I32))
+        to_quadrants(nc.scalar, carried_planes[:, 0 : 2 * BANK], stage[opaque_rows, :])
+        v2_rows = placed_tile([P, S], U8, "v2_rows", GATHERED_ROWS_AT + HALF // 2)
         nc.vector.tensor_copy(v2_rows[:], tab2_s[:].indirect(idx2[:]))
+        nc.vector.tensor_copy(v1_rows[1][:], tab1_s[:].indirect(halves1[1]))
 
         w2_rows = w2.rearrange("(p i) (b c) -> b p i c", i=4, b=2)
         w2_early_raw = load(placed_tile([P, 4, BANK], F32, "w2_early_raw", W2_EARLY_RAW_AT), w2_rows[0])
-        to_quadrants(nc.sync, v2_plane, v2_rows[translucent_rows, :])
-        tab2_w = load(placed_tile([P, T], I32, "tab2_w", TAB2_WORDS_AT), words_of(tab2_words))
+        v1_planes, w1_plane = (carried_planes[:, 0:BANK], carried_planes[:, 2 * BANK :]), carried_planes[:, BANK : 2 * BANK]
+        to_quadrants(nc.sync, v1_planes[1], v1_rows[1][opaque_rows, :])
 
         def gather_words(table, idx, name):
             halves = []
@@ -158,14 +161,17 @@ def tile_list_deferred_tile_shading_kernel(
 
         v1_codes = gather_words(tab1_w, idx1, "v1_codes")
 
-        w3_plane = placed_tile([P, BANK], U8, "w3_plane", AFTER_TAB1_AT)
-        nc.gpsimd.memset(w3_plane[:].bitcast(I32), 0)
+        tab2_w = load(placed_tile([P, T], I32, "tab2_w", TAB2_WORDS_AT), words_of(tab2_words))
+        translucent_planes = placed_tile([P, S + BANK], U8, "translucent_planes", AFTER_TAB1_AT)
+        nc.gpsimd.memset(translucent_planes[:].bitcast(I32), 0)
         nc.gpsimd.memset(late_planes[:].bitcast(I32), 0)
+        v2_plane, w3_plane = translucent_planes[:, 0:S], translucent_planes[:, S:]
+        to_quadrants(nc.sync, v2_plane, v2_rows[translucent_rows, :])
         to_quadrants(nc.sync, w3_plane, w3_scales[0, :, 0:BANK])
 
         identity = {}
         for dtype, name, at in ((F32, "identity_words", 0), (BF16, "identity_values", HALF)):
-            identity.setdefault(dtype, placed_tile([P, P], dtype, name, AFTER_TAB1_AT + KIB + HALF + at))
+            identity.setdefault(dtype, placed_tile([P, P], dtype, name, AFTER_TAB1_AT + 2 * KIB + HALF + at))
             make_identity(nc, identity[dtype][:])
 
         def deal_columns(dealt, raw):
@@ -190,7 +196,7 @@ def tile_list_deferred_tile_shading_kernel(
         def rectify(s, lo, hi, dst):
             h = lo // BANK
             acc = product(page_columns(w1_words_sb, late.get("w1_codes"), s, 2 * P), page_columns(w1_plane, late.get("w1_plane"), s, P),
-                          FP4X4, v1_codes[h][:, lo - h * BANK : hi - h * BANK], v1_plane[:, lo:hi], hi - lo)
+                          FP4X4, v1_codes[h][:, lo - h * BANK : hi - h * BANK], v1_planes[h][:, lo - h * BANK : hi - h * BANK], hi - lo)
             nc.scalar.activation(dst, acc, ACT.Relu)
 
         def opaque_layer(s, squared):
@@ -214,8 +220,9 @@ def tile_list_deferred_tile_shading_kernel(
         new_page(0)
         for i, (lo, hi) in enumerate(FIRST_PIECES):
             squared = placed_tile([P, hi - lo], F32, "first_squared%d" % i, FIRST_SQUARED_AT[i])
-            rectify(0, lo, hi, squared[:])
-            nc.scalar.activation(squared[:], squared[:], ACT.Square)
+            rectified = placed_tile([P, hi - lo], F32, "last_rectified", LAST_RECTIFIED_AT) if hi == S else squared
+            rectify(0, lo, hi, rectified[:])
+            nc.scalar.activation(squared[:], rectified[:], ACT.Square)
             nc.vector.tensor_tensor(pages[0][:].indirect(idx3[:, lo // 16 : hi // 16]), squared[:], opaque_exposure[:, lo:hi], MULT)
 
         w3_early_codes = load(placed_tile([P, BANK], I32, "w3_early_codes", W3_EARLY_CODES_AT), words_of(w3_words)[:, 0:BANK])
@@ -398,7 +405,7 @@ def tile_list_deferred_tile_shading_kernel(
         nc.scalar.copy(
             w2_late_rounded[:].rearrange("p (t a b i) -> p t a b i", t=4, b=4, i=4),
             w2_late_raw[:].rearrange("p i (a t b) -> p t a b i", t=4, b=4))
-        w2_late = quantised(placed_tile([P, BANK], U32, "w2_late_codes", SECOND_TRANSLUCENT_AT), "w2_late_plane", w2_late_rounded[:])
+        w2_late = quantised(new_tile([P, BANK], U32, "w2_late_codes"), "w2_late_plane", w2_late_rounded[:])
         late.setdefault("w2_codes", w2_late[0])
         late.setdefault("w2_plane", w2_late[1])
         layers(2)
@@ -447,7 +454,7 @@ def tile_list_deferred_tile_shading_kernel(
             if b == 0:
                 plane = placed_tile([P, BANK], U8, "z_plane0_%d" % c, MIX_AT[0] + c * 2 * KIB)
             else:
-                plane = placed_tile([P, BANK], U8, "z_plane1_%d" % c, STAGE_AT + 3 * KIB + HALF + c * HALF)
+                plane = placed_tile([P, BANK], U8, "z_plane1_%d" % c, AFTER_TAB1_AT + 5 * KIB + HALF + c * HALF)
             nc.vector.quantize_mx(out=codes[:].bitcast(FP8X4), scales=plane[:], in_=woven[b, c][:])
             for half in range(2):
                 if b == 0:
@@ -466,7 +473,7 @@ def tile_list_deferred_tile_shading_kernel(
             nc.sync.dma_start(out[half * P : (half + 1) * P, c * BANK : (c + 1) * BANK], result[:])
 
         last_row(0)
-        w4_codes = placed_tile([P, 2 * N], U32, "w4_codes", STAGE_AT + KIB + HALF)
+        w4_codes = placed_tile([P, 2 * N], U32, "w4_codes", AFTER_TAB1_AT + 3 * KIB + HALF)
         w4_plane = placed_tile([P, 2 * N], U8, "w4_plane", LAST_SOURCES_AT + 2 * KIB)
         nc.vector.quantize_mx(out=w4_codes[:].bitcast(FP8X4), scales=w4_plane[:], in_=w4_rounded[:].rearrange("p b x -> p (b x)"))
         for c in range(CHUNKS):

@@ -126,7 +126,6 @@ def tile_list_deferred_tile_shading_kernel(
         w1_words_sb = new_tile([P, 2 * H], U8, "w1_words_sb")
         nc.sync.dma_start(w1_words_sb[:].bitcast(I32), w1_words[0].bitcast(I32))
         idx4 = load_list(offs4, "idx4")
-        opaque_exposure = load(new_tile([P, S], F32, "opaque_exposure"), wg1)
 
         table_warm_up = new_tile([P, 2], F32, "table_warm_up")
         nc.gpsimd.memset(table_warm_up[:, 0:1], 0.0)
@@ -145,12 +144,13 @@ def tile_list_deferred_tile_shading_kernel(
         to_quadrants(nc.scalar, carried_planes[:, 0 : 2 * BANK], stage[opaque_rows, :])
         v2_rows = placed_tile([P, S], U8, "v2_rows", GATHERED_ROWS_AT + HALF // 2)
         nc.vector.tensor_copy(v2_rows[:], tab2_s[:].indirect(idx2[:]))
+        opaque_exposure = load(placed_tile([P, S], F32, "opaque_exposure", PAIRS_AT + 3 * KIB + HALF), wg1)
         nc.vector.tensor_copy(v1_rows[1][:], tab1_s[:].indirect(halves1[1]))
+        v1_planes, w1_plane = (carried_planes[:, 0:BANK], carried_planes[:, 2 * BANK :]), carried_planes[:, BANK : 2 * BANK]
+        to_quadrants(nc.sync, v1_planes[1], v1_rows[1][opaque_rows, :])
 
         w2_rows = w2.rearrange("(p i) (b c) -> b p i c", i=4, b=2)
         w2_early_raw = load(placed_tile([P, 4, BANK], F32, "w2_early_raw", W2_EARLY_RAW_AT), w2_rows[0])
-        v1_planes, w1_plane = (carried_planes[:, 0:BANK], carried_planes[:, 2 * BANK :]), carried_planes[:, BANK : 2 * BANK]
-        to_quadrants(nc.sync, v1_planes[1], v1_rows[1][opaque_rows, :])
 
         def gather_words(table, idx, name):
             halves = []

@@ -30,38 +30,46 @@ OPAQUE_ROWS_FROM = 112
 TRANSLUCENT_ROWS_FROM = 48
 FIRST_PIECES = ((0, 256), (256, 512), (512, 1024))
 
-AFTER_TAB1_AT = 0
-TAB1_WORDS_AT = AFTER_TAB1_AT
-PAGE_AT = (191 * KIB, 8 * KIB, 54 * KIB + HALF)
-W2_EARLY_CODES_AT = PAGE_AT[1] + 8 * KIB
-TAB2_WORDS_AT = W2_EARLY_CODES_AT - HALF
-MIX_AT = (18 * KIB, 26 * KIB, 42 * KIB + HALF)
-ACTIVATIONS_AT = (183 * KIB, 34 * KIB)
-W2_EARLY_RAW_AT = ACTIVATIONS_AT[1]
-TAB1_ROWS_AT = W2_EARLY_RAW_AT + 8 * KIB - HALF
-SECOND_OPAQUE_AT = MIX_AT[2] + 4 * KIB
-SECOND_TRANSLUCENT_AT = MIX_AT[2] + 8 * KIB
-ROWS_AT = PAGE_AT[2] + 8 * KIB
-Z_AT = (ROWS_AT, ROWS_AT + 6 * KIB, ROWS_AT + 12 * KIB, ROWS_AT + 16 * KIB)
-COLOUR_AT = (SECOND_TRANSLUCENT_AT - 2 * KIB, ROWS_AT + 2 * KIB, ROWS_AT + 8 * KIB, Z_AT[2], Z_AT[3])
-W2_LATE_ROUNDED_AT = ROWS_AT + 4 * KIB
-RESULTS_AT = ROWS_AT
-PAIRS_AT = ROWS_AT + 20 * KIB
-GATHERED_ROWS_AT = PAIRS_AT + 8 * KIB
-WOVEN_AT = (PAIRS_AT + 16 * KIB, PAIRS_AT + 32 * KIB)
-TURNED_AT = WOVEN_AT[1]
-STAGE_AT = TURNED_AT
-FIRST_OPAQUE_AT = WOVEN_AT[0] + 7 * KIB
-EARLY_EXPOSURES_AT = 199 * KIB
-LAST_RECTIFIED_AT = EARLY_EXPOSURES_AT + 7 * KIB
-W2_EARLY_ROUNDED_AT = LAST_RECTIFIED_AT + KIB
-W3_EARLY_CODES_AT = W2_EARLY_ROUNDED_AT + 4 * KIB
-FIRST_SQUARED_AT = (STAGE_AT + 2 * KIB, W3_EARLY_CODES_AT, FIRST_OPAQUE_AT)
-FIRST_TRANSLUCENT_AT = 163 * KIB
-EXPOSURES_AT = FIRST_TRANSLUCENT_AT + HALF - 32 * KIB
-LATE_ROWS_AT = 171 * KIB
-LAST_SOURCES_AT = 179 * KIB
-Z_CODES_AT = (PAGE_AT[2], MIX_AT[2])
+PAGE_AT = tuple(KIB * at for at in (0, 36, 24, 16, 8, 44, 52, 60))
+FIRST_TRANSLUCENT_AT = 32 * KIB
+W2_LATE_ROUNDED_AT = 30 * KIB
+TAB1_WORDS_AT = 57 * KIB
+TAB2_WORDS_AT = TAB1_WORDS_AT + HALF - 16 * KIB
+W2_LATE_RAW_AT = TAB1_WORDS_AT + HALF
+THIRD_SQUARED_AT = W2_LATE_RAW_AT
+LATE_SCALE_ROWS_AT = W2_LATE_RAW_AT + 8 * KIB
+W3_LATE_WORDS_AT = 45 * KIB
+W2_EARLY_PLANE_AT = PAGE_AT[6]
+TRANSLUCENT_PLANES_AT = 68 * KIB
+LATE_PLANES_AT = TRANSLUCENT_PLANES_AT + KIB + HALF
+W3_EARLY_CODES_AT = LATE_PLANES_AT + KIB
+TRANSLUCENT_EXPOSURE_AT = W3_EARLY_CODES_AT + 2 * KIB
+SOURCES_AT = {1: 77 * KIB, 2: 81 * KIB, 4: 89 * KIB, 6: 97 * KIB}
+RECTIFIED_AT = {0: 92 * KIB + HALF, 2: 93 * KIB}
+W2_EARLY_ROUNDED_AT = 94 * KIB
+W4_RAW_AT = SOURCES_AT[6]
+GATES_AT = (105 * KIB, 113 * KIB)
+FIRST_OPAQUE_AT = 121 * KIB
+FIRST_SQUARED_AT = (FIRST_OPAQUE_AT + 2 * KIB, FIRST_OPAQUE_AT + 3 * KIB, FIRST_OPAQUE_AT)
+SECOND_SQUARED_AT = 125 * KIB
+LATE_SQUARED_AT = {4: 133 * KIB, 6: FIRST_OPAQUE_AT}
+LATE_ROWS_AT = FIRST_OPAQUE_AT
+Z_AT = (133 * KIB, 137 * KIB)
+OPAQUE_EXPOSURE_AT = 141 * KIB
+TAB1_ROWS_AT = OPAQUE_EXPOSURE_AT + HALF - 4 * KIB
+LATE_EXPOSURES_AT = {4: 145 * KIB, 6: 153 * KIB}
+W2_EARLY_RAW_AT = LATE_EXPOSURES_AT[4] + HALF
+TAB2_ROWS_AT = LATE_EXPOSURES_AT[6]
+GATHERED_ROWS_AT = 161 * KIB
+STAGE_AT = GATHERED_ROWS_AT + HALF
+TURNED_AT = 165 * KIB
+WOVEN_AT = (181 * KIB, PAGE_AT[0])
+W4_ROUNDED_AT = 197 * KIB
+MIX_AT = (LATE_EXPOSURES_AT[4], GATES_AT[1], LATE_EXPOSURES_AT[6], GATES_AT[0], LATE_EXPOSURES_AT[4], GATES_AT[1])
+LAST_MIX_AT = LATE_EXPOSURES_AT[6]
+PAIRS_AT = TURNED_AT
+Z_CODES_AT = (PAGE_AT[3], PAGE_AT[2])
+RESULTS_AT = PAGE_AT[1]
 OPAQUE_BANKS = (0, 1)
 TRANSLUCENT_BANKS = (2, 3, 4, 5, 5, 4, 3, 2)
 TURN_BANKS = (6, 7)
@@ -97,6 +105,9 @@ def tile_list_deferred_tile_shading_kernel(
             nc.sync.dma_start(dst[:], src)
             return dst
 
+        def entries(idx, lo, hi):
+            return idx[:, lo // 16 : hi // 16]
+
         def words_of(src):
             return src[0].rearrange("p n i -> p (n i)").bitcast(I32)
 
@@ -114,7 +125,7 @@ def tile_list_deferred_tile_shading_kernel(
         opaque_rows = slice(OPAQUE_ROWS_FROM, OPAQUE_ROWS_FROM + SCALE_ROWS)
         translucent_rows = slice(TRANSLUCENT_ROWS_FROM, TRANSLUCENT_ROWS_FROM + SCALE_ROWS)
         tab1_s = placed_tile([P, T], U8, "tab1_s", TAB1_ROWS_AT)
-        tab2_s = placed_tile([P, T], U8, "tab2_s", PAIRS_AT)
+        tab2_s = placed_tile([P, T], U8, "tab2_s", TAB2_ROWS_AT)
         stage = placed_tile([P, 2 * BANK], U8, "stage", STAGE_AT)
         nc.scalar.dma_start(tab1_s[opaque_rows, :].bitcast(I32), tab_scales[0].bitcast(I32))
         nc.scalar.dma_start(tab2_s[translucent_rows, :].bitcast(I32), tab2_scales[0].bitcast(I32))
@@ -134,45 +145,40 @@ def tile_list_deferred_tile_shading_kernel(
         nc.gpsimd.memset(carried_planes[:].bitcast(I32), 0)
         nc.gpsimd.memset(tab2_s[0 : translucent_rows.start, :].bitcast(I32), 0)
         nc.gpsimd.memset(tab2_s[translucent_rows.stop :, :].bitcast(I32), 0)
-        late_planes = placed_tile([P, 2 * BANK], U8, "late_planes", AFTER_TAB1_AT + KIB + HALF)
         nc.scalar.activation(table_warm_up[:, 1:2], table_warm_up[:, 0:1], ACT.Sigmoid)
 
-        halves1 = [idx1[:, h * BANK // 16 : (h + 1) * BANK // 16] for h in range(2)]
-        v1_rows = [placed_tile([P, BANK], U8, "v1_rows%d" % h, GATHERED_ROWS_AT - h * HALF // 2) for h in range(2)]
-        nc.vector.tensor_copy(v1_rows[0][:], tab1_s[:].indirect(halves1[0]))
+        v1_rows = [placed_tile([P, BANK], U8, "v1_rows%d" % h, GATHERED_ROWS_AT + h * 3 * HALF) for h in range(2)]
+        nc.vector.tensor_copy(v1_rows[0][:], tab1_s[:].indirect(entries(idx1, 0, BANK)))
         nc.vector.tensor_copy(stage[96:, 0:BANK].bitcast(I32), v1_rows[0][96:, :].bitcast(I32))
         to_quadrants(nc.scalar, carried_planes[:, 0 : 2 * BANK], stage[opaque_rows, :])
-        v2_rows = placed_tile([P, S], U8, "v2_rows", GATHERED_ROWS_AT + HALF // 2)
-        nc.vector.tensor_copy(v2_rows[:], tab2_s[:].indirect(idx2[:]))
-        opaque_exposure = load(placed_tile([P, S], F32, "opaque_exposure", PAIRS_AT + 3 * KIB + HALF), wg1)
-        nc.vector.tensor_copy(v1_rows[1][:], tab1_s[:].indirect(halves1[1]))
+        nc.vector.tensor_copy(v1_rows[1][:], tab1_s[:].indirect(entries(idx1, BANK, S)))
+        opaque_exposure = load(placed_tile([P, S], F32, "opaque_exposure", OPAQUE_EXPOSURE_AT), wg1)
         v1_planes, w1_plane = (carried_planes[:, 0:BANK], carried_planes[:, 2 * BANK :]), carried_planes[:, BANK : 2 * BANK]
         to_quadrants(nc.sync, v1_planes[1], v1_rows[1][opaque_rows, :])
+        v2_rows = new_tile([P, S], U8, "v2_rows")
+        nc.vector.tensor_copy(v2_rows[:], tab2_s[:].indirect(idx2[:]))
 
         w2_rows = w2.rearrange("(p i) (b c) -> b p i c", i=4, b=2)
         w2_early_raw = load(placed_tile([P, 4, BANK], F32, "w2_early_raw", W2_EARLY_RAW_AT), w2_rows[0])
 
-        def gather_words(table, idx, name):
-            halves = []
-            for h in range(2):
-                halves.append(new_tile([P, BANK], U32, "%s%d" % (name, h)))
-                nc.vector.tensor_copy(halves[h][:], table[:].bitcast(U32).indirect(idx[:, h * BANK // 16 : (h + 1) * BANK // 16]))
-            return halves
-
-        v1_codes = gather_words(tab1_w, idx1, "v1_codes")
+        v1_codes = new_tile([P, S], U32, "v1_codes")
+        for lo, hi in FIRST_PIECES:
+            nc.vector.tensor_copy(v1_codes[:, lo:hi], tab1_w[:].bitcast(U32).indirect(entries(idx1, lo, hi)))
 
         tab2_w = load(placed_tile([P, T], I32, "tab2_w", TAB2_WORDS_AT), words_of(tab2_words))
-        translucent_planes = placed_tile([P, S + BANK], U8, "translucent_planes", AFTER_TAB1_AT)
+        w2_late_raw = load(placed_tile([P, 4, BANK], F32, "w2_late_raw", W2_LATE_RAW_AT), w2_rows[1])
+        translucent_planes = placed_tile([P, S + BANK], U8, "translucent_planes", TRANSLUCENT_PLANES_AT)
+        late_planes = placed_tile([P, 2 * BANK], U8, "late_planes", LATE_PLANES_AT)
         nc.gpsimd.memset(translucent_planes[:].bitcast(I32), 0)
         nc.gpsimd.memset(late_planes[:].bitcast(I32), 0)
         v2_plane, w3_plane = translucent_planes[:, 0:S], translucent_planes[:, S:]
         to_quadrants(nc.sync, v2_plane, v2_rows[translucent_rows, :])
         to_quadrants(nc.sync, w3_plane, w3_scales[0, :, 0:BANK])
-
-        identity = {}
-        for dtype, name, at in ((F32, "identity_words", 0), (BF16, "identity_values", HALF)):
-            identity.setdefault(dtype, placed_tile([P, P], dtype, name, AFTER_TAB1_AT + 2 * KIB + HALF + at))
-            make_identity(nc, identity[dtype][:])
+        w3_early_codes = load(placed_tile([P, BANK], I32, "w3_early_codes", W3_EARLY_CODES_AT), words_of(w3_words)[:, 0:BANK])
+        translucent_exposure = load(placed_tile([P, S], F32, "translucent_exposure", TRANSLUCENT_EXPOSURE_AT), wg2)
+        late_scale_rows = placed_tile([P, 2, BANK], U8, "late_scale_rows", LATE_SCALE_ROWS_AT)
+        to_quadrants(nc.sync, late_scale_rows[:, 0], w1_scales[0, :, BANK:])
+        to_quadrants(nc.sync, late_scale_rows[:, 1], w3_scales[0, :, BANK:])
 
         def deal_columns(dealt, raw):
             nc.scalar.copy(
@@ -196,7 +202,7 @@ def tile_list_deferred_tile_shading_kernel(
         def rectify(s, lo, hi, dst):
             h = lo // BANK
             acc = product(page_columns(w1_words_sb, late.get("w1_codes"), s, 2 * P), page_columns(w1_plane, late.get("w1_plane"), s, P),
-                          FP4X4, v1_codes[h][:, lo - h * BANK : hi - h * BANK], v1_planes[h][:, lo - h * BANK : hi - h * BANK], hi - lo)
+                          FP4X4, v1_codes[:, lo:hi], v1_planes[h][:, lo - h * BANK : hi - h * BANK], hi - lo)
             nc.scalar.activation(dst, acc, ACT.Relu)
 
         def opaque_layer(s, squared):
@@ -204,159 +210,141 @@ def tile_list_deferred_tile_shading_kernel(
                 rectify(s, h * BANK, (h + 1) * BANK, squared[:, h * BANK : (h + 1) * BANK])
             nc.scalar.activation(squared, squared, ACT.Square)
 
-        activations = {}
-
-        def activation_pair(j):
-            if j not in activations:
-                activations.setdefault(j, placed_tile([P, 2, S], F32, "activations%d" % j, ACTIVATIONS_AT[j % 2]))
-            return activations[j]
-
         pages = {}
 
-        def new_page(s):
-            pages.setdefault(s, placed_tile([P, T2], F32, "page%d" % s, PAGE_AT[s % 3]))
-            return pages[s]
+        def put_opaque(s, values):
+            pages.setdefault(s, placed_tile([P, T2], F32, "page%d" % s, PAGE_AT[s]))
+            nc.vector.tensor_copy(pages[s][:].indirect(idx3[:]), values)
 
-        new_page(0)
+        def put_translucent(s, values):
+            nc.vector.tensor_copy(pages[s][:].indirect(idx4[:]), values)
+
+        pages.setdefault(0, placed_tile([P, T2], F32, "page0", PAGE_AT[0]))
         for i, (lo, hi) in enumerate(FIRST_PIECES):
             squared = placed_tile([P, hi - lo], F32, "first_squared%d" % i, FIRST_SQUARED_AT[i])
-            rectified = placed_tile([P, hi - lo], F32, "last_rectified", LAST_RECTIFIED_AT) if hi == S else squared
+            rectified = placed_tile([P, hi - lo], F32, "rectified%d" % i, RECTIFIED_AT[i]) if i in RECTIFIED_AT else squared
             rectify(0, lo, hi, rectified[:])
             nc.scalar.activation(squared[:], rectified[:], ACT.Square)
-            nc.vector.tensor_tensor(pages[0][:].indirect(idx3[:, lo // 16 : hi // 16]), squared[:], opaque_exposure[:, lo:hi], MULT)
-
-        w3_early_codes = load(placed_tile([P, BANK], I32, "w3_early_codes", W3_EARLY_CODES_AT), words_of(w3_words)[:, 0:BANK])
-        early_exposures = placed_tile([P, 2, S], F32, "early_exposures", EARLY_EXPOSURES_AT)
-        nc.sync.dma_start(early_exposures[:, 1], wg2)
+            nc.vector.tensor_tensor(pages[0][:].indirect(entries(idx3, lo, hi)), squared[:], opaque_exposure[:, lo:hi], MULT)
 
         def round_rows(rounded, raw):
             nc.scalar.copy(
                 rounded.rearrange("p (n i t) -> p n t i", i=4, t=4), raw.rearrange("p t (n i) -> p n t i", i=4))
 
-        def quantised(codes, name, rounded):
-            plane = new_tile([P, BANK], U8, name)
+        def quantised(name, plane, rounded):
+            codes = new_tile([P, BANK], U32, name)
             nc.vector.quantize_mx(out=codes[:].bitcast(FP8X4), scales=plane[:], in_=rounded)
             return codes, plane
 
-        w2_early_rounded = placed_tile([P, 4 * BANK], BF16, "w2_early_rounded", W2_EARLY_ROUNDED_AT)
-        opaque_layer(1, activation_pair(0)[:, 0])
-        round_rows(w2_early_rounded[:], w2_early_raw[:])
-        late.setdefault("w1_codes", deal_columns(new_tile([P, H], U8, "w1_late_codes")[:], w1_words_sb[:, H:]))
-        nc.scalar.copy(early_exposures[:, 0], opaque_exposure[:])
-        v2_codes = gather_words(tab2_w, idx2, "v2_codes")
-        w2_early_codes, w2_early_plane = quantised(
-            placed_tile([P, BANK], U32, "w2_early_codes", W2_EARLY_CODES_AT), "w2_early_plane", w2_early_rounded[:])
-        opaque1 = placed_tile([P, S], F32, "opaque1", FIRST_OPAQUE_AT)
-        nc.gpsimd.tensor_tensor(opaque1[:], activations[0][:, 0], opaque_exposure[:], MULT)
-        nc.vector.tensor_copy(new_page(1)[:].indirect(idx3[:]), opaque1[:])
-
-        late_rows = placed_tile([P, 2 * T2], BF16, "late_rows", LATE_ROWS_AT)
-        pairs = placed_tile([P, 2, T2, 2], BF16, "pairs", PAIRS_AT)
-        last_pairs = pairs[:, 1].rearrange("p m e -> p (m e)").bitcast(F32)
-        mix_tiles = {}
-
-        def load_mix(s):
-            src = mix[s * P : (s + 1) * P, :].unsqueeze(0) if s < EARLY else dealt_rows(mix[K:, :], s - EARLY)
-            if s + 1 < PAGES:
-                rows = last_pairs if s + 2 == PAGES else placed_tile([P, T2], F32, "mix%d" % s, MIX_AT[s % 3])[:]
-                nc.sync.dma_start(rows, src)
-            else:
-                rows = [
-                    load(placed_tile([P, BANK], F32, "last_mix%d" % c, MIX_AT[0] + c * 2 * KIB), src[:, :, c * BANK : (c + 1) * BANK])
-                    for c in range(CHUNKS)]
-            mix_tiles.setdefault(s, rows)
-
-        w2_late_raw = load(placed_tile([P, 4, BANK], F32, "w2_late_raw", WOVEN_AT[0]), w2_rows[1])
-        load_mix(0)
-        load_mix(1)
-        w4_raw = placed_tile([P, 2, 4, N], F32, "w4_raw", WOVEN_AT[0] + 8 * KIB)
-        nc.sync.dma_start(w4_raw[:, 0].rearrange("p t n -> p (t n)"), w4[0:K, :].rearrange("(p t) n -> p (t n)", t=4))
-        for t in range(4):
-            nc.sync.dma_start(w4_raw[:, 1, t], dealt_rows(w4[K:, :], t))
-        late_exposures = placed_tile([P, 8, S], F32, "late_exposures", EXPOSURES_AT)
-
-        def load_exposure(dst, src, t):
-            for q in QUADRANTS:
-                nc.sync.dma_start(dst[32 * q : 32 * q + 32], dealt_rows(src, t))
-
-
-        colours = {}
-
-        def z_row(s):
-            if s < EARLY:
-                return placed_tile([P, T2], BF16, "z%d" % s, Z_AT[s])[:]
-            if s < EARLY + 2:
-                return late_rows[:, (s - EARLY) * T2 : (s - EARLY + 1) * T2]
-            return pairs[:, 1, :, s - EARLY - 2]
-
-        def colour_halves(s):
-            if s == PAGES - 1:
-                return [z_row(s - 2).bitcast(F32)[:, 0:BANK], last_pairs[:, 0:BANK]]
-            if s == EARLY + 1:
-                whole = z_row(s - 1).bitcast(F32)
-            else:
-                whole = placed_tile([P, S], F32, "colour%d" % s, LAST_SOURCES_AT if s == PAGES - 2 else COLOUR_AT[s])[:]
-            colours.setdefault(s, whole)
-            return [whole[:, h * BANK : (h + 1) * BANK] for h in range(2)]
-
-        def translucent_layer(s):
-            gate = activation_pair(s)[:, 1]
-            colour = colour_halves(s)
+        def translucent_layer(s, colour, gate):
             for h in range(2):
                 cols = slice(h * BANK, (h + 1) * BANK)
                 acc = product(page_columns(w2_early_codes, late.get("w2_codes"), s, P), page_columns(w2_early_plane, late.get("w2_plane"), s, P),
-                              FP8X4, v2_codes[h][:], v2_plane[:, cols])
-                nc.scalar.copy(colour[h], acc)
+                              FP8X4, v2_codes[:, cols], v2_plane[:, cols])
+                nc.scalar.copy(colour[:, cols], acc)
             for h in range(2):
                 cols = slice(h * BANK, (h + 1) * BANK)
                 acc = product(page_columns(w3_early_codes, late.get("w3_codes"), s, P), page_columns(w3_plane, late.get("w3_plane"), s, P),
-                              FP8X4, v2_codes[h][:], v2_plane[:, cols])
+                              FP8X4, v2_codes[:, cols], v2_plane[:, cols])
                 nc.scalar.activation(gate[:, cols], acc, ACT.Sigmoid)
-            colours.setdefault(s, colour)
 
-        def expose(j):
-            opaque = None
-            if j == 0:
-                translucent = placed_tile([P, S], F32, "sources0", FIRST_TRANSLUCENT_AT)[:]
-                for h in range(2):
-                    cols = slice(h * BANK, (h + 1) * BANK)
-                    nc.gpsimd.tensor_tensor(translucent[:, cols], colours[0][:, cols], early_exposures[:, 1, cols], MULT)
-                for h in range(2):
-                    cols = slice(h * BANK, (h + 1) * BANK)
-                    nc.gpsimd.tensor_tensor(translucent[:, cols], translucent[:, cols], activations[0][:, 1, cols], MULT)
-                    nc.vector.tensor_copy(
-                        pages[0][:].indirect(idx4[:, h * BANK // 16 : (h + 1) * BANK // 16]), translucent[:, cols])
-                return opaque, translucent
-            if j == PAGES - 1:
-                translucent = placed_tile([P, S], F32, "sources%d" % j, LAST_SOURCES_AT)[:]
-                nc.gpsimd.tensor_tensor(translucent, activations[j][:, 1], late_exposures[:, 7], MULT)
-            else:
-                vals = placed_tile([P, 2, S], F32, "sources%d" % j, SECOND_OPAQUE_AT if j == 1 else MIX_AT[(j + 1) % 3])
-                if j + 1 == EARLY:
-                    nc.gpsimd.tensor_tensor(vals[:, 1], activations[j][:, 1], early_exposures[:, 1], MULT)
-                    nc.gpsimd.tensor_tensor(vals[:, 0], activations[j][:, 0], late_exposures[:, 0], MULT)
-                else:
-                    exposures = early_exposures[:] if j < EARLY else late_exposures[:, j - EARLY + 1 : j - EARLY + 5 : 3]
-                    nc.gpsimd.tensor_tensor(vals[:], activations[j][:], exposures, MULT)
-                opaque, translucent = vals[:, 0], vals[:, 1]
-            if j + 1 < PAGES:
-                nc.gpsimd.tensor_tensor(translucent, translucent, colours[j], MULT)
-            else:
-                for h in range(2):
-                    cols = slice(h * BANK, (h + 1) * BANK)
-                    nc.gpsimd.tensor_tensor(translucent[:, cols], translucent[:, cols], colours[j][h], MULT)
-            return opaque, translucent
+        def late_exposures(src, s, name):
+            dst = placed_tile([P, 2, S], F32, "%s%d" % (name, s), LATE_EXPOSURES_AT[s])
+            for u in range(2):
+                for q in QUADRANTS:
+                    nc.sync.dma_start(dst[32 * q : 32 * q + 32, u], dealt_rows(src, s - EARLY + u))
+            return dst
 
-        def scatter(j, sources):
-            opaque, translucent = sources
-            if opaque is not None:
-                nc.vector.tensor_copy(new_page(j + 1)[:].indirect(idx3[:]), opaque)
-            nc.vector.tensor_copy(pages[j][:].indirect(idx4[:]), translucent)
+        w2_early_rounded = placed_tile([P, 4 * BANK], BF16, "w2_early_rounded", W2_EARLY_ROUNDED_AT)
+        squared1 = placed_tile([P, S], F32, "squared1", GATHERED_ROWS_AT)
+        opaque_layer(1, squared1[:])
+        round_rows(w2_early_rounded[:], w2_early_raw[:])
+        v2_codes = new_tile([P, S], U32, "v2_codes")
+        nc.vector.tensor_copy(v2_codes[:], tab2_w[:].bitcast(U32).indirect(idx2[:]))
+        w2_early_codes, w2_early_plane = quantised(
+            "w2_early_codes", placed_tile([P, BANK], U8, "w2_early_plane", W2_EARLY_PLANE_AT), w2_early_rounded[:])
+        opaque1 = placed_tile([P, S], F32, "opaque1", FIRST_OPAQUE_AT)
+        nc.gpsimd.tensor_tensor(opaque1[:], squared1[:], opaque_exposure[:], MULT)
+        put_opaque(1, opaque1[:])
 
-        def layers(j):
-            if j + 1 < PAGES:
-                opaque_layer(j + 1, activation_pair(j)[:, 0])
-            translucent_layer(j)
+        late_opaque_exposures = {s: late_exposures(wg1, s, "opaque_exposures") for s in (4, 6)}
+        w3_late_words = load(placed_tile([P, BANK], I32, "w3_late_words", W3_LATE_WORDS_AT), words_of(w3_words)[:, BANK:])
+        w4_raw = placed_tile([P, 2, 4, N], F32, "w4_raw", W4_RAW_AT)
+        nc.sync.dma_start(w4_raw[:, 0].rearrange("p t n -> p (t n)"), w4[0:K, :].rearrange("(p t) n -> p (t n)", t=4))
+        for t in range(4):
+            nc.sync.dma_start(w4_raw[:, 1, t], dealt_rows(w4[K:, :], t))
+
+        def early_opaque_source(s, at):
+            squared = placed_tile([P, S], F32, "squared%d" % s, at)
+            opaque_layer(s, squared[:])
+            nc.gpsimd.tensor_tensor(squared[:], squared[:], opaque_exposure[:], MULT)
+            return squared
+
+        opaque2 = early_opaque_source(2, SECOND_SQUARED_AT)
+        identity = {}
+        for dtype, name, at in ((F32, "identity_words", GATHERED_ROWS_AT), (BF16, "identity_values", GATHERED_ROWS_AT + HALF)):
+            identity.setdefault(dtype, placed_tile([P, P], dtype, name, at))
+            make_identity(nc, identity[dtype][:])
+
+        w2_late_rounded = placed_tile([P, 4 * BANK], BF16, "w2_late_rounded", W2_LATE_ROUNDED_AT)
+        nc.scalar.copy(
+            w2_late_rounded[:].rearrange("p (t a b i) -> p t a b i", t=4, b=4, i=4),
+            w2_late_raw[:].rearrange("p i (a t b) -> p t a b i", t=4, b=4))
+        w2_late = quantised("w2_late_codes", new_tile([P, BANK], U8, "w2_late_plane"), w2_late_rounded[:])
+        late.setdefault("w2_codes", w2_late[0])
+        late.setdefault("w2_plane", w2_late[1])
+        put_opaque(2, opaque2[:])
+
+        first = placed_tile([P, 2, S], F32, "colour_and_gate0", GATES_AT[0])
+        translucent_layer(0, first[:, 0], first[:, 1])
+        translucent0 = placed_tile([P, S], F32, "translucent0", FIRST_TRANSLUCENT_AT)
+        nc.gpsimd.tensor_tensor(first[:, 0], first[:, 0], translucent_exposure[:], MULT)
+        nc.gpsimd.tensor_tensor(translucent0[:], first[:, 0], first[:, 1], MULT)
+        put_opaque(3, early_opaque_source(3, THIRD_SQUARED_AT)[:])
+        put_translucent(0, translucent0[:])
+
+        def translucent_sources(s, count, exposures):
+            colours = placed_tile([P, count, S], F32, "colours%d" % s, SOURCES_AT[s])
+            gates = placed_tile([P, count, S], F32, "gates%d" % s, GATES_AT[(s // 2 + 1) % 2])
+            for u in range(count):
+                translucent_layer(s + u, colours[:, u], gates[:, u])
+            nc.gpsimd.tensor_tensor(colours[:], colours[:], exposures, MULT)
+            nc.gpsimd.tensor_tensor(colours[:], colours[:], gates[:], MULT)
+            for u in range(count):
+                put_translucent(s + u, colours[:, u])
+
+        def late_opaque_pair(s):
+            squared = placed_tile([P, 2, S], F32, "squared%d" % s, LATE_SQUARED_AT[s])
+            for u in range(2):
+                opaque_layer(s + u, squared[:, u])
+            nc.gpsimd.tensor_tensor(squared[:], squared[:], late_opaque_exposures[s][:], MULT)
+            return squared
+
+        translucent_sources(1, 1, translucent_exposure[:].unsqueeze(1))
+
+        late.setdefault("w1_codes", deal_columns(new_tile([P, H], U8, "w1_late_codes")[:], w1_words_sb[:, H:]))
+        for q in QUADRANTS:
+            live = slice(32 * q, 32 * q + 4)
+            nc.scalar.copy(
+                late_planes[live, :].bitcast(U32).rearrange("p (o t a) -> p o t a", o=2, t=4),
+                late_scale_rows[live].rearrange("p o n -> p (o n)").bitcast(U32).rearrange("p (o a t) -> p o t a", o=2, t=4))
+        late.setdefault("w1_plane", late_planes[:, 0:BANK])
+        late.setdefault("w3_plane", late_planes[:, BANK:])
+        opaque45 = late_opaque_pair(4)
+        late.setdefault("w3_codes", deal_columns(new_tile([P, BANK], I32, "w3_late_codes")[:], w3_late_words[:]))
+        for u in range(2):
+            put_opaque(4 + u, opaque45[:, u])
+        exposures45 = late_exposures(wg2, 4, "translucent_exposures")
+        translucent_sources(2, 2, translucent_exposure[:].unsqueeze(1).to_broadcast([P, 2, S]))
+        opaque67 = late_opaque_pair(6)
+        for u in range(2):
+            put_opaque(6 + u, opaque67[:, u])
+        exposures67 = late_exposures(wg2, 6, "translucent_exposures")
+        w4_rounded = placed_tile([P, 2, 4 * N], BF16, "w4_rounded", W4_ROUNDED_AT)
+        for b in range(2):
+            round_rows(w4_rounded[:, b], w4_raw[:, b])
+        translucent_sources(4, 2, exposures45[:])
+        translucent_sources(6, 2, exposures67[:])
 
         turned = [placed_tile([P, BLOCKS, 2, P], F32, "turned%d" % c, TURNED_AT + c * 4 * KIB) for c in range(CHUNKS)]
 
@@ -388,63 +376,41 @@ def tile_list_deferred_tile_shading_kernel(
                     words[:, pair * BANK : (pair + 1) * BANK].rearrange("p (k m v) -> p k m v", k=2, v=2),
                     acc[:].rearrange("p (k v m) -> p k m v", k=2, v=2))
 
-        translucent_layer(0)
-        expose(0)
-        w3_late_words = load(placed_tile([P, BANK], I32, "w3_late_words", FIRST_TRANSLUCENT_AT + KIB + HALF), words_of(w3_words)[:, BANK:])
-        late_scale_rows = placed_tile([P, 2, BANK], U8, "late_scale_rows", FIRST_TRANSLUCENT_AT + HALF)
-        to_quadrants(nc.sync, late_scale_rows[:, 0], w1_scales[0, :, BANK:])
-        to_quadrants(nc.sync, late_scale_rows[:, 1], w3_scales[0, :, BANK:])
-        load_exposure(late_exposures[:, 0], wg1, 0)
-        for t in range(3):
-            load_exposure(late_exposures[:, t + 1], wg1, t + 1)
-            load_exposure(late_exposures[:, 4 + t], wg2, t)
-        load_exposure(late_exposures[:, 7], wg2, 3)
-        layers(1)
-        scatter(1, expose(1))
-        w2_late_rounded = placed_tile([P, 4 * BANK], BF16, "w2_late_rounded", W2_LATE_ROUNDED_AT)
-        nc.scalar.copy(
-            w2_late_rounded[:].rearrange("p (t a b i) -> p t a b i", t=4, b=4, i=4),
-            w2_late_raw[:].rearrange("p i (a t b) -> p t a b i", t=4, b=4))
-        w2_late = quantised(new_tile([P, BANK], U32, "w2_late_codes"), "w2_late_plane", w2_late_rounded[:])
-        late.setdefault("w2_codes", w2_late[0])
-        late.setdefault("w2_plane", w2_late[1])
-        layers(2)
-        late.setdefault("w3_codes", deal_columns(new_tile([P, BANK], I32, "w3_late_codes")[:], w3_late_words[:]))
-        for q in QUADRANTS:
-            live = slice(32 * q, 32 * q + 4)
-            nc.scalar.copy(
-                late_planes[live, :].bitcast(U32).rearrange("p (o t a) -> p o t a", o=2, t=4),
-                late_scale_rows[live].rearrange("p o n -> p (o n)").bitcast(U32).rearrange("p (o a t) -> p o t a", o=2, t=4))
-        late.setdefault("w1_plane", late_planes[:, 0:BANK])
-        late.setdefault("w3_plane", late_planes[:, BANK:])
-        for s in range(PAGES - 1):
-            z = z_row(s)
-            nc.gpsimd.tensor_tensor(z, pages[s][:], mix_tiles[s], MULT)
-            if s + 3 < PAGES:
-                scatter(s + 2, expose(s + 2))
-                layers(s + 3)
-            if s + 4 == PAGES:
-                scatter(s + 3, expose(s + 3))
-            if s >= 1:
-                load_mix(s + 1)
-            if s < EARLY:
-                turn(s, z)
-            if s == 1:
-                w4_rounded = placed_tile([P, 2, 4 * N], BF16, "w4_rounded", FIRST_TRANSLUCENT_AT + 3 * KIB + HALF)
-                for b in range(2):
-                    round_rows(w4_rounded[:, b], w4_raw[:, b])
-            if s + 1 == EARLY:
-                for c in range(CHUNKS):
-                    turn_back(c)
-            if s == EARLY + 1:
-                nc.scalar.copy(pairs[:, 0], late_rows[:].rearrange("p (e m) -> p m e", e=2))
+        def mix_rows(s):
+            return mix[s * P : (s + 1) * P, :].unsqueeze(0) if s < EARLY else dealt_rows(mix[K:, :], s - EARLY)
+
+        def load_mix(s):
+            return load(placed_tile([P, T2], F32, "mix%d" % s, MIX_AT[s]), mix_rows(s))
+
+        mix_tiles = {s: load_mix(s) for s in range(EARLY)}
+        for s in range(EARLY):
+            z = placed_tile([P, T2], BF16, "z%d" % s, Z_AT[s % 2])
+            nc.gpsimd.tensor_tensor(z[:], pages[s][:], mix_tiles[s][:], MULT)
+            turn(s, z)
+            if s < 2:
+                mix_tiles.setdefault(EARLY + s, load_mix(EARLY + s))
+            if s == 2:
+                last_mix = [
+                    load(placed_tile([P, BANK], F32, "last_mix%d" % c, LAST_MIX_AT + c * 2 * KIB),
+                         mix_rows(PAGES - 1)[:, :, c * BANK : (c + 1) * BANK])
+                    for c in range(CHUNKS)]
+        for c in range(CHUNKS):
+            turn_back(c)
+        pairs = placed_tile([P, 2, T2, 2], BF16, "pairs", PAIRS_AT)
+        last_pairs = pairs[:, 1].rearrange("p m e -> p (m e)").bitcast(F32)
+        nc.sync.dma_start(last_pairs, mix_rows(PAGES - 2))
+        late_rows = placed_tile([P, 2 * T2], BF16, "late_rows", LATE_ROWS_AT)
+        for u in range(2):
+            nc.gpsimd.tensor_tensor(late_rows[:, u * T2 : (u + 1) * T2], pages[EARLY + u][:], mix_tiles[EARLY + u][:], MULT)
+        nc.scalar.copy(pairs[:, 0], late_rows[:].rearrange("p (e m) -> p m e", e=2))
+        nc.gpsimd.tensor_tensor(pairs[:, 1, :, 0], pages[PAGES - 2][:], last_pairs, MULT)
 
         last = PAGES - 1
         accs = {}
 
         def last_row(c):
             cols = slice(c * BANK, (c + 1) * BANK)
-            nc.vector.tensor_tensor(z_row(last)[:, cols], pages[last][:, cols], mix_tiles[last][c][:], MULT)
+            nc.vector.tensor_tensor(pairs[:, 1, cols, 1], pages[last][:, cols], last_mix[c][:], MULT)
             words = pairs[:].rearrange("p u m e -> p u (m e)").bitcast(U32)
             nc.scalar.copy(
                 woven_tile(1, c)[:].bitcast(U32).rearrange("p (m u) -> p m u", u=2), words[:, :, cols].rearrange("p u m -> p m u"))
@@ -452,9 +418,9 @@ def tile_list_deferred_tile_shading_kernel(
         def shade(b, c):
             codes = placed_tile([P, BANK], U32, "z_codes%d_%d" % (b, c), Z_CODES_AT[b] + c * 2 * KIB)
             if b == 0:
-                plane = placed_tile([P, BANK], U8, "z_plane0_%d" % c, MIX_AT[0] + c * 2 * KIB)
+                plane = placed_tile([P, BANK], U8, "z_plane0_%d" % c, LAST_MIX_AT + c * 2 * KIB)
             else:
-                plane = placed_tile([P, BANK], U8, "z_plane1_%d" % c, AFTER_TAB1_AT + 5 * KIB + HALF + c * HALF)
+                plane = new_tile([P, BANK], U8, "z_plane1_%d" % c)
             nc.vector.quantize_mx(out=codes[:].bitcast(FP8X4), scales=plane[:], in_=woven[b, c][:])
             for half in range(2):
                 if b == 0:
@@ -473,8 +439,8 @@ def tile_list_deferred_tile_shading_kernel(
             nc.sync.dma_start(out[half * P : (half + 1) * P, c * BANK : (c + 1) * BANK], result[:])
 
         last_row(0)
-        w4_codes = placed_tile([P, 2 * N], U32, "w4_codes", AFTER_TAB1_AT + 3 * KIB + HALF)
-        w4_plane = placed_tile([P, 2 * N], U8, "w4_plane", LAST_SOURCES_AT + 2 * KIB)
+        w4_codes = new_tile([P, 2 * N], U32, "w4_codes")
+        w4_plane = placed_tile([P, 2 * N], U8, "w4_plane", SOURCES_AT[6])
         nc.vector.quantize_mx(out=w4_codes[:].bitcast(FP8X4), scales=w4_plane[:], in_=w4_rounded[:].rearrange("p b x -> p (b x)"))
         for c in range(CHUNKS):
             if c + 1 < CHUNKS:

@@ -30,27 +30,26 @@ OPAQUE_ROWS_FROM = 112
 TRANSLUCENT_ROWS_FROM = 48
 FIRST_PIECES = ((0, 256), (256, 512), (512, 1024))
 
-PAGE_AT = tuple(KIB * at for at in (0, 36, 24, 16, 8, 44, 52, 60))
-FIRST_TRANSLUCENT_AT = 32 * KIB
-W2_LATE_ROUNDED_AT = 30 * KIB
+PAGE_AT = tuple(KIB * at for at in (0, 36, 28, 16, 8, 44, 52, 60))
+FIRST_TRANSLUCENT_AT = 129 * KIB
+THIRD_OPAQUE_AT = 24 * KIB
+W2_ROUNDED_AT = THIRD_OPAQUE_AT
 TAB1_WORDS_AT = 57 * KIB
 TAB2_WORDS_AT = TAB1_WORDS_AT + HALF - 16 * KIB
 W2_LATE_RAW_AT = TAB1_WORDS_AT + HALF
 THIRD_SQUARED_AT = W2_LATE_RAW_AT
 LATE_SCALE_ROWS_AT = W2_LATE_RAW_AT + 8 * KIB
 W3_LATE_WORDS_AT = 45 * KIB
-W2_EARLY_PLANE_AT = PAGE_AT[6]
 TRANSLUCENT_PLANES_AT = 68 * KIB
 LATE_PLANES_AT = TRANSLUCENT_PLANES_AT + KIB + HALF
 W3_EARLY_CODES_AT = LATE_PLANES_AT + KIB
 TRANSLUCENT_EXPOSURE_AT = W3_EARLY_CODES_AT + 2 * KIB
 SOURCES_AT = {1: 77 * KIB, 2: 81 * KIB, 4: 89 * KIB, 6: 97 * KIB}
-RECTIFIED_AT = {0: 92 * KIB + HALF, 2: 93 * KIB}
-W2_EARLY_ROUNDED_AT = 94 * KIB
+RECTIFIED_AT = {0: W2_ROUNDED_AT - HALF, 2: W2_ROUNDED_AT}
 W4_RAW_AT = SOURCES_AT[6]
 GATES_AT = (105 * KIB, 113 * KIB)
 FIRST_OPAQUE_AT = 121 * KIB
-FIRST_SQUARED_AT = (FIRST_OPAQUE_AT + 2 * KIB, FIRST_OPAQUE_AT + 3 * KIB, FIRST_OPAQUE_AT)
+FIRST_SQUARED_AT = (FIRST_OPAQUE_AT + 2 * KIB, W4_RAW_AT, FIRST_OPAQUE_AT)
 SECOND_SQUARED_AT = 125 * KIB
 LATE_SQUARED_AT = {4: 133 * KIB, 6: FIRST_OPAQUE_AT}
 LATE_ROWS_AT = FIRST_OPAQUE_AT
@@ -140,7 +139,7 @@ def tile_list_deferred_tile_shading_kernel(
 
         table_warm_up = new_tile([P, 2], F32, "table_warm_up")
         nc.gpsimd.memset(table_warm_up[:, 0:1], 0.0)
-        nc.gpsimd.memset(tab1_s[0 : opaque_rows.start, :].bitcast(I32), 0)
+        nc.vector.memset(tab1_s[0 : opaque_rows.start, :].bitcast(I32), 0)
         carried_planes = new_tile([P, 3 * BANK], U8, "carried_planes")
         nc.gpsimd.memset(carried_planes[:].bitcast(I32), 0)
         nc.gpsimd.memset(tab2_s[0 : translucent_rows.start, :].bitcast(I32), 0)
@@ -231,15 +230,10 @@ def tile_list_deferred_tile_shading_kernel(
             nc.scalar.copy(
                 rounded.rearrange("p (n i t) -> p n t i", i=4, t=4), raw.rearrange("p t (n i) -> p n t i", i=4))
 
-        def quantised(name, plane, rounded):
-            codes = new_tile([P, BANK], U32, name)
-            nc.vector.quantize_mx(out=codes[:].bitcast(FP8X4), scales=plane[:], in_=rounded)
-            return codes, plane
-
         def translucent_layer(s, colour, gate):
             for h in range(2):
                 cols = slice(h * BANK, (h + 1) * BANK)
-                acc = product(page_columns(w2_early_codes, late.get("w2_codes"), s, P), page_columns(w2_early_plane, late.get("w2_plane"), s, P),
+                acc = product(w2_codes[:, s * P : (s + 1) * P], w2_plane[:, s * P : (s + 1) * P],
                               FP8X4, v2_codes[:, cols], v2_plane[:, cols])
                 nc.scalar.copy(colour[:, cols], acc)
             for h in range(2):
@@ -255,52 +249,50 @@ def tile_list_deferred_tile_shading_kernel(
                     nc.sync.dma_start(dst[32 * q : 32 * q + 32, u], dealt_rows(src, s - EARLY + u))
             return dst
 
-        w2_early_rounded = placed_tile([P, 4 * BANK], BF16, "w2_early_rounded", W2_EARLY_ROUNDED_AT)
         squared1 = placed_tile([P, S], F32, "squared1", GATHERED_ROWS_AT)
         opaque_layer(1, squared1[:])
-        round_rows(w2_early_rounded[:], w2_early_raw[:])
         v2_codes = new_tile([P, S], U32, "v2_codes")
         nc.vector.tensor_copy(v2_codes[:], tab2_w[:].bitcast(U32).indirect(idx2[:]))
-        w2_early_codes, w2_early_plane = quantised(
-            "w2_early_codes", placed_tile([P, BANK], U8, "w2_early_plane", W2_EARLY_PLANE_AT), w2_early_rounded[:])
         opaque1 = placed_tile([P, S], F32, "opaque1", FIRST_OPAQUE_AT)
         nc.gpsimd.tensor_tensor(opaque1[:], squared1[:], opaque_exposure[:], MULT)
         put_opaque(1, opaque1[:])
 
-        late_opaque_exposures = {s: late_exposures(wg1, s, "opaque_exposures") for s in (4, 6)}
-        w3_late_words = load(placed_tile([P, BANK], I32, "w3_late_words", W3_LATE_WORDS_AT), words_of(w3_words)[:, BANK:])
-        w4_raw = placed_tile([P, 2, 4, N], F32, "w4_raw", W4_RAW_AT)
-        nc.sync.dma_start(w4_raw[:, 0].rearrange("p t n -> p (t n)"), w4[0:K, :].rearrange("(p t) n -> p (t n)", t=4))
-        for t in range(4):
-            nc.sync.dma_start(w4_raw[:, 1, t], dealt_rows(w4[K:, :], t))
-
-        def early_opaque_source(s, at):
-            squared = placed_tile([P, S], F32, "squared%d" % s, at)
-            opaque_layer(s, squared[:])
-            nc.gpsimd.tensor_tensor(squared[:], squared[:], opaque_exposure[:], MULT)
-            return squared
-
-        opaque2 = early_opaque_source(2, SECOND_SQUARED_AT)
+        opaque2 = placed_tile([P, S], F32, "opaque2", SECOND_SQUARED_AT)
+        opaque_layer(2, opaque2[:])
+        nc.gpsimd.tensor_tensor(opaque2[:], opaque2[:], opaque_exposure[:], MULT)
         identity = {}
         for dtype, name, at in ((F32, "identity_words", GATHERED_ROWS_AT), (BF16, "identity_values", GATHERED_ROWS_AT + HALF)):
             identity.setdefault(dtype, placed_tile([P, P], dtype, name, at))
             make_identity(nc, identity[dtype][:])
 
-        w2_late_rounded = placed_tile([P, 4 * BANK], BF16, "w2_late_rounded", W2_LATE_ROUNDED_AT)
+        w2_rounded = placed_tile([P, 2, 4 * BANK], BF16, "w2_rounded", W2_ROUNDED_AT)
+        round_rows(w2_rounded[:, 0], w2_early_raw[:])
         nc.scalar.copy(
-            w2_late_rounded[:].rearrange("p (t a b i) -> p t a b i", t=4, b=4, i=4),
+            w2_rounded[:, 1].rearrange("p (t a b i) -> p t a b i", t=4, b=4, i=4),
             w2_late_raw[:].rearrange("p i (a t b) -> p t a b i", t=4, b=4))
-        w2_late = quantised("w2_late_codes", new_tile([P, BANK], U8, "w2_late_plane"), w2_late_rounded[:])
-        late.setdefault("w2_codes", w2_late[0])
-        late.setdefault("w2_plane", w2_late[1])
+        w2_codes = new_tile([P, H], U32, "w2_codes")
+        w2_plane = new_tile([P, H], U8, "w2_plane")
+        nc.vector.quantize_mx(out=w2_codes[:].bitcast(FP8X4), scales=w2_plane[:], in_=w2_rounded[:].rearrange("p b x -> p (b x)"))
         put_opaque(2, opaque2[:])
+
+        w4_raw = placed_tile([P, 2, 4, N], F32, "w4_raw", W4_RAW_AT)
+        nc.sync.dma_start(w4_raw[:, 0].rearrange("p t n -> p (t n)"), w4[0:K, :].rearrange("(p t) n -> p (t n)", t=4))
+        for t in range(4):
+            nc.sync.dma_start(w4_raw[:, 1, t], dealt_rows(w4[K:, :], t))
+        w3_late_words = load(placed_tile([P, BANK], I32, "w3_late_words", W3_LATE_WORDS_AT), words_of(w3_words)[:, BANK:])
+        late_opaque_exposures = {s: late_exposures(wg1, s, "opaque_exposures") for s in (4, 6)}
+
+        squared3 = placed_tile([P, S], F32, "squared3", THIRD_SQUARED_AT)
+        opaque_layer(3, squared3[:])
+        opaque3 = placed_tile([P, S], F32, "opaque3", THIRD_OPAQUE_AT)
+        nc.gpsimd.tensor_tensor(opaque3[:], squared3[:], opaque_exposure[:], MULT)
+        put_opaque(3, opaque3[:])
 
         first = placed_tile([P, 2, S], F32, "colour_and_gate0", GATES_AT[0])
         translucent_layer(0, first[:, 0], first[:, 1])
         translucent0 = placed_tile([P, S], F32, "translucent0", FIRST_TRANSLUCENT_AT)
         nc.gpsimd.tensor_tensor(first[:, 0], first[:, 0], translucent_exposure[:], MULT)
         nc.gpsimd.tensor_tensor(translucent0[:], first[:, 0], first[:, 1], MULT)
-        put_opaque(3, early_opaque_source(3, THIRD_SQUARED_AT)[:])
         put_translucent(0, translucent0[:])
 
         def translucent_sources(s, count, exposures):

@@ -30,10 +30,11 @@ OPAQUE_ROWS_FROM = 112
 TRANSLUCENT_ROWS_FROM = 48
 FIRST_PIECES = ((0, 256), (256, 512), (512, 1024))
 
-PAGE_AT = tuple(KIB * at for at in (0, 36, 28, 16, 8, 44, 52, 60))
-FIRST_TRANSLUCENT_AT = 129 * KIB
-THIRD_OPAQUE_AT = 24 * KIB
-W2_ROUNDED_AT = THIRD_OPAQUE_AT
+PAGE_AT = tuple(KIB * at for at in (0, 8, 24, 16, 36, 44, 52, 60))
+FIRST_TRANSLUCENT_AT = 32 * KIB
+W2_ROUNDED_AT = 125 * KIB
+SECOND_OPAQUE_AT = W2_ROUNDED_AT
+V2_CODES_AT = W2_ROUNDED_AT + 4 * KIB
 TAB1_WORDS_AT = 57 * KIB
 TAB2_WORDS_AT = TAB1_WORDS_AT + HALF - 16 * KIB
 W2_LATE_RAW_AT = TAB1_WORDS_AT + HALF
@@ -50,7 +51,6 @@ W4_RAW_AT = SOURCES_AT[6]
 GATES_AT = (105 * KIB, 113 * KIB)
 FIRST_OPAQUE_AT = 121 * KIB
 FIRST_SQUARED_AT = (FIRST_OPAQUE_AT + 2 * KIB, W4_RAW_AT, FIRST_OPAQUE_AT)
-SECOND_SQUARED_AT = 125 * KIB
 LATE_SQUARED_AT = {4: 133 * KIB, 6: FIRST_OPAQUE_AT}
 LATE_ROWS_AT = FIRST_OPAQUE_AT
 Z_AT = (133 * KIB, 137 * KIB)
@@ -68,7 +68,7 @@ MIX_AT = (LATE_EXPOSURES_AT[4], GATES_AT[1], LATE_EXPOSURES_AT[6], GATES_AT[0], 
 LAST_MIX_AT = LATE_EXPOSURES_AT[6]
 PAIRS_AT = TURNED_AT
 Z_CODES_AT = (PAGE_AT[3], PAGE_AT[2])
-RESULTS_AT = PAGE_AT[1]
+RESULTS_AT = PAGE_AT[4]
 OPAQUE_BANKS = (0, 1)
 TRANSLUCENT_BANKS = (2, 3, 4, 5, 5, 4, 3, 2)
 TURN_BANKS = (6, 7)
@@ -164,8 +164,8 @@ def tile_list_deferred_tile_shading_kernel(
         for lo, hi in FIRST_PIECES:
             nc.vector.tensor_copy(v1_codes[:, lo:hi], tab1_w[:].bitcast(U32).indirect(entries(idx1, lo, hi)))
 
-        tab2_w = load(placed_tile([P, T], I32, "tab2_w", TAB2_WORDS_AT), words_of(tab2_words))
         w2_late_raw = load(placed_tile([P, 4, BANK], F32, "w2_late_raw", W2_LATE_RAW_AT), w2_rows[1])
+        tab2_w = load(placed_tile([P, T], I32, "tab2_w", TAB2_WORDS_AT), words_of(tab2_words))
         translucent_planes = placed_tile([P, S + BANK], U8, "translucent_planes", TRANSLUCENT_PLANES_AT)
         late_planes = placed_tile([P, 2 * BANK], U8, "late_planes", LATE_PLANES_AT)
         nc.gpsimd.memset(translucent_planes[:].bitcast(I32), 0)
@@ -204,10 +204,11 @@ def tile_list_deferred_tile_shading_kernel(
                           FP4X4, v1_codes[:, lo:hi], v1_planes[h][:, lo - h * BANK : hi - h * BANK], hi - lo)
             nc.scalar.activation(dst, acc, ACT.Relu)
 
-        def opaque_layer(s, squared):
+        def opaque_layer(s, squared, rectified=None):
+            rectified = squared if rectified is None else rectified
             for h in range(2):
-                rectify(s, h * BANK, (h + 1) * BANK, squared[:, h * BANK : (h + 1) * BANK])
-            nc.scalar.activation(squared, squared, ACT.Square)
+                rectify(s, h * BANK, (h + 1) * BANK, rectified[:, h * BANK : (h + 1) * BANK])
+            nc.scalar.activation(squared, rectified, ACT.Square)
 
         pages = {}
 
@@ -249,21 +250,10 @@ def tile_list_deferred_tile_shading_kernel(
                     nc.sync.dma_start(dst[32 * q : 32 * q + 32, u], dealt_rows(src, s - EARLY + u))
             return dst
 
-        squared1 = placed_tile([P, S], F32, "squared1", GATHERED_ROWS_AT)
-        opaque_layer(1, squared1[:])
-        v2_codes = new_tile([P, S], U32, "v2_codes")
-        nc.vector.tensor_copy(v2_codes[:], tab2_w[:].bitcast(U32).indirect(idx2[:]))
-        opaque1 = placed_tile([P, S], F32, "opaque1", FIRST_OPAQUE_AT)
-        nc.gpsimd.tensor_tensor(opaque1[:], squared1[:], opaque_exposure[:], MULT)
-        put_opaque(1, opaque1[:])
-
-        opaque2 = placed_tile([P, S], F32, "opaque2", SECOND_SQUARED_AT)
-        opaque_layer(2, opaque2[:])
-        nc.gpsimd.tensor_tensor(opaque2[:], opaque2[:], opaque_exposure[:], MULT)
-        identity = {}
-        for dtype, name, at in ((F32, "identity_words", GATHERED_ROWS_AT), (BF16, "identity_values", GATHERED_ROWS_AT + HALF)):
-            identity.setdefault(dtype, placed_tile([P, P], dtype, name, at))
-            make_identity(nc, identity[dtype][:])
+        squared1 = placed_tile([P, S], F32, "squared1", LATE_SQUARED_AT[4])
+        opaque_layer(1, squared1[:], placed_tile([P, S], F32, "rectified_page1", V2_CODES_AT)[:])
+        pages.setdefault(1, placed_tile([P, T2], F32, "page1", PAGE_AT[1]))
+        nc.vector.tensor_tensor(pages[1][:].indirect(idx3[:]), squared1[:], opaque_exposure[:], MULT)
 
         w2_rounded = placed_tile([P, 2, 4 * BANK], BF16, "w2_rounded", W2_ROUNDED_AT)
         round_rows(w2_rounded[:, 0], w2_early_raw[:])
@@ -273,6 +263,13 @@ def tile_list_deferred_tile_shading_kernel(
         w2_codes = new_tile([P, H], U32, "w2_codes")
         w2_plane = new_tile([P, H], U8, "w2_plane")
         nc.vector.quantize_mx(out=w2_codes[:].bitcast(FP8X4), scales=w2_plane[:], in_=w2_rounded[:].rearrange("p b x -> p (b x)"))
+        v2_codes = placed_tile([P, S], U32, "v2_codes", V2_CODES_AT)
+        nc.vector.tensor_copy(v2_codes[:], tab2_w[:].bitcast(U32).indirect(idx2[:]))
+
+        squared2 = placed_tile([P, S], F32, "squared2", GATHERED_ROWS_AT)
+        opaque_layer(2, squared2[:])
+        opaque2 = placed_tile([P, S], F32, "opaque2", SECOND_OPAQUE_AT)
+        nc.gpsimd.tensor_tensor(opaque2[:], squared2[:], opaque_exposure[:], MULT)
         put_opaque(2, opaque2[:])
 
         w4_raw = placed_tile([P, 2, 4, N], F32, "w4_raw", W4_RAW_AT)
@@ -284,9 +281,12 @@ def tile_list_deferred_tile_shading_kernel(
 
         squared3 = placed_tile([P, S], F32, "squared3", THIRD_SQUARED_AT)
         opaque_layer(3, squared3[:])
-        opaque3 = placed_tile([P, S], F32, "opaque3", THIRD_OPAQUE_AT)
-        nc.gpsimd.tensor_tensor(opaque3[:], squared3[:], opaque_exposure[:], MULT)
-        put_opaque(3, opaque3[:])
+        nc.gpsimd.tensor_tensor(squared3[:], squared3[:], opaque_exposure[:], MULT)
+        put_opaque(3, squared3[:])
+        identity = {}
+        for dtype, name, at in ((F32, "identity_words", GATHERED_ROWS_AT), (BF16, "identity_values", GATHERED_ROWS_AT + HALF)):
+            identity.setdefault(dtype, placed_tile([P, P], dtype, name, at))
+            make_identity(nc, identity[dtype][:])
 
         first = placed_tile([P, 2, S], F32, "colour_and_gate0", GATES_AT[0])
         translucent_layer(0, first[:, 0], first[:, 1])

@@ -28,7 +28,8 @@ QUADRANTS = (0, 2, 1, 3)
 SCALE_ROWS = 16
 OPAQUE_ROWS_FROM = 112
 TRANSLUCENT_ROWS_FROM = 48
-FIRST_PIECES = ((0, 256), (256, 512), (512, 1024))
+FIRST_GATHERS = ((0, 256), (256, 512), (512, 1024))
+FIRST_PIECES = ((0, 0, 256), (1, 0, 512), (0, 256, 1024), (1, 512, 1024))
 
 PAGE_AT = tuple(KIB * at for at in (0, 8, 24, 16, 36, 44, 52, 60))
 FIRST_TRANSLUCENT_AT = 32 * KIB
@@ -37,20 +38,19 @@ SECOND_OPAQUE_AT = W2_ROUNDED_AT
 V2_CODES_AT = W2_ROUNDED_AT + 4 * KIB
 TAB1_WORDS_AT = 57 * KIB
 TAB2_WORDS_AT = TAB1_WORDS_AT + HALF - 16 * KIB
-W2_LATE_RAW_AT = TAB1_WORDS_AT + HALF
-THIRD_SQUARED_AT = W2_LATE_RAW_AT
-LATE_SCALE_ROWS_AT = W2_LATE_RAW_AT + 8 * KIB
+THIRD_SQUARED_AT = TAB1_WORDS_AT + HALF
+LATE_SCALE_ROWS_AT = THIRD_SQUARED_AT + 8 * KIB
 W3_LATE_WORDS_AT = 45 * KIB
 TRANSLUCENT_PLANES_AT = 68 * KIB
 LATE_PLANES_AT = TRANSLUCENT_PLANES_AT + KIB + HALF
 W3_EARLY_CODES_AT = LATE_PLANES_AT + KIB
 TRANSLUCENT_EXPOSURE_AT = W3_EARLY_CODES_AT + 2 * KIB
 SOURCES_AT = {1: 77 * KIB, 2: 81 * KIB, 4: 89 * KIB, 6: 97 * KIB}
-RECTIFIED_AT = {0: W2_ROUNDED_AT - HALF, 2: W2_ROUNDED_AT}
+RECTIFIED_AT = W2_ROUNDED_AT
 W4_RAW_AT = SOURCES_AT[6]
 GATES_AT = (105 * KIB, 113 * KIB)
 FIRST_OPAQUE_AT = 121 * KIB
-FIRST_SQUARED_AT = (FIRST_OPAQUE_AT + 2 * KIB, W4_RAW_AT, FIRST_OPAQUE_AT)
+FIRST_SQUARED_AT = (FIRST_OPAQUE_AT, FIRST_OPAQUE_AT + KIB, W4_RAW_AT, 133 * KIB)
 LATE_SQUARED_AT = {4: 133 * KIB, 6: FIRST_OPAQUE_AT}
 LATE_ROWS_AT = FIRST_OPAQUE_AT
 Z_AT = (133 * KIB, 137 * KIB)
@@ -58,6 +58,7 @@ OPAQUE_EXPOSURE_AT = 141 * KIB
 TAB1_ROWS_AT = OPAQUE_EXPOSURE_AT + HALF - 4 * KIB
 LATE_EXPOSURES_AT = {4: 145 * KIB, 6: 153 * KIB}
 W2_EARLY_RAW_AT = LATE_EXPOSURES_AT[4] + HALF
+W2_LATE_RAW_AT = W2_EARLY_RAW_AT + 8 * KIB
 TAB2_ROWS_AT = LATE_EXPOSURES_AT[6]
 GATHERED_ROWS_AT = 161 * KIB
 STAGE_AT = GATHERED_ROWS_AT + HALF
@@ -159,12 +160,12 @@ def tile_list_deferred_tile_shading_kernel(
 
         w2_rows = w2.rearrange("(p i) (b c) -> b p i c", i=4, b=2)
         w2_early_raw = load(placed_tile([P, 4, BANK], F32, "w2_early_raw", W2_EARLY_RAW_AT), w2_rows[0])
+        w2_late_raw = load(placed_tile([P, 4, BANK], F32, "w2_late_raw", W2_LATE_RAW_AT), w2_rows[1])
 
         v1_codes = new_tile([P, S], U32, "v1_codes")
-        for lo, hi in FIRST_PIECES:
+        for lo, hi in FIRST_GATHERS:
             nc.vector.tensor_copy(v1_codes[:, lo:hi], tab1_w[:].bitcast(U32).indirect(entries(idx1, lo, hi)))
 
-        w2_late_raw = load(placed_tile([P, 4, BANK], F32, "w2_late_raw", W2_LATE_RAW_AT), w2_rows[1])
         tab2_w = load(placed_tile([P, T], I32, "tab2_w", TAB2_WORDS_AT), words_of(tab2_words))
         translucent_planes = placed_tile([P, S + BANK], U8, "translucent_planes", TRANSLUCENT_PLANES_AT)
         late_planes = placed_tile([P, 2 * BANK], U8, "late_planes", LATE_PLANES_AT)
@@ -204,11 +205,10 @@ def tile_list_deferred_tile_shading_kernel(
                           FP4X4, v1_codes[:, lo:hi], v1_planes[h][:, lo - h * BANK : hi - h * BANK], hi - lo)
             nc.scalar.activation(dst, acc, ACT.Relu)
 
-        def opaque_layer(s, squared, rectified=None):
-            rectified = squared if rectified is None else rectified
+        def opaque_layer(s, squared):
             for h in range(2):
-                rectify(s, h * BANK, (h + 1) * BANK, rectified[:, h * BANK : (h + 1) * BANK])
-            nc.scalar.activation(squared, rectified, ACT.Square)
+                rectify(s, h * BANK, (h + 1) * BANK, squared[:, h * BANK : (h + 1) * BANK])
+            nc.scalar.activation(squared, squared, ACT.Square)
 
         pages = {}
 
@@ -219,13 +219,16 @@ def tile_list_deferred_tile_shading_kernel(
         def put_translucent(s, values):
             nc.vector.tensor_copy(pages[s][:].indirect(idx4[:]), values)
 
-        pages.setdefault(0, placed_tile([P, T2], F32, "page0", PAGE_AT[0]))
-        for i, (lo, hi) in enumerate(FIRST_PIECES):
+        for i, (s, lo, hi) in enumerate(FIRST_PIECES):
             squared = placed_tile([P, hi - lo], F32, "first_squared%d" % i, FIRST_SQUARED_AT[i])
-            rectified = placed_tile([P, hi - lo], F32, "rectified%d" % i, RECTIFIED_AT[i]) if i in RECTIFIED_AT else squared
-            rectify(0, lo, hi, rectified[:])
+            rectified = placed_tile([P, hi - lo], F32, "rectified%d" % i, RECTIFIED_AT)
+            for a, b in ((lo, min(hi, BANK)), (max(lo, BANK), hi)):
+                if a < b:
+                    rectify(s, a, b, rectified[:, a - lo : b - lo])
             nc.scalar.activation(squared[:], rectified[:], ACT.Square)
-            nc.vector.tensor_tensor(pages[0][:].indirect(entries(idx3, lo, hi)), squared[:], opaque_exposure[:, lo:hi], MULT)
+            if lo == 0:
+                pages.setdefault(s, placed_tile([P, T2], F32, "page%d" % s, PAGE_AT[s]))
+            nc.vector.tensor_tensor(pages[s][:].indirect(entries(idx3, lo, hi)), squared[:], opaque_exposure[:, lo:hi], MULT)
 
         def round_rows(rounded, raw):
             nc.scalar.copy(
@@ -249,11 +252,6 @@ def tile_list_deferred_tile_shading_kernel(
                 for q in QUADRANTS:
                     nc.sync.dma_start(dst[32 * q : 32 * q + 32, u], dealt_rows(src, s - EARLY + u))
             return dst
-
-        squared1 = placed_tile([P, S], F32, "squared1", LATE_SQUARED_AT[4])
-        opaque_layer(1, squared1[:], placed_tile([P, S], F32, "rectified_page1", V2_CODES_AT)[:])
-        pages.setdefault(1, placed_tile([P, T2], F32, "page1", PAGE_AT[1]))
-        nc.vector.tensor_tensor(pages[1][:].indirect(idx3[:]), squared1[:], opaque_exposure[:], MULT)
 
         w2_rounded = placed_tile([P, 2, 4 * BANK], BF16, "w2_rounded", W2_ROUNDED_AT)
         round_rows(w2_rounded[:, 0], w2_early_raw[:])

@@ -55,13 +55,12 @@ LATE_SQUARED_AT = {4: 133 * KIB, 6: FIRST_OPAQUE_AT}
 LATE_ROWS_AT = FIRST_OPAQUE_AT
 Z_AT = (133 * KIB, 137 * KIB)
 OPAQUE_EXPOSURE_AT = 141 * KIB
-TAB1_ROWS_AT = OPAQUE_EXPOSURE_AT + HALF - 4 * KIB
+TAB1_ROWS_AT = OPAQUE_EXPOSURE_AT - 4 * KIB
 LATE_EXPOSURES_AT = {4: 145 * KIB, 6: 153 * KIB}
 W2_EARLY_RAW_AT = LATE_EXPOSURES_AT[4] + HALF
 W2_LATE_RAW_AT = W2_EARLY_RAW_AT + 8 * KIB
 TAB2_ROWS_AT = LATE_EXPOSURES_AT[6]
 GATHERED_ROWS_AT = 161 * KIB
-STAGE_AT = GATHERED_ROWS_AT + HALF
 TURNED_AT = 165 * KIB
 WOVEN_AT = (181 * KIB, PAGE_AT[0])
 W4_ROUNDED_AT = 197 * KIB
@@ -126,35 +125,39 @@ def tile_list_deferred_tile_shading_kernel(
         translucent_rows = slice(TRANSLUCENT_ROWS_FROM, TRANSLUCENT_ROWS_FROM + SCALE_ROWS)
         tab1_s = placed_tile([P, T], U8, "tab1_s", TAB1_ROWS_AT)
         tab2_s = placed_tile([P, T], U8, "tab2_s", TAB2_ROWS_AT)
-        stage = placed_tile([P, 2 * BANK], U8, "stage", STAGE_AT)
-        nc.scalar.dma_start(tab1_s[opaque_rows, :].bitcast(I32), tab_scales[0].bitcast(I32))
-        nc.scalar.dma_start(tab2_s[translucent_rows, :].bitcast(I32), tab2_scales[0].bitcast(I32))
-        nc.scalar.dma_start(stage[opaque_rows, BANK:].bitcast(I32), w1_scales[0, :, 0:BANK].bitcast(I32))
-        idx1 = load_list(offs, "idx1")
-        idx2 = load_list(offs2, "idx2")
-        idx3 = load_list(offs3, "idx3")
-        tab1_w = load(placed_tile([P, T], I32, "tab1_w", TAB1_WORDS_AT), words_of(tab_words))
-        w1_words_sb = new_tile([P, 2 * H], U8, "w1_words_sb")
-        nc.sync.dma_start(w1_words_sb[:].bitcast(I32), w1_words[0].bitcast(I32))
-        idx4 = load_list(offs4, "idx4")
-
+        carried_planes = new_tile([P, 2 * BANK], U8, "carried_planes")
+        w1_plane = new_tile([P, BANK], U8, "w1_plane")
         table_warm_up = new_tile([P, 2], F32, "table_warm_up")
+        nc.gpsimd.memset(w1_plane[:].bitcast(I32), 0)
         nc.gpsimd.memset(table_warm_up[:, 0:1], 0.0)
-        nc.vector.memset(tab1_s[0 : opaque_rows.start, :].bitcast(I32), 0)
-        carried_planes = new_tile([P, 3 * BANK], U8, "carried_planes")
         nc.gpsimd.memset(carried_planes[:].bitcast(I32), 0)
+        nc.vector.memset(tab1_s[0 : opaque_rows.start, :].bitcast(I32), 0)
         nc.gpsimd.memset(tab2_s[0 : translucent_rows.start, :].bitcast(I32), 0)
         nc.gpsimd.memset(tab2_s[translucent_rows.stop :, :].bitcast(I32), 0)
+
+        def load_w1_rows(queue, q):
+            queue.dma_start(w1_plane[32 * q : 32 * q + 4, :].bitcast(I32), w1_scales[0, 4 * q : 4 * q + 4, 0:BANK].bitcast(I32))
+
+        nc.scalar.dma_start(tab1_s[opaque_rows, :].bitcast(I32), tab_scales[0].bitcast(I32))
+        for q in QUADRANTS[:3]:
+            load_w1_rows(nc.scalar, q)
+        idx1 = load_list(offs, "idx1")
+        nc.sync.dma_start(tab2_s[translucent_rows, :].bitcast(I32), tab2_scales[0].bitcast(I32))
+        idx2 = load_list(offs2, "idx2")
+        tab1_w = load(placed_tile([P, T], I32, "tab1_w", TAB1_WORDS_AT), words_of(tab_words))
+        w1_words_sb = new_tile([P, H], U8, "w1_words_sb")
+        nc.sync.dma_start(w1_words_sb[:].bitcast(I32), w1_words[0, :, 0:H].bitcast(I32))
+        load_w1_rows(nc.sync, QUADRANTS[3])
+        opaque_exposure = load(placed_tile([P, S], F32, "opaque_exposure", OPAQUE_EXPOSURE_AT), wg1)
+        idx3 = load_list(offs3, "idx3")
+        idx4 = load_list(offs4, "idx4")
         nc.scalar.activation(table_warm_up[:, 1:2], table_warm_up[:, 0:1], ACT.Sigmoid)
 
-        v1_rows = [placed_tile([P, BANK], U8, "v1_rows%d" % h, GATHERED_ROWS_AT + h * 3 * HALF) for h in range(2)]
-        nc.vector.tensor_copy(v1_rows[0][:], tab1_s[:].indirect(entries(idx1, 0, BANK)))
-        nc.vector.tensor_copy(stage[96:, 0:BANK].bitcast(I32), v1_rows[0][96:, :].bitcast(I32))
-        to_quadrants(nc.scalar, carried_planes[:, 0 : 2 * BANK], stage[opaque_rows, :])
-        nc.vector.tensor_copy(v1_rows[1][:], tab1_s[:].indirect(entries(idx1, BANK, S)))
-        opaque_exposure = load(placed_tile([P, S], F32, "opaque_exposure", OPAQUE_EXPOSURE_AT), wg1)
-        v1_planes, w1_plane = (carried_planes[:, 0:BANK], carried_planes[:, 2 * BANK :]), carried_planes[:, BANK : 2 * BANK]
-        to_quadrants(nc.sync, v1_planes[1], v1_rows[1][opaque_rows, :])
+        v1_planes = (carried_planes[:, 0:BANK], carried_planes[:, BANK:])
+        v1_rows = [new_tile([P, BANK], U8, "v1_rows%d" % h) for h in range(2)]
+        for h, queue in enumerate((nc.scalar, nc.sync)):
+            nc.vector.tensor_copy(v1_rows[h][:], tab1_s[:].indirect(entries(idx1, h * BANK, (h + 1) * BANK)))
+            to_quadrants(queue, v1_planes[h], v1_rows[h][opaque_rows, :])
         v2_rows = new_tile([P, S], U8, "v2_rows")
         nc.vector.tensor_copy(v2_rows[:], tab2_s[:].indirect(idx2[:]))
 
@@ -274,6 +277,8 @@ def tile_list_deferred_tile_shading_kernel(
         nc.sync.dma_start(w4_raw[:, 0].rearrange("p t n -> p (t n)"), w4[0:K, :].rearrange("(p t) n -> p (t n)", t=4))
         for t in range(4):
             nc.sync.dma_start(w4_raw[:, 1, t], dealt_rows(w4[K:, :], t))
+        w1_late_words = placed_tile([P, H], U8, "w1_late_words", W3_LATE_WORDS_AT + 2 * KIB)
+        nc.sync.dma_start(w1_late_words[:].bitcast(I32), w1_words[0, :, H:].bitcast(I32))
         w3_late_words = load(placed_tile([P, BANK], I32, "w3_late_words", W3_LATE_WORDS_AT), words_of(w3_words)[:, BANK:])
         late_opaque_exposures = {s: late_exposures(wg1, s, "opaque_exposures") for s in (4, 6)}
 
@@ -312,7 +317,7 @@ def tile_list_deferred_tile_shading_kernel(
 
         translucent_sources(1, 1, translucent_exposure[:].unsqueeze(1))
 
-        late.setdefault("w1_codes", deal_columns(new_tile([P, H], U8, "w1_late_codes")[:], w1_words_sb[:, H:]))
+        late.setdefault("w1_codes", deal_columns(new_tile([P, H], U8, "w1_late_codes")[:], w1_late_words[:]))
         for q in QUADRANTS:
             live = slice(32 * q, 32 * q + 4)
             nc.scalar.copy(

@@ -73,6 +73,11 @@ OPAQUE_BANKS = (0, 1)
 TRANSLUCENT_BANKS = (2, 3, 4, 5, 5, 4, 3, 2)
 TURN_BANKS = (6, 7)
 SUM_BANKS = (0, 1, 2, 3, 4, 5, 6, 7)
+FLIP_BANKS = (3, 4)
+MIX_BANKS = (5, 6, 7)
+MIX_IN_PSUM = 3
+WOVEN_COLUMNS = T2 - BANK
+FLIPPED_AT = PAIRS_AT + 8 * KIB
 
 
 def tile_list_deferred_tile_shading_kernel(
@@ -391,57 +396,96 @@ def tile_list_deferred_tile_shading_kernel(
                     for c in range(CHUNKS)]
         for c in range(CHUNKS):
             turn_back(c)
-        pairs = placed_tile([P, 2, T2, 2], BF16, "pairs", PAIRS_AT)
-        last_pairs = pairs[:, 1].rearrange("p m e -> p (m e)").bitcast(F32)
-        nc.sync.dma_start(last_pairs, mix_rows(PAGES - 2))
+        last = PAGES - 1
+        shared_cols = slice(WOVEN_COLUMNS, T2)
+        mix_banks = []
+        for c in range(MIX_IN_PSUM):
+            flipped = bank(FLIP_BANKS)
+            for k in range(BLOCKS):
+                nc.tensor.transpose(flipped[:, k * P : (k + 1) * P], last_mix[c][:, k * P : (k + 1) * P], identity[F32][:])
+            flipped_rows = placed_tile([P, BANK], F32, "flipped_mix%d" % c, FLIPPED_AT + c * 2 * KIB)
+            nc.scalar.copy(flipped_rows[:], flipped[:])
+            mix_banks.append(bank(MIX_BANKS))
+            for k in range(BLOCKS):
+                nc.tensor.transpose(mix_banks[c][:, k * P : (k + 1) * P], flipped_rows[:, k * P : (k + 1) * P], identity[F32][:])
+
+        shares = ((0, WOVEN_COLUMNS), (WOVEN_COLUMNS, T2))
+        pairs = [placed_tile([P, 2, hi - lo, 2], BF16, "pairs%d" % lo, PAIRS_AT + 8 * lo) for lo, hi in shares]
+        last_pairs = [tile[:, 1].rearrange("p m e -> p (m e)").bitcast(F32) for tile in pairs]
+        for i, (lo, hi) in enumerate(shares):
+            nc.sync.dma_start(last_pairs[i], mix_rows(last - 1)[:, :, lo:hi])
         late_rows = placed_tile([P, 2 * T2], BF16, "late_rows", LATE_ROWS_AT)
         for u in range(2):
             nc.gpsimd.tensor_tensor(late_rows[:, u * T2 : (u + 1) * T2], pages[EARLY + u][:], mix_tiles[EARLY + u][:], MULT)
-        nc.scalar.copy(pairs[:, 0], late_rows[:].rearrange("p (e m) -> p m e", e=2))
-        nc.gpsimd.tensor_tensor(pairs[:, 1, :, 0], pages[PAGES - 2][:], last_pairs, MULT)
+        for i, (lo, hi) in enumerate(shares):
+            nc.scalar.copy(pairs[i][:, 0], late_rows[:].rearrange("p (e m) -> p m e", e=2)[:, lo:hi])
 
-        last = PAGES - 1
+        def weave(c, tile, cols):
+            words = tile[:].rearrange("p u m e -> p u (m e)").bitcast(U32)
+            nc.scalar.copy(
+                woven_tile(1, c)[:].bitcast(U32).rearrange("p (m u) -> p m u", u=2), words[:, :, cols].rearrange("p u m -> p m u"))
+
+        for i, (lo, hi) in reversed(list(enumerate(shares))):
+            nc.gpsimd.tensor_tensor(pairs[i][:, 1, :, 0], pages[last - 1][:, lo:hi], last_pairs[i], MULT)
+        weave(CHUNKS - 1, pairs[1], slice(0, BANK))
+
         accs = {}
 
         def last_row(c):
             cols = slice(c * BANK, (c + 1) * BANK)
-            nc.vector.tensor_tensor(pairs[:, 1, cols, 1], pages[last][:, cols], last_mix[c][:], MULT)
-            words = pairs[:].rearrange("p u m e -> p u (m e)").bitcast(U32)
-            nc.scalar.copy(
-                woven_tile(1, c)[:].bitcast(U32).rearrange("p (m u) -> p m u", u=2), words[:, :, cols].rearrange("p u m -> p m u"))
+            nc.vector.tensor_tensor(pairs[0][:, 1, cols, 1], pages[last][:, cols], (mix_banks[c] if c < MIX_IN_PSUM else last_mix[c])[:], MULT)
+            weave(c, pairs[0], cols)
+
+        def pieces(c):
+            return ((0, BANK // 2), (BANK // 2, BANK)) if c + 1 == CHUNKS else ((0, BANK),)
 
         def shade(b, c):
             codes = placed_tile([P, BANK], U32, "z_codes%d_%d" % (b, c), Z_CODES_AT[b] + c * 2 * KIB)
             if b == 0:
-                plane = placed_tile([P, BANK], U8, "z_plane0_%d" % c, LAST_MIX_AT + c * 2 * KIB)
+                plane = placed_tile([P, BANK], U8, "z_plane0_%d" % c, LAST_MIX_AT + (CHUNKS - 1) * 2 * KIB + c * HALF + HALF // 2)
+                nc.vector.quantize_mx(out=codes[:].bitcast(FP8X4), scales=plane[:], in_=woven[b, c][:])
             else:
                 plane = new_tile([P, BANK], U8, "z_plane1_%d" % c)
-            nc.vector.quantize_mx(out=codes[:].bitcast(FP8X4), scales=plane[:], in_=woven[b, c][:])
-            for half in range(2):
-                if b == 0:
-                    accs.setdefault((c, half), bank(SUM_BANKS))
-                cols = slice(b * N + half * P, b * N + (half + 1) * P)
-                nc.tensor.matmul_mx(
-                    out=accs[c, half][:], lhsT=w4_codes[:, cols].bitcast(FP8X4), lhsT_scale=w4_plane[:, cols],
-                    rhs=codes[:].bitcast(FP8X4), rhs_scale=plane[:], start=(b == 0), stop=(b == 1))
+            for lo, hi in pieces(c):
+                if b == 1:
+                    nc.vector.quantize_mx(
+                        out=codes[:, lo:hi].bitcast(FP8X4), scales=plane[:, lo:hi], in_=woven[b, c][:, 4 * lo : 4 * hi])
+                for half in range(2):
+                    if b == 0:
+                        accs.setdefault((c, lo, half), bank(SUM_BANKS)[:, 0 : hi - lo])
+                    cols = slice(b * N + half * P, b * N + (half + 1) * P)
+                    nc.tensor.matmul_mx(
+                        out=accs[c, lo, half], lhsT=w4_codes[:, cols].bitcast(FP8X4), lhsT_scale=w4_plane[:, cols],
+                        rhs=codes[:, lo:hi].bitcast(FP8X4), rhs_scale=plane[:, lo:hi], start=(b == 0), stop=(b == 1))
 
-        def store(c, half, on_vector):
-            result = placed_tile([P, BANK], F32, "result%d_%d" % (c, half), RESULTS_AT + (2 * c + half) * 2 * KIB)
+        def store(c, lo, hi, half, on_vector):
+            result = placed_tile([P, hi - lo], F32, "result%d_%d_%d" % (c, lo, half), RESULTS_AT + (2 * c + half) * 2 * KIB + 4 * lo)
             if on_vector:
-                nc.vector.tensor_copy(result[:], accs[c, half][:])
+                nc.vector.tensor_copy(result[:], accs[c, lo, half])
             else:
-                nc.scalar.copy(result[:], accs[c, half][:])
-            nc.sync.dma_start(out[half * P : (half + 1) * P, c * BANK : (c + 1) * BANK], result[:])
+                nc.scalar.copy(result[:], accs[c, lo, half])
+            nc.sync.dma_start(out[half * P : (half + 1) * P, c * BANK + lo : c * BANK + hi], result[:])
 
-        last_row(0)
+        nc.gpsimd.tensor_tensor(
+            woven[1, CHUNKS - 1][:].rearrange("p (m t) -> p m t", t=4)[:, :, 3], pages[last][:, shared_cols], last_mix[CHUNKS - 1][:], MULT)
+        for c in range(CHUNKS - 1):
+            last_row(c)
+        for c in range(2):
+            warm_up = ps.tile([P, BANK], F32, name="warm_up%d" % c, tag="bank%d" % MIX_BANKS[c])
+            for repeat in range(2):
+                nc.tensor.matmul_mx(
+                    out=warm_up[:], lhsT=w2_codes[:, 0:P].bitcast(FP8X4), lhsT_scale=w2_plane[:, 0:P],
+                    rhs=v2_codes[:, 0:BANK].bitcast(FP8X4), rhs_scale=v2_plane[:, 0:BANK], start=True, stop=True)
         w4_codes = new_tile([P, 2 * N], U32, "w4_codes")
-        w4_plane = placed_tile([P, 2 * N], U8, "w4_plane", SOURCES_AT[6])
+        w4_plane = placed_tile([P, 2 * N], U8, "w4_plane", LAST_MIX_AT + (CHUNKS - 1) * 2 * KIB - HALF // 2)
         nc.vector.quantize_mx(out=w4_codes[:].bitcast(FP8X4), scales=w4_plane[:], in_=w4_rounded[:].rearrange("p b x -> p (b x)"))
         for c in range(CHUNKS):
-            if c + 1 < CHUNKS:
-                last_row(c + 1)
+            if c + 1 == CHUNKS:
+                for half in range(2):
+                    store(0, 0, BANK, half, False)
             shade(0, c)
             shade(1, c)
-        for c in range(CHUNKS):
-            for half in range(2):
-                store(c, half, c >= CHUNKS // 2 and half == 1)
+        for c in range(1, CHUNKS):
+            for lo, hi in pieces(c):
+                for half in range(2):
+                    store(c, lo, hi, half, c + 1 == CHUNKS and half == 1)

@@ -48,12 +48,11 @@ TRANSLUCENT_EXPOSURE_AT = W3_EARLY_CODES_AT + 2 * KIB
 SOURCES_AT = {1: 77 * KIB, 2: 81 * KIB, 4: 89 * KIB, 6: 97 * KIB}
 RECTIFIED_AT = W2_ROUNDED_AT
 W4_RAW_AT = SOURCES_AT[6]
-GATES_AT = (105 * KIB, 113 * KIB)
+GATES_AT = {0: 181 * KIB, 1: 105 * KIB, 2: 189 * KIB, 4: 113 * KIB, 6: 145 * KIB}
 FIRST_OPAQUE_AT = 121 * KIB
 FIRST_SQUARED_AT = (FIRST_OPAQUE_AT, FIRST_OPAQUE_AT + KIB, W4_RAW_AT, 133 * KIB)
 LATE_SQUARED_AT = {4: 133 * KIB, 6: FIRST_OPAQUE_AT}
-LATE_ROWS_AT = FIRST_OPAQUE_AT
-Z_AT = (133 * KIB, 137 * KIB)
+Z_AT = (202 * KIB, GATES_AT[0])
 OPAQUE_EXPOSURE_AT = 141 * KIB
 TAB1_ROWS_AT = OPAQUE_EXPOSURE_AT - 4 * KIB
 LATE_EXPOSURES_AT = {4: 145 * KIB, 6: 153 * KIB}
@@ -62,22 +61,22 @@ W2_LATE_RAW_AT = W2_EARLY_RAW_AT + 8 * KIB
 TAB2_ROWS_AT = LATE_EXPOSURES_AT[6]
 GATHERED_ROWS_AT = 161 * KIB
 TURNED_AT = 165 * KIB
-WOVEN_AT = (181 * KIB, PAGE_AT[0])
-W4_ROUNDED_AT = 197 * KIB
-MIX_AT = (LATE_EXPOSURES_AT[4], GATES_AT[1], LATE_EXPOSURES_AT[6], GATES_AT[0], LATE_EXPOSURES_AT[4], GATES_AT[1])
-LAST_MIX_AT = LATE_EXPOSURES_AT[6]
-PAIRS_AT = TURNED_AT
+WOVEN_AT = (182 * KIB, PAGE_AT[0])
+W4_ROUNDED_AT = 198 * KIB
+MIX_AT = (SOURCES_AT[6], GATES_AT[2], GATES_AT[6], GATES_AT[4], GATES_AT[1], GATES_AT[4])
+LAST_MIX_AT = (OPAQUE_EXPOSURE_AT, OPAQUE_EXPOSURE_AT + 2 * KIB, GATHERED_ROWS_AT + KIB, LATE_EXPOSURES_AT[6] + 2 * KIB)
+PAIRS_AT = (TURNED_AT + KIB, TURNED_AT + 13 * KIB)
 Z_CODES_AT = (PAGE_AT[3], PAGE_AT[2])
 RESULTS_AT = PAGE_AT[4]
 OPAQUE_BANKS = (0, 1)
 TRANSLUCENT_BANKS = (2, 3, 4, 5, 5, 4, 3, 2)
-TURN_BANKS = (6, 7)
+TURN_BANKS = (1, 0)
 SUM_BANKS = (0, 1, 2, 3, 4, 5, 6, 7)
 FLIP_BANKS = (3, 4)
 MIX_BANKS = (5, 6, 7)
 MIX_IN_PSUM = 3
 WOVEN_COLUMNS = T2 - BANK
-FLIPPED_AT = PAIRS_AT + 8 * KIB
+FLIPPED_AT = 210 * KIB
 
 
 def tile_list_deferred_tile_shading_kernel(
@@ -291,10 +290,8 @@ def tile_list_deferred_tile_shading_kernel(
         opaque_layer(3, squared3[:])
         nc.gpsimd.tensor_tensor(squared3[:], squared3[:], opaque_exposure[:], MULT)
         put_opaque(3, squared3[:])
-        identity = {}
-        for dtype, name, at in ((F32, "identity_words", GATHERED_ROWS_AT), (BF16, "identity_values", GATHERED_ROWS_AT + HALF)):
-            identity.setdefault(dtype, placed_tile([P, P], dtype, name, at))
-            make_identity(nc, identity[dtype][:])
+        identity = placed_tile([P, P], F32, "identity", GATHERED_ROWS_AT)
+        make_identity(nc, identity[:])
 
         first = placed_tile([P, 2, S], F32, "colour_and_gate0", GATES_AT[0])
         translucent_layer(0, first[:, 0], first[:, 1])
@@ -305,7 +302,7 @@ def tile_list_deferred_tile_shading_kernel(
 
         def translucent_sources(s, count, exposures):
             colours = placed_tile([P, count, S], F32, "colours%d" % s, SOURCES_AT[s])
-            gates = placed_tile([P, count, S], F32, "gates%d" % s, GATES_AT[(s // 2 + 1) % 2])
+            gates = placed_tile([P, count, S], F32, "gates%d" % s, GATES_AT[s])
             for u in range(count):
                 translucent_layer(s + u, colours[:, u], gates[:, u])
             nc.gpsimd.tensor_tensor(colours[:], colours[:], exposures, MULT)
@@ -344,19 +341,21 @@ def tile_list_deferred_tile_shading_kernel(
         for b in range(2):
             round_rows(w4_rounded[:, b], w4_raw[:, b])
         translucent_sources(4, 2, exposures45[:])
-        translucent_sources(6, 2, exposures67[:])
 
         turned = [placed_tile([P, BLOCKS, 2, P], F32, "turned%d" % c, TURNED_AT + c * 4 * KIB) for c in range(CHUNKS)]
 
-        def turn(s, z):
+        def turn(first, z_pair):
+            words = z_pair[:].rearrange("p m u -> p (m u)").bitcast(F32)
             for c in range(CHUNKS):
-                acc = bank(TURN_BANKS, BF16)
+                acc = bank(TURN_BANKS)
                 for k in range(BLOCKS):
                     at = c * BANK + k * P
-                    nc.tensor.transpose(acc[:, k * P : (k + 1) * P], z[:, at : at + P], identity[BF16][:])
-                nc.scalar.copy(
-                    turned[c][:, :, :, 32 * s : 32 * (s + 1)],
-                    acc[:].bitcast(F32).rearrange("p (k q v) -> p k v q", k=BLOCKS, v=2))
+                    nc.tensor.transpose(acc[:, k * P : (k + 1) * P], words[:, at : at + P], identity[:])
+                rows = acc[:].bitcast(BF16).rearrange("p (k q v e u) -> p u k v q e", k=BLOCKS, v=2, e=2, u=2)
+                places = turned[c][:].rearrange("p k v w -> p (k v w)").bitcast(BF16).rearrange(
+                    "p (k v s q e) -> p s k v q e", k=BLOCKS, v=2, s=EARLY, e=2)
+                for u in range(2):
+                    nc.scalar.copy(places[:, first + u], rows[:, u])
 
         woven = {}
 
@@ -371,7 +370,7 @@ def tile_list_deferred_tile_shading_kernel(
                 for k in range(2):
                     for v in range(2):
                         at = (2 * k + v) * P
-                        nc.tensor.transpose(acc[:, at : at + P], turned[c][:, 2 * pair + k, v], identity[F32][:])
+                        nc.tensor.transpose(acc[:, at : at + P], turned[c][:, 2 * pair + k, v], identity[:])
                 nc.scalar.copy(
                     words[:, pair * BANK : (pair + 1) * BANK].rearrange("p (k m v) -> p k m v", k=2, v=2),
                     acc[:].rearrange("p (k v m) -> p k m v", k=2, v=2))
@@ -382,43 +381,43 @@ def tile_list_deferred_tile_shading_kernel(
         def load_mix(s):
             return load(placed_tile([P, T2], F32, "mix%d" % s, MIX_AT[s]), mix_rows(s))
 
-        mix_tiles = {s: load_mix(s) for s in range(EARLY)}
-        for s in range(EARLY):
-            z = placed_tile([P, T2], BF16, "z%d" % s, Z_AT[s % 2])
-            nc.gpsimd.tensor_tensor(z[:], pages[s][:], mix_tiles[s][:], MULT)
-            turn(s, z)
-            if s < 2:
-                mix_tiles.setdefault(EARLY + s, load_mix(EARLY + s))
-            if s == 2:
-                last_mix = [
-                    load(placed_tile([P, BANK], F32, "last_mix%d" % c, LAST_MIX_AT + c * 2 * KIB),
-                         mix_rows(PAGES - 1)[:, :, c * BANK : (c + 1) * BANK])
-                    for c in range(CHUNKS)]
-        for c in range(CHUNKS):
-            turn_back(c)
+        def load_last_mix(c):
+            return load(placed_tile([P, BANK], F32, "last_mix%d" % c, LAST_MIX_AT[c]), mix_rows(PAGES - 1)[:, :, c * BANK : (c + 1) * BANK])
+
+        mix_tiles = {s: load_mix(s) for s in range(EARLY + 1)}
+        z_pairs = {}
+        for s in (0, 2, 1, 3):
+            if s % 2 == 0:
+                z_pairs.setdefault(s // 2, placed_tile([P, T2, 2], BF16, "z_pair%d" % s, Z_AT[s // 2]))
+            nc.gpsimd.tensor_tensor(z_pairs[s // 2][:, :, s % 2], pages[s][:], mix_tiles[s][:], MULT)
+            if s % 2 == 1:
+                turn(s - 1, z_pairs[s // 2])
+        mix_tiles.setdefault(EARLY + 1, load_mix(EARLY + 1))
+        translucent_sources(6, 2, exposures67[:])
+        last_mix = [load_last_mix(c) for c in range(CHUNKS)]
         last = PAGES - 1
         shared_cols = slice(WOVEN_COLUMNS, T2)
         mix_banks = []
         for c in range(MIX_IN_PSUM):
             flipped = bank(FLIP_BANKS)
             for k in range(BLOCKS):
-                nc.tensor.transpose(flipped[:, k * P : (k + 1) * P], last_mix[c][:, k * P : (k + 1) * P], identity[F32][:])
+                nc.tensor.transpose(flipped[:, k * P : (k + 1) * P], last_mix[c][:, k * P : (k + 1) * P], identity[:])
             flipped_rows = placed_tile([P, BANK], F32, "flipped_mix%d" % c, FLIPPED_AT + c * 2 * KIB)
             nc.scalar.copy(flipped_rows[:], flipped[:])
             mix_banks.append(bank(MIX_BANKS))
             for k in range(BLOCKS):
-                nc.tensor.transpose(mix_banks[c][:, k * P : (k + 1) * P], flipped_rows[:, k * P : (k + 1) * P], identity[F32][:])
+                nc.tensor.transpose(mix_banks[c][:, k * P : (k + 1) * P], flipped_rows[:, k * P : (k + 1) * P], identity[:])
 
+        for c in range(CHUNKS):
+            turn_back(c)
         shares = ((0, WOVEN_COLUMNS), (WOVEN_COLUMNS, T2))
-        pairs = [placed_tile([P, 2, hi - lo, 2], BF16, "pairs%d" % lo, PAIRS_AT + 8 * lo) for lo, hi in shares]
+        pairs = [placed_tile([P, 2, hi - lo, 2], BF16, "pairs%d" % i, PAIRS_AT[i]) for i, (lo, hi) in enumerate(shares)]
         last_pairs = [tile[:, 1].rearrange("p m e -> p (m e)").bitcast(F32) for tile in pairs]
-        for i, (lo, hi) in enumerate(shares):
+        for i, (lo, hi) in reversed(list(enumerate(shares))):
             nc.sync.dma_start(last_pairs[i], mix_rows(last - 1)[:, :, lo:hi])
-        late_rows = placed_tile([P, 2 * T2], BF16, "late_rows", LATE_ROWS_AT)
         for u in range(2):
-            nc.gpsimd.tensor_tensor(late_rows[:, u * T2 : (u + 1) * T2], pages[EARLY + u][:], mix_tiles[EARLY + u][:], MULT)
-        for i, (lo, hi) in enumerate(shares):
-            nc.scalar.copy(pairs[i][:, 0], late_rows[:].rearrange("p (e m) -> p m e", e=2)[:, lo:hi])
+            for i, (lo, hi) in reversed(list(enumerate(shares))):
+                nc.gpsimd.tensor_tensor(pairs[i][:, 0, :, u], pages[EARLY + u][:, lo:hi], mix_tiles[EARLY + u][:, lo:hi], MULT)
 
         def weave(c, tile, cols):
             words = tile[:].rearrange("p u m e -> p u (m e)").bitcast(U32)
@@ -427,7 +426,8 @@ def tile_list_deferred_tile_shading_kernel(
 
         for i, (lo, hi) in reversed(list(enumerate(shares))):
             nc.gpsimd.tensor_tensor(pairs[i][:, 1, :, 0], pages[last - 1][:, lo:hi], last_pairs[i], MULT)
-        weave(CHUNKS - 1, pairs[1], slice(0, BANK))
+            if hi == T2:
+                weave(CHUNKS - 1, pairs[i], slice(0, BANK))
 
         accs = {}
 
@@ -442,7 +442,7 @@ def tile_list_deferred_tile_shading_kernel(
         def shade(b, c):
             codes = placed_tile([P, BANK], U32, "z_codes%d_%d" % (b, c), Z_CODES_AT[b] + c * 2 * KIB)
             if b == 0:
-                plane = placed_tile([P, BANK], U8, "z_plane0_%d" % c, LAST_MIX_AT + (CHUNKS - 1) * 2 * KIB + c * HALF + HALF // 2)
+                plane = placed_tile([P, BANK], U8, "z_plane0_%d" % c, LAST_MIX_AT[-1] + c * HALF + HALF // 2)
                 nc.vector.quantize_mx(out=codes[:].bitcast(FP8X4), scales=plane[:], in_=woven[b, c][:])
             else:
                 plane = new_tile([P, BANK], U8, "z_plane1_%d" % c)
@@ -477,7 +477,7 @@ def tile_list_deferred_tile_shading_kernel(
                     out=warm_up[:], lhsT=w2_codes[:, 0:P].bitcast(FP8X4), lhsT_scale=w2_plane[:, 0:P],
                     rhs=v2_codes[:, 0:BANK].bitcast(FP8X4), rhs_scale=v2_plane[:, 0:BANK], start=True, stop=True)
         w4_codes = new_tile([P, 2 * N], U32, "w4_codes")
-        w4_plane = placed_tile([P, 2 * N], U8, "w4_plane", LAST_MIX_AT + (CHUNKS - 1) * 2 * KIB - HALF // 2)
+        w4_plane = placed_tile([P, 2 * N], U8, "w4_plane", LAST_MIX_AT[-1] - HALF // 2)
         nc.vector.quantize_mx(out=w4_codes[:].bitcast(FP8X4), scales=w4_plane[:], in_=w4_rounded[:].rearrange("p b x -> p (b x)"))
         for c in range(CHUNKS):
             if c + 1 == CHUNKS:

@@ -53,6 +53,7 @@ FIRST_OPAQUE_AT = 121 * KIB
 FIRST_SQUARED_AT = (FIRST_OPAQUE_AT, FIRST_OPAQUE_AT + KIB, W4_RAW_AT, 133 * KIB)
 LATE_SQUARED_AT = {4: 133 * KIB, 6: FIRST_OPAQUE_AT}
 Z_AT = (202 * KIB, GATES_AT[0])
+LATE_ROWS_AT = GATES_AT[6]
 OPAQUE_EXPOSURE_AT = 141 * KIB
 TAB1_ROWS_AT = OPAQUE_EXPOSURE_AT - 4 * KIB
 LATE_EXPOSURES_AT = {4: 145 * KIB, 6: 153 * KIB}
@@ -63,8 +64,8 @@ GATHERED_ROWS_AT = 161 * KIB
 TURNED_AT = 165 * KIB
 WOVEN_AT = (182 * KIB, PAGE_AT[0])
 W4_ROUNDED_AT = 198 * KIB
-MIX_AT = (SOURCES_AT[6], GATES_AT[2], GATES_AT[6], GATES_AT[4], GATES_AT[1], GATES_AT[4])
-LAST_MIX_AT = (OPAQUE_EXPOSURE_AT, OPAQUE_EXPOSURE_AT + 2 * KIB, GATHERED_ROWS_AT + KIB, LATE_EXPOSURES_AT[6] + 2 * KIB)
+MIX_AT = (SOURCES_AT[6], GATES_AT[2], GATES_AT[6], GATES_AT[4], GATES_AT[4], LATE_EXPOSURES_AT[6])
+LAST_MIX_AT = (OPAQUE_EXPOSURE_AT, OPAQUE_EXPOSURE_AT + 2 * KIB, GATHERED_ROWS_AT + KIB, GATES_AT[1] + 2 * KIB)
 PAIRS_AT = (TURNED_AT + KIB, TURNED_AT + 13 * KIB)
 Z_CODES_AT = (PAGE_AT[3], PAGE_AT[2])
 RESULTS_AT = PAGE_AT[4]
@@ -300,15 +301,21 @@ def tile_list_deferred_tile_shading_kernel(
         nc.gpsimd.tensor_tensor(translucent0[:], first[:, 0], first[:, 1], MULT)
         put_translucent(0, translucent0[:])
 
-        def translucent_sources(s, count, exposures):
+        def translucent_layers(s, count):
             colours = placed_tile([P, count, S], F32, "colours%d" % s, SOURCES_AT[s])
             gates = placed_tile([P, count, S], F32, "gates%d" % s, GATES_AT[s])
             for u in range(count):
                 translucent_layer(s + u, colours[:, u], gates[:, u])
+            return colours, gates
+
+        def expose_and_put(s, count, colours, gates, exposures):
             nc.gpsimd.tensor_tensor(colours[:], colours[:], exposures, MULT)
             nc.gpsimd.tensor_tensor(colours[:], colours[:], gates[:], MULT)
             for u in range(count):
                 put_translucent(s + u, colours[:, u])
+
+        def translucent_sources(s, count, exposures):
+            expose_and_put(s, count, *translucent_layers(s, count), exposures)
 
         def late_opaque_pair(s):
             squared = placed_tile([P, 2, S], F32, "squared%d" % s, LATE_SQUARED_AT[s])
@@ -360,7 +367,7 @@ def tile_list_deferred_tile_shading_kernel(
         woven = {}
 
         def woven_tile(b, c):
-            woven.setdefault((b, c), placed_tile([P, 4 * BANK], BF16, "woven%d_%d" % (b, c), WOVEN_AT[b] + c * 4 * KIB))
+            woven.setdefault((b, c), placed_tile([P, 4 * BANK], BF16, "woven%d_%d" % (b, c), LATE_ROWS_AT if (b, c) == (1, CHUNKS - 1) else WOVEN_AT[b] + c * 4 * KIB))
             return woven[b, c]
 
         def turn_back(c):
@@ -384,16 +391,19 @@ def tile_list_deferred_tile_shading_kernel(
         def load_last_mix(c):
             return load(placed_tile([P, BANK], F32, "last_mix%d" % c, LAST_MIX_AT[c]), mix_rows(PAGES - 1)[:, :, c * BANK : (c + 1) * BANK])
 
-        mix_tiles = {s: load_mix(s) for s in range(EARLY + 1)}
+        mix_tiles = {s: load_mix(s) for s in range(EARLY)}
         z_pairs = {}
         for s in (0, 2, 1, 3):
             if s % 2 == 0:
                 z_pairs.setdefault(s // 2, placed_tile([P, T2, 2], BF16, "z_pair%d" % s, Z_AT[s // 2]))
             nc.gpsimd.tensor_tensor(z_pairs[s // 2][:, :, s % 2], pages[s][:], mix_tiles[s][:], MULT)
+            if s == 2:
+                last_layers = translucent_layers(6, 2)
             if s % 2 == 1:
                 turn(s - 1, z_pairs[s // 2])
+        mix_tiles.setdefault(EARLY, load_mix(EARLY))
+        expose_and_put(6, 2, *last_layers, exposures67[:])
         mix_tiles.setdefault(EARLY + 1, load_mix(EARLY + 1))
-        translucent_sources(6, 2, exposures67[:])
         last_mix = [load_last_mix(c) for c in range(CHUNKS)]
         last = PAGES - 1
         shared_cols = slice(WOVEN_COLUMNS, T2)
@@ -415,9 +425,11 @@ def tile_list_deferred_tile_shading_kernel(
         last_pairs = [tile[:, 1].rearrange("p m e -> p (m e)").bitcast(F32) for tile in pairs]
         for i, (lo, hi) in reversed(list(enumerate(shares))):
             nc.sync.dma_start(last_pairs[i], mix_rows(last - 1)[:, :, lo:hi])
+        late_rows = placed_tile([P, 2 * T2], BF16, "late_rows", LATE_ROWS_AT)
         for u in range(2):
-            for i, (lo, hi) in reversed(list(enumerate(shares))):
-                nc.gpsimd.tensor_tensor(pairs[i][:, 0, :, u], pages[EARLY + u][:, lo:hi], mix_tiles[EARLY + u][:, lo:hi], MULT)
+            nc.gpsimd.tensor_tensor(late_rows[:, u * T2 : (u + 1) * T2], pages[EARLY + u][:], mix_tiles[EARLY + u][:], MULT)
+        for i, (lo, hi) in reversed(list(enumerate(shares))):
+            nc.scalar.copy(pairs[i][:, 0], late_rows[:].rearrange("p (e m) -> p m e", e=2)[:, lo:hi])
 
         def weave(c, tile, cols):
             words = tile[:].rearrange("p u m e -> p u (m e)").bitcast(U32)

@@ -34,8 +34,8 @@ FIRST_PIECES = ((0, 0, 256), (1, 0, 512), (0, 256, 1024), (1, 512, 1024))
 PAGE_AT = tuple(KIB * at for at in (0, 8, 24, 16, 36, 44, 52, 60))
 FIRST_TRANSLUCENT_AT = 32 * KIB
 W2_ROUNDED_AT = 125 * KIB
-SECOND_OPAQUE_AT = W2_ROUNDED_AT
-V2_CODES_AT = W2_ROUNDED_AT + 4 * KIB
+THIRD_OPAQUE_AT = W2_ROUNDED_AT - 2 * KIB
+V2_CODES_AT = 109 * KIB
 TAB1_WORDS_AT = 57 * KIB
 TAB2_WORDS_AT = TAB1_WORDS_AT + HALF - 16 * KIB
 THIRD_SQUARED_AT = TAB1_WORDS_AT + HALF
@@ -65,7 +65,7 @@ TURNED_AT = 165 * KIB
 WOVEN_AT = (182 * KIB, PAGE_AT[0])
 W4_ROUNDED_AT = 198 * KIB
 MIX_AT = (SOURCES_AT[6], GATES_AT[2], GATES_AT[6], GATES_AT[4], GATES_AT[4], LATE_EXPOSURES_AT[6])
-LAST_MIX_AT = (OPAQUE_EXPOSURE_AT, OPAQUE_EXPOSURE_AT + 2 * KIB, GATHERED_ROWS_AT + KIB, GATES_AT[1] + 2 * KIB)
+LAST_MIX_AT = (OPAQUE_EXPOSURE_AT, OPAQUE_EXPOSURE_AT + 2 * KIB, GATHERED_ROWS_AT + KIB, GATES_AT[1] + KIB)
 PAIRS_AT = (TURNED_AT + KIB, TURNED_AT + 13 * KIB)
 Z_CODES_AT = (PAGE_AT[3], PAGE_AT[2])
 RESULTS_AT = PAGE_AT[4]
@@ -135,8 +135,8 @@ def tile_list_deferred_tile_shading_kernel(
         table_warm_up = new_tile([P, 2], F32, "table_warm_up")
         nc.gpsimd.memset(w1_plane[:].bitcast(I32), 0)
         nc.gpsimd.memset(table_warm_up[:, 0:1], 0.0)
+        nc.gpsimd.memset(tab1_s[0 : opaque_rows.start, :].bitcast(I32), 0)
         nc.gpsimd.memset(carried_planes[:].bitcast(I32), 0)
-        nc.vector.memset(tab1_s[0 : opaque_rows.start, :].bitcast(I32), 0)
         nc.gpsimd.memset(tab2_s[0 : translucent_rows.start, :].bitcast(I32), 0)
         nc.gpsimd.memset(tab2_s[translucent_rows.stop :, :].bitcast(I32), 0)
 
@@ -266,17 +266,26 @@ def tile_list_deferred_tile_shading_kernel(
         nc.scalar.copy(
             w2_rounded[:, 1].rearrange("p (t a b i) -> p t a b i", t=4, b=4, i=4),
             w2_late_raw[:].rearrange("p i (a t b) -> p t a b i", t=4, b=4))
+        v2_codes = placed_tile([P, S], U32, "v2_codes", V2_CODES_AT)
+        nc.vector.tensor_copy(v2_codes[:], tab2_w[:].bitcast(U32).indirect(idx2[:]))
         w2_codes = new_tile([P, H], U32, "w2_codes")
         w2_plane = new_tile([P, H], U8, "w2_plane")
         nc.vector.quantize_mx(out=w2_codes[:].bitcast(FP8X4), scales=w2_plane[:], in_=w2_rounded[:].rearrange("p b x -> p (b x)"))
-        v2_codes = placed_tile([P, S], U32, "v2_codes", V2_CODES_AT)
-        nc.vector.tensor_copy(v2_codes[:], tab2_w[:].bitcast(U32).indirect(idx2[:]))
 
         squared2 = placed_tile([P, S], F32, "squared2", GATHERED_ROWS_AT)
-        opaque_layer(2, squared2[:])
-        opaque2 = placed_tile([P, S], F32, "opaque2", SECOND_OPAQUE_AT)
-        nc.gpsimd.tensor_tensor(opaque2[:], squared2[:], opaque_exposure[:], MULT)
-        put_opaque(2, opaque2[:])
+        for h in range(2):
+            half_page = squared2[:, h * BANK : (h + 1) * BANK]
+            rectify(2, h * BANK, (h + 1) * BANK, half_page)
+            nc.scalar.activation(half_page, half_page, ACT.Square)
+        pages.setdefault(2, placed_tile([P, T2], F32, "page2", PAGE_AT[2]))
+
+        def put_half_of_page2(h, at):
+            cols = slice(h * BANK, (h + 1) * BANK)
+            values = placed_tile([P, BANK], F32, "opaque2_%d" % h, at)
+            nc.gpsimd.tensor_tensor(values[:], squared2[:, cols], opaque_exposure[:, cols], MULT)
+            nc.vector.tensor_copy(pages[2][:].indirect(entries(idx3, cols.start, cols.stop)), values[:])
+
+        put_half_of_page2(0, FIRST_SQUARED_AT[-1])
 
         w4_raw = placed_tile([P, 2, 4, N], F32, "w4_raw", W4_RAW_AT)
         nc.sync.dma_start(w4_raw[:, 0].rearrange("p t n -> p (t n)"), w4[0:K, :].rearrange("(p t) n -> p (t n)", t=4))
@@ -289,8 +298,10 @@ def tile_list_deferred_tile_shading_kernel(
 
         squared3 = placed_tile([P, S], F32, "squared3", THIRD_SQUARED_AT)
         opaque_layer(3, squared3[:])
-        nc.gpsimd.tensor_tensor(squared3[:], squared3[:], opaque_exposure[:], MULT)
-        put_opaque(3, squared3[:])
+        opaque3 = placed_tile([P, S], F32, "opaque3", THIRD_OPAQUE_AT)
+        nc.gpsimd.tensor_tensor(opaque3[:], squared3[:], opaque_exposure[:], MULT)
+        put_opaque(3, opaque3[:])
+        put_half_of_page2(1, THIRD_SQUARED_AT)
         identity = placed_tile([P, P], F32, "identity", GATHERED_ROWS_AT)
         make_identity(nc, identity[:])
 

from contextlib import ExitStack

import concourse.mybir as mybir
from concourse.masks import make_identity

F32 = mybir.dt.float32
BF16 = mybir.dt.bfloat16
I32 = mybir.dt.int32
U32 = mybir.dt.uint32
U16 = mybir.dt.uint16
U8 = mybir.dt.uint8
FP8X4 = mybir.dt.float8_e4m3fn_x4
FP4X4 = mybir.dt.float4_e2m1fn_x4
ACT = mybir.ActivationFunctionType
MULT = mybir.AluOpType.mult

K, T, S, T2, H, N = 512, 4096, 1024, 2048, 1024, 256
P = 128
BANK = 512
FLOPS = 2 * (3 * K * H * S + H * N * T2)
PAGES = H // P
EARLY = PAGES // 2
CHUNKS = T2 // BANK
BLOCKS = BANK // P
KIB = 1024
HALF = KIB // 2
QUADRANTS = (0, 2, 1, 3)
SCALE_ROWS = 16
OPAQUE_ROWS_FROM = 112
TRANSLUCENT_ROWS_FROM = 48
FIRST_GATHERS = ((0, 256), (256, 512), (512, 1024))
FIRST_PIECES = ((0, 0, 256), (1, 0, 512), (0, 256, 1024), (1, 512, 1024))

PAGE_AT = tuple(KIB * at for at in (0, 8, 24, 16, 36, 44, 52, 60))
FIRST_TRANSLUCENT_AT = 32 * KIB
W2_ROUNDED_AT = 125 * KIB
THIRD_OPAQUE_AT = W2_ROUNDED_AT - 2 * KIB
V2_CODES_AT = 109 * KIB
TAB1_WORDS_AT = 57 * KIB
TAB2_WORDS_AT = TAB1_WORDS_AT + HALF - 16 * KIB
THIRD_SQUARED_AT = TAB1_WORDS_AT + HALF
LATE_SCALE_ROWS_AT = THIRD_SQUARED_AT + 8 * KIB
W3_LATE_WORDS_AT = 45 * KIB
TRANSLUCENT_PLANES_AT = 68 * KIB
LATE_PLANES_AT = TRANSLUCENT_PLANES_AT + KIB + HALF
W3_EARLY_CODES_AT = LATE_PLANES_AT + KIB
TRANSLUCENT_EXPOSURE_AT = W3_EARLY_CODES_AT + 2 * KIB
SOURCES_AT = {1: 77 * KIB, 2: 81 * KIB, 4: 89 * KIB, 6: 97 * KIB}
RECTIFIED_AT = W2_ROUNDED_AT
W4_RAW_AT = SOURCES_AT[6]
GATES_AT = {0: 181 * KIB, 1: 105 * KIB, 2: 189 * KIB, 4: 113 * KIB, 6: 145 * KIB}
FIRST_OPAQUE_AT = 121 * KIB
FIRST_SQUARED_AT = (FIRST_OPAQUE_AT, FIRST_OPAQUE_AT + KIB, W4_RAW_AT, 133 * KIB)
LATE_SQUARED_AT = {4: 133 * KIB, 6: FIRST_OPAQUE_AT}
Z_AT = (202 * KIB, GATES_AT[0])
LATE_ROWS_AT = GATES_AT[6]
OPAQUE_EXPOSURE_AT = 141 * KIB
TAB1_ROWS_AT = OPAQUE_EXPOSURE_AT - 4 * KIB
LATE_EXPOSURES_AT = {4: 145 * KIB, 6: 153 * KIB}
W2_EARLY_RAW_AT = LATE_EXPOSURES_AT[4] + HALF
W2_LATE_RAW_AT = W2_EARLY_RAW_AT + 8 * KIB
TAB2_ROWS_AT = LATE_EXPOSURES_AT[6]
GATHERED_ROWS_AT = 161 * KIB
TURNED_AT = 165 * KIB
WOVEN_AT = (182 * KIB, PAGE_AT[0])
W4_ROUNDED_AT = 198 * KIB
MIX_AT = (SOURCES_AT[6], GATES_AT[2], GATES_AT[6], GATES_AT[4], GATES_AT[4], LATE_EXPOSURES_AT[6])
LAST_MIX_AT = (OPAQUE_EXPOSURE_AT, OPAQUE_EXPOSURE_AT + 2 * KIB, GATHERED_ROWS_AT + KIB, GATES_AT[1] + KIB)
PAIRS_AT = (TURNED_AT + KIB, TURNED_AT + 13 * KIB)
Z_CODES_AT = (PAGE_AT[3], PAGE_AT[2])
RESULTS_AT = PAGE_AT[4]
OPAQUE_BANKS = (0, 1)
TRANSLUCENT_BANKS = (2, 3, 4, 5, 5, 4, 3, 2)
TURN_BANKS = (1, 0)
SUM_BANKS = (0, 1, 2, 3, 4, 5, 6, 7)
FLIP_BANKS = (3, 4)
MIX_BANKS = (5, 6, 7)
MIX_IN_PSUM = 3
WOVEN_COLUMNS = T2 - BANK
FLIPPED_AT = 210 * KIB


def tile_list_deferred_tile_shading_kernel(
    tc, tab_words, tab_scales, tab2_words, tab2_scales, offs, offs2, offs3, offs4,
    w1_words, w1_scales, w2, w3_words, w3_scales, wg1, wg2, mix, w4, out,
):
    nc = tc.nc
    with ExitStack() as ctx:
        lists = ctx.enter_context(tc.tile_pool(name="lists", bufs=1))
        sb = ctx.enter_context(tc.tile_pool(name="sb", bufs=1))
        shared = ctx.enter_context(tc.tile_pool(name="shared", bufs=1))
        ps = ctx.enter_context(tc.psum_pool(name="ps", bufs=1))

        def new_tile(shape, dtype, name):
            return sb.tile(shape, dtype, name=name, tag=name, bufs=1, align_bytes=64)

        def placed_tile(shape, dtype, name, offset):
            return shared.tile(shape, dtype, name=name, tag=name, bufs=1, align_bytes=64, offset=offset)

        turns_taken = {}

        def bank(ring, dtype=F32):
            taken = turns_taken.setdefault(ring, [])
            taken.append(ring[len(taken) % len(ring)])
            return ps.tile([P, BANK], dtype, name="bank%d_%d_%d" % (ring[0], len(ring), len(taken)), tag="bank%d" % taken[-1])

        def load_list(src, name):
            dst = lists.tile([P, S // 16], U16, name=name)
            nc.sync.dma_start(dst[:], src)
            return dst

        def entries(idx, lo, hi):
            return idx[:, lo // 16 : hi // 16]

        def words_of(src):
            return src[0].rearrange("p n i -> p (n i)").bitcast(I32)

        def load(dst, src):
            nc.sync.dma_start(dst[:], src)
            return dst

        def dealt_rows(src, t):
            return src.rearrange("(a t b) j -> t a b j", t=4, b=4)[t]

        def to_quadrants(queue, plane, rows):
            for q in QUADRANTS:
                queue.dma_start(plane[32 * q : 32 * q + 4, :].bitcast(I32), rows[4 * q : 4 * q + 4, :].bitcast(I32))

        opaque_rows = slice(OPAQUE_ROWS_FROM, OPAQUE_ROWS_FROM + SCALE_ROWS)
        translucent_rows = slice(TRANSLUCENT_ROWS_FROM, TRANSLUCENT_ROWS_FROM + SCALE_ROWS)
        tab1_s = placed_tile([P, T], U8, "tab1_s", TAB1_ROWS_AT)
        tab2_s = placed_tile([P, T], U8, "tab2_s", TAB2_ROWS_AT)
        carried_planes = new_tile([P, 2 * BANK], U8, "carried_planes")
        w1_plane = new_tile([P, BANK], U8, "w1_plane")
        table_warm_up = new_tile([P, 2], F32, "table_warm_up")
        nc.gpsimd.memset(w1_plane[:].bitcast(I32), 0)
        nc.gpsimd.memset(table_warm_up[:, 0:1], 0.0)
        nc.gpsimd.memset(tab1_s[0 : opaque_rows.start, :].bitcast(I32), 0)
        nc.gpsimd.memset(carried_planes[:].bitcast(I32), 0)
        nc.gpsimd.memset(tab2_s[0 : translucent_rows.start, :].bitcast(I32), 0)
        nc.gpsimd.memset(tab2_s[translucent_rows.stop :, :].bitcast(I32), 0)

        def load_w1_rows(queue, q):
            queue.dma_start(w1_plane[32 * q : 32 * q + 4, :].bitcast(I32), w1_scales[0, 4 * q : 4 * q + 4, 0:BANK].bitcast(I32))

        nc.scalar.dma_start(tab1_s[opaque_rows, :].bitcast(I32), tab_scales[0].bitcast(I32))
        for q in QUADRANTS[:3]:
            load_w1_rows(nc.scalar, q)
        idx1 = load_list(offs, "idx1")
        nc.sync.dma_start(tab2_s[translucent_rows, :].bitcast(I32), tab2_scales[0].bitcast(I32))
        idx2 = load_list(offs2, "idx2")
        tab1_w = load(placed_tile([P, T], I32, "tab1_w", TAB1_WORDS_AT), words_of(tab_words))
        w1_words_sb = new_tile([P, H], U8, "w1_words_sb")
        nc.sync.dma_start(w1_words_sb[:].bitcast(I32), w1_words[0, :, 0:H].bitcast(I32))
        load_w1_rows(nc.sync, QUADRANTS[3])
        opaque_exposure = load(placed_tile([P, S], F32, "opaque_exposure", OPAQUE_EXPOSURE_AT), wg1)
        idx3 = load_list(offs3, "idx3")
        idx4 = load_list(offs4, "idx4")
        nc.scalar.activation(table_warm_up[:, 1:2], table_warm_up[:, 0:1], ACT.Sigmoid)

        v1_planes = (carried_planes[:, 0:BANK], carried_planes[:, BANK:])
        v1_rows = [new_tile([P, BANK], U8, "v1_rows%d" % h) for h in range(2)]
        for h, queue in enumerate((nc.scalar, nc.sync)):
            nc.vector.tensor_copy(v1_rows[h][:], tab1_s[:].indirect(entries(idx1, h * BANK, (h + 1) * BANK)))
            to_quadrants(queue, v1_planes[h], v1_rows[h][opaque_rows, :])
        v2_rows = new_tile([P, S], U8, "v2_rows")
        nc.vector.tensor_copy(v2_rows[:], tab2_s[:].indirect(idx2[:]))

        w2_rows = w2.rearrange("(p i) (b c) -> b p i c", i=4, b=2)
        w2_early_raw = load(placed_tile([P, 4, BANK], F32, "w2_early_raw", W2_EARLY_RAW_AT), w2_rows[0])
        w2_late_raw = load(placed_tile([P, 4, BANK], F32, "w2_late_raw", W2_LATE_RAW_AT), w2_rows[1])

        v1_codes = new_tile([P, S], U32, "v1_codes")
        for lo, hi in FIRST_GATHERS:
            nc.vector.tensor_copy(v1_codes[:, lo:hi], tab1_w[:].bitcast(U32).indirect(entries(idx1, lo, hi)))

        tab2_w = load(placed_tile([P, T], I32, "tab2_w", TAB2_WORDS_AT), words_of(tab2_words))
        translucent_planes = placed_tile([P, S + BANK], U8, "translucent_planes", TRANSLUCENT_PLANES_AT)
        late_planes = placed_tile([P, 2 * BANK], U8, "late_planes", LATE_PLANES_AT)
        nc.gpsimd.memset(translucent_planes[:].bitcast(I32), 0)
        nc.gpsimd.memset(late_planes[:].bitcast(I32), 0)
        v2_plane, w3_plane = translucent_planes[:, 0:S], translucent_planes[:, S:]
        to_quadrants(nc.sync, v2_plane, v2_rows[translucent_rows, :])
        to_quadrants(nc.sync, w3_plane, w3_scales[0, :, 0:BANK])
        w3_early_codes = load(placed_tile([P, BANK], I32, "w3_early_codes", W3_EARLY_CODES_AT), words_of(w3_words)[:, 0:BANK])
        translucent_exposure = load(placed_tile([P, S], F32, "translucent_exposure", TRANSLUCENT_EXPOSURE_AT), wg2)
        late_scale_rows = placed_tile([P, 2, BANK], U8, "late_scale_rows", LATE_SCALE_ROWS_AT)
        to_quadrants(nc.sync, late_scale_rows[:, 0], w1_scales[0, :, BANK:])
        to_quadrants(nc.sync, late_scale_rows[:, 1], w3_scales[0, :, BANK:])

        def deal_columns(dealt, raw):
            nc.scalar.copy(
                dealt.bitcast(U32).rearrange("p (t a w) -> p t a w", t=4, a=32),
                raw.bitcast(U32).rearrange("p (a t w) -> p t a w", t=4, a=32))
            return dealt

        def page_columns(early, late, s, width):
            u = s % EARLY
            return (early if s < EARLY else late)[:, width * u : width * (u + 1)]

        def product(codes, plane, dtype, moving, moving_plane, width=BANK):
            acc = bank(OPAQUE_BANKS if dtype == FP4X4 else TRANSLUCENT_BANKS)[:, 0:width]
            nc.tensor.matmul_mx(
                out=acc, lhsT=codes.bitcast(dtype), lhsT_scale=plane,
                rhs=moving.bitcast(FP8X4), rhs_scale=moving_plane, start=True, stop=True)
            return acc

        late = {}

        def rectify(s, lo, hi, dst):
            h = lo // BANK
            acc = product(page_columns(w1_words_sb, late.get("w1_codes"), s, 2 * P), page_columns(w1_plane, late.get("w1_plane"), s, P),
                          FP4X4, v1_codes[:, lo:hi], v1_planes[h][:, lo - h * BANK : hi - h * BANK], hi - lo)
            nc.scalar.activation(dst, acc, ACT.Relu)

        def opaque_layer(s, squared):
            for h in range(2):
                rectify(s, h * BANK, (h + 1) * BANK, squared[:, h * BANK : (h + 1) * BANK])
            nc.scalar.activation(squared, squared, ACT.Square)

        pages = {}

        def put_opaque(s, values):
            pages.setdefault(s, placed_tile([P, T2], F32, "page%d" % s, PAGE_AT[s]))
            nc.vector.tensor_copy(pages[s][:].indirect(idx3[:]), values)

        def put_translucent(s, values):
            nc.vector.tensor_copy(pages[s][:].indirect(idx4[:]), values)

        for i, (s, lo, hi) in enumerate(FIRST_PIECES):
            squared = placed_tile([P, hi - lo], F32, "first_squared%d" % i, FIRST_SQUARED_AT[i])
            rectified = placed_tile([P, hi - lo], F32, "rectified%d" % i, RECTIFIED_AT)
            for a, b in ((lo, min(hi, BANK)), (max(lo, BANK), hi)):
                if a < b:
                    rectify(s, a, b, rectified[:, a - lo : b - lo])
            nc.scalar.activation(squared[:], rectified[:], ACT.Square)
            if lo == 0:
                pages.setdefault(s, placed_tile([P, T2], F32, "page%d" % s, PAGE_AT[s]))
            nc.vector.tensor_tensor(pages[s][:].indirect(entries(idx3, lo, hi)), squared[:], opaque_exposure[:, lo:hi], MULT)

        def round_rows(rounded, raw):
            nc.scalar.copy(
                rounded.rearrange("p (n i t) -> p n t i", i=4, t=4), raw.rearrange("p t (n i) -> p n t i", i=4))

        def translucent_layer(s, colour, gate):
            for h in range(2):
                cols = slice(h * BANK, (h + 1) * BANK)
                acc = product(w2_codes[:, s * P : (s + 1) * P], w2_plane[:, s * P : (s + 1) * P],
                              FP8X4, v2_codes[:, cols], v2_plane[:, cols])
                nc.scalar.copy(colour[:, cols], acc)
            for h in range(2):
                cols = slice(h * BANK, (h + 1) * BANK)
                acc = product(page_columns(w3_early_codes, late.get("w3_codes"), s, P), page_columns(w3_plane, late.get("w3_plane"), s, P),
                              FP8X4, v2_codes[:, cols], v2_plane[:, cols])
                nc.scalar.activation(gate[:, cols], acc, ACT.Sigmoid)

        def late_exposures(src, s, name):
            dst = placed_tile([P, 2, S], F32, "%s%d" % (name, s), LATE_EXPOSURES_AT[s])
            for u in range(2):
                for q in QUADRANTS:
                    nc.sync.dma_start(dst[32 * q : 32 * q + 32, u], dealt_rows(src, s - EARLY + u))
            return dst

        w2_rounded = placed_tile([P, 2, 4 * BANK], BF16, "w2_rounded", W2_ROUNDED_AT)
        round_rows(w2_rounded[:, 0], w2_early_raw[:])
        nc.scalar.copy(
            w2_rounded[:, 1].rearrange("p (t a b i) -> p t a b i", t=4, b=4, i=4),
            w2_late_raw[:].rearrange("p i (a t b) -> p t a b i", t=4, b=4))
        v2_codes = placed_tile([P, S], U32, "v2_codes", V2_CODES_AT)
        nc.vector.tensor_copy(v2_codes[:], tab2_w[:].bitcast(U32).indirect(idx2[:]))
        w2_codes = new_tile([P, H], U32, "w2_codes")
        w2_plane = new_tile([P, H], U8, "w2_plane")
        nc.vector.quantize_mx(out=w2_codes[:].bitcast(FP8X4), scales=w2_plane[:], in_=w2_rounded[:].rearrange("p b x -> p (b x)"))

        squared2 = placed_tile([P, S], F32, "squared2", GATHERED_ROWS_AT)
        for h in range(2):
            half_page = squared2[:, h * BANK : (h + 1) * BANK]
            rectify(2, h * BANK, (h + 1) * BANK, half_page)
            nc.scalar.activation(half_page, half_page, ACT.Square)
        pages.setdefault(2, placed_tile([P, T2], F32, "page2", PAGE_AT[2]))

        def put_half_of_page2(h, at):
            cols = slice(h * BANK, (h + 1) * BANK)
            values = placed_tile([P, BANK], F32, "opaque2_%d" % h, at)
            nc.gpsimd.tensor_tensor(values[:], squared2[:, cols], opaque_exposure[:, cols], MULT)
            nc.vector.tensor_copy(pages[2][:].indirect(entries(idx3, cols.start, cols.stop)), values[:])

        put_half_of_page2(0, FIRST_SQUARED_AT[-1])

        w4_raw = placed_tile([P, 2, 4, N], F32, "w4_raw", W4_RAW_AT)
        nc.sync.dma_start(w4_raw[:, 0].rearrange("p t n -> p (t n)"), w4[0:K, :].rearrange("(p t) n -> p (t n)", t=4))
        for t in range(4):
            nc.sync.dma_start(w4_raw[:, 1, t], dealt_rows(w4[K:, :], t))
        w1_late_words = placed_tile([P, H], U8, "w1_late_words", W3_LATE_WORDS_AT + 2 * KIB)
        nc.sync.dma_start(w1_late_words[:].bitcast(I32), w1_words[0, :, H:].bitcast(I32))
        w3_late_words = load(placed_tile([P, BANK], I32, "w3_late_words", W3_LATE_WORDS_AT), words_of(w3_words)[:, BANK:])
        late_opaque_exposures = {s: late_exposures(wg1, s, "opaque_exposures") for s in (4, 6)}

        squared3 = placed_tile([P, S], F32, "squared3", THIRD_SQUARED_AT)
        opaque_layer(3, squared3[:])
        opaque3 = placed_tile([P, S], F32, "opaque3", THIRD_OPAQUE_AT)
        nc.gpsimd.tensor_tensor(opaque3[:], squared3[:], opaque_exposure[:], MULT)
        put_opaque(3, opaque3[:])
        put_half_of_page2(1, THIRD_SQUARED_AT)
        identity = placed_tile([P, P], F32, "identity", GATHERED_ROWS_AT)
        make_identity(nc, identity[:])

        first = placed_tile([P, 2, S], F32, "colour_and_gate0", GATES_AT[0])
        translucent_layer(0, first[:, 0], first[:, 1])
        translucent0 = placed_tile([P, S], F32, "translucent0", FIRST_TRANSLUCENT_AT)
        nc.gpsimd.tensor_tensor(first[:, 0], first[:, 0], translucent_exposure[:], MULT)
        nc.gpsimd.tensor_tensor(translucent0[:], first[:, 0], first[:, 1], MULT)
        put_translucent(0, translucent0[:])

        def translucent_layers(s, count):
            colours = placed_tile([P, count, S], F32, "colours%d" % s, SOURCES_AT[s])
            gates = placed_tile([P, count, S], F32, "gates%d" % s, GATES_AT[s])
            for u in range(count):
                translucent_layer(s + u, colours[:, u], gates[:, u])
            return colours, gates

        def expose_and_put(s, count, colours, gates, exposures):
            nc.gpsimd.tensor_tensor(colours[:], colours[:], exposures, MULT)
            nc.gpsimd.tensor_tensor(colours[:], colours[:], gates[:], MULT)
            for u in range(count):
                put_translucent(s + u, colours[:, u])

        def translucent_sources(s, count, exposures):
            expose_and_put(s, count, *translucent_layers(s, count), exposures)

        def late_opaque_pair(s):
            squared = placed_tile([P, 2, S], F32, "squared%d" % s, LATE_SQUARED_AT[s])
            for u in range(2):
                opaque_layer(s + u, squared[:, u])
            nc.gpsimd.tensor_tensor(squared[:], squared[:], late_opaque_exposures[s][:], MULT)
            return squared

        translucent_sources(1, 1, translucent_exposure[:].unsqueeze(1))

        late.setdefault("w1_codes", deal_columns(new_tile([P, H], U8, "w1_late_codes")[:], w1_late_words[:]))
        for q in QUADRANTS:
            live = slice(32 * q, 32 * q + 4)
            nc.scalar.copy(
                late_planes[live, :].bitcast(U32).rearrange("p (o t a) -> p o t a", o=2, t=4),
                late_scale_rows[live].rearrange("p o n -> p (o n)").bitcast(U32).rearrange("p (o a t) -> p o t a", o=2, t=4))
        late.setdefault("w1_plane", late_planes[:, 0:BANK])
        late.setdefault("w3_plane", late_planes[:, BANK:])
        opaque45 = late_opaque_pair(4)
        late.setdefault("w3_codes", deal_columns(new_tile([P, BANK], I32, "w3_late_codes")[:], w3_late_words[:]))
        for u in range(2):
            put_opaque(4 + u, opaque45[:, u])
        exposures45 = late_exposures(wg2, 4, "translucent_exposures")
        translucent_sources(2, 2, translucent_exposure[:].unsqueeze(1).to_broadcast([P, 2, S]))
        opaque67 = late_opaque_pair(6)
        for u in range(2):
            put_opaque(6 + u, opaque67[:, u])
        exposures67 = late_exposures(wg2, 6, "translucent_exposures")
        w4_rounded = placed_tile([P, 2, 4 * N], BF16, "w4_rounded", W4_ROUNDED_AT)
        for b in range(2):
            round_rows(w4_rounded[:, b], w4_raw[:, b])
        translucent_sources(4, 2, exposures45[:])

        turned = [placed_tile([P, BLOCKS, 2, P], F32, "turned%d" % c, TURNED_AT + c * 4 * KIB) for c in range(CHUNKS)]

        def turn(first, z_pair):
            words = z_pair[:].rearrange("p m u -> p (m u)").bitcast(F32)
            for c in range(CHUNKS):
                acc = bank(TURN_BANKS)
                for k in range(BLOCKS):
                    at = c * BANK + k * P
                    nc.tensor.transpose(acc[:, k * P : (k + 1) * P], words[:, at : at + P], identity[:])
                rows = acc[:].bitcast(BF16).rearrange("p (k q v e u) -> p u k v q e", k=BLOCKS, v=2, e=2, u=2)
                places = turned[c][:].rearrange("p k v w -> p (k v w)").bitcast(BF16).rearrange(
                    "p (k v s q e) -> p s k v q e", k=BLOCKS, v=2, s=EARLY, e=2)
                for u in range(2):
                    nc.scalar.copy(places[:, first + u], rows[:, u])

        woven = {}

        def woven_tile(b, c):
            woven.setdefault((b, c), placed_tile([P, 4 * BANK], BF16, "woven%d_%d" % (b, c), LATE_ROWS_AT if (b, c) == (1, CHUNKS - 1) else WOVEN_AT[b] + c * 4 * KIB))
            return woven[b, c]

        def turn_back(c):
            words = woven_tile(0, c)[:].bitcast(F32)
            for pair in range(BLOCKS // 2):
                acc = bank(TURN_BANKS)
                for k in range(2):
                    for v in range(2):
                        at = (2 * k + v) * P
                        nc.tensor.transpose(acc[:, at : at + P], turned[c][:, 2 * pair + k, v], identity[:])
                nc.scalar.copy(
                    words[:, pair * BANK : (pair + 1) * BANK].rearrange("p (k m v) -> p k m v", k=2, v=2),
                    acc[:].rearrange("p (k v m) -> p k m v", k=2, v=2))

        def mix_rows(s):
            return mix[s * P : (s + 1) * P, :].unsqueeze(0) if s < EARLY else dealt_rows(mix[K:, :], s - EARLY)

        def load_mix(s):
            return load(placed_tile([P, T2], F32, "mix%d" % s, MIX_AT[s]), mix_rows(s))

        def load_last_mix(c):
            return load(placed_tile([P, BANK], F32, "last_mix%d" % c, LAST_MIX_AT[c]), mix_rows(PAGES - 1)[:, :, c * BANK : (c + 1) * BANK])

        mix_tiles = {s: load_mix(s) for s in range(EARLY)}
        z_pairs = {}
        for s in (0, 2, 1, 3):
            if s % 2 == 0:
                z_pairs.setdefault(s // 2, placed_tile([P, T2, 2], BF16, "z_pair%d" % s, Z_AT[s // 2]))
            nc.gpsimd.tensor_tensor(z_pairs[s // 2][:, :, s % 2], pages[s][:], mix_tiles[s][:], MULT)
            if s == 2:
                last_layers = translucent_layers(6, 2)
            if s % 2 == 1:
                turn(s - 1, z_pairs[s // 2])
        mix_tiles.setdefault(EARLY, load_mix(EARLY))
        expose_and_put(6, 2, *last_layers, exposures67[:])
        mix_tiles.setdefault(EARLY + 1, load_mix(EARLY + 1))
        last_mix = [load_last_mix(c) for c in range(CHUNKS)]
        last = PAGES - 1
        shared_cols = slice(WOVEN_COLUMNS, T2)
        mix_banks = []
        for c in range(MIX_IN_PSUM):
            flipped = bank(FLIP_BANKS)
            for k in range(BLOCKS):
                nc.tensor.transpose(flipped[:, k * P : (k + 1) * P], last_mix[c][:, k * P : (k + 1) * P], identity[:])
            flipped_rows = placed_tile([P, BANK], F32, "flipped_mix%d" % c, FLIPPED_AT + c * 2 * KIB)
            nc.scalar.copy(flipped_rows[:], flipped[:])
            mix_banks.append(bank(MIX_BANKS))
            for k in range(BLOCKS):
                nc.tensor.transpose(mix_banks[c][:, k * P : (k + 1) * P], flipped_rows[:, k * P : (k + 1) * P], identity[:])

        for c in range(CHUNKS):
            turn_back(c)
        shares = ((0, WOVEN_COLUMNS), (WOVEN_COLUMNS, T2))
        pairs = [placed_tile([P, 2, hi - lo, 2], BF16, "pairs%d" % i, PAIRS_AT[i]) for i, (lo, hi) in enumerate(shares)]
        last_pairs = [tile[:, 1].rearrange("p m e -> p (m e)").bitcast(F32) for tile in pairs]
        for i, (lo, hi) in reversed(list(enumerate(shares))):
            nc.sync.dma_start(last_pairs[i], mix_rows(last - 1)[:, :, lo:hi])
        late_rows = placed_tile([P, 2 * T2], BF16, "late_rows", LATE_ROWS_AT)
        for u in range(2):
            nc.gpsimd.tensor_tensor(late_rows[:, u * T2 : (u + 1) * T2], pages[EARLY + u][:], mix_tiles[EARLY + u][:], MULT)
        for i, (lo, hi) in reversed(list(enumerate(shares))):
            nc.scalar.copy(pairs[i][:, 0], late_rows[:].rearrange("p (e m) -> p m e", e=2)[:, lo:hi])

        def weave(c, tile, cols):
            words = tile[:].rearrange("p u m e -> p u (m e)").bitcast(U32)
            nc.scalar.copy(
                woven_tile(1, c)[:].bitcast(U32).rearrange("p (m u) -> p m u", u=2), words[:, :, cols].rearrange("p u m -> p m u"))

        for i, (lo, hi) in reversed(list(enumerate(shares))):
            nc.gpsimd.tensor_tensor(pairs[i][:, 1, :, 0], pages[last - 1][:, lo:hi], last_pairs[i], MULT)
            if hi == T2:
                weave(CHUNKS - 1, pairs[i], slice(0, BANK))

        accs = {}

        def last_row(c):
            cols = slice(c * BANK, (c + 1) * BANK)
            nc.vector.tensor_tensor(pairs[0][:, 1, cols, 1], pages[last][:, cols], (mix_banks[c] if c < MIX_IN_PSUM else last_mix[c])[:], MULT)
            weave(c, pairs[0], cols)

        def pieces(c):
            return ((0, BANK // 2), (BANK // 2, BANK)) if c + 1 == CHUNKS else ((0, BANK),)

        def shade(b, c):
            codes = placed_tile([P, BANK], U32, "z_codes%d_%d" % (b, c), Z_CODES_AT[b] + c * 2 * KIB)
            if b == 0:
                plane = placed_tile([P, BANK], U8, "z_plane0_%d" % c, LAST_MIX_AT[-1] + c * HALF + HALF // 2)
                nc.vector.quantize_mx(out=codes[:].bitcast(FP8X4), scales=plane[:], in_=woven[b, c][:])
            else:
                plane = new_tile([P, BANK], U8, "z_plane1_%d" % c)
            for lo, hi in pieces(c):
                if b == 1:
                    nc.vector.quantize_mx(
                        out=codes[:, lo:hi].bitcast(FP8X4), scales=plane[:, lo:hi], in_=woven[b, c][:, 4 * lo : 4 * hi])
                for half in range(2):
                    if b == 0:
                        accs.setdefault((c, lo, half), bank(SUM_BANKS)[:, 0 : hi - lo])
                    cols = slice(b * N + half * P, b * N + (half + 1) * P)
                    nc.tensor.matmul_mx(
                        out=accs[c, lo, half], lhsT=w4_codes[:, cols].bitcast(FP8X4), lhsT_scale=w4_plane[:, cols],
                        rhs=codes[:, lo:hi].bitcast(FP8X4), rhs_scale=plane[:, lo:hi], start=(b == 0), stop=(b == 1))

        def store(c, lo, hi, half, on_vector):
            result = placed_tile([P, hi - lo], F32, "result%d_%d_%d" % (c, lo, half), RESULTS_AT + (2 * c + half) * 2 * KIB + 4 * lo)
            if on_vector:
                nc.vector.tensor_copy(result[:], accs[c, lo, half])
            else:
                nc.scalar.copy(result[:], accs[c, lo, half])
            nc.sync.dma_start(out[half * P : (half + 1) * P, c * BANK + lo : c * BANK + hi], result[:])

        nc.gpsimd.tensor_tensor(
            woven[1, CHUNKS - 1][:].rearrange("p (m t) -> p m t", t=4)[:, :, 3], pages[last][:, shared_cols], last_mix[CHUNKS - 1][:], MULT)
        for c in range(CHUNKS - 1):
            last_row(c)
        for c in range(2):
            warm_up = ps.tile([P, BANK], F32, name="warm_up%d" % c, tag="bank%d" % MIX_BANKS[c])
            for repeat in range(2):
                nc.tensor.matmul_mx(
                    out=warm_up[:], lhsT=w2_codes[:, 0:P].bitcast(FP8X4), lhsT_scale=w2_plane[:, 0:P],
                    rhs=v2_codes[:, 0:BANK].bitcast(FP8X4), rhs_scale=v2_plane[:, 0:BANK], start=True, stop=True)
        w4_codes = new_tile([P, 2 * N], U32, "w4_codes")
        w4_plane = placed_tile([P, 2 * N], U8, "w4_plane", LAST_MIX_AT[-1] - HALF // 2)
        nc.vector.quantize_mx(out=w4_codes[:].bitcast(FP8X4), scales=w4_plane[:], in_=w4_rounded[:].rearrange("p b x -> p (b x)"))
        for c in range(CHUNKS):
            if c + 1 == CHUNKS:
                for half in range(2):
                    store(0, 0, BANK, half, False)
            shade(0, c)
            shade(1, c)
        for c in range(1, CHUNKS):
            for lo, hi in pieces(c):
                for half in range(2):
                    store(c, lo, hi, half, c + 1 == CHUNKS and half == 1)
